import numpy as np, ml_dtypes
CORES = [40,41,42,43,44,45,46,47]
N = 8
BF = ml_dtypes.bfloat16
W, C, M, V, D, Q = 4096, 128, 4, 5, 3, 9
LM = 127
def parts(rng):
    return (rng.integers(0, 256, (N, 8, 16, W)), rng.integers(0, W, (N, 8, 16, C)), rng.integers(0, 256, (N, 8, 16, C)),
            rng.integers(0, 16, (N, 8, 16, 1)), rng.integers(48, 81, (N, 8, 16, 1)))
def pack(x, f, z, w, lm):
    return {"rock": x.reshape(N, 128, W).astype(np.float32).astype(BF), "front": np.ascontiguousarray(f.reshape(N, 128, C)).astype(np.int32),
            "vein": z.reshape(N, 128, C).astype(np.float32).astype(BF), "w": w.reshape(N, 128, 1).astype(np.int32), "lim": lm.reshape(N, 128, 1).astype(np.int32)}
def setup_inputs(rng):
    return pack(*parts(rng))
def setup_inputs_alike(rng):
    x, f, z, w, lm = parts(rng); lm = rng.integers(10, 41, (N, 8, 16, 1)); rec = rng.integers(100, 156, (N, 8, 16, 4))
    x = np.take_along_axis(rec, rng.integers(0, 4, (N, 8, 1, W)), 3)
    far = lm + rng.choice(np.array([-1, 0, 0, 0, 1, 2, 3, 4]), (N, 8, 16, C))
    z = np.take_along_axis(rec, rng.integers(0, 4, (N, 8, 1, C)), 3) + rng.choice(np.array([-1, 1]), (N, 8, 16, C)) * far
    f[:, ::2] = rng.choice(np.array([0, W - 1, W // 2, 3]), (N, 4, 16, C))
    f[:, 1] = f[:, 1][..., rng.integers(0, 4, C)]
    return pack(x, f, z, w, lm)
def setup_inputs_corners(rng):
    x, f, z, w, lm = parts(rng); end = np.array([0, 1, 14, 15]); P = C // 2; h = np.arange(P)
    for a in range(N):
        o = [int(b) for b in rng.permutation(8)]
        for g in range(8):
            v = o[g]
            if v == 0:
                lm[a, g] = 0; w[a, g] = 0
            elif v == 1:
                lm[a, g] = LM; w[a, g] = 15
            elif v in (2, 3, 4):
                x[a, g] = rng.integers(200, 256, (16, W)); z[a, g] = rng.integers(0, 61, (16, C)); lm[a, g] = rng.integers(0, 101, (16, 1))
                s = np.arange(16)[:, None] * (W // 32) + rng.integers(0, W // 32, (16, P)); j = rng.integers(W // 2, W, (16, P))
                if v == 2:
                    k = rng.choice(end, P); l = rng.choice(end, P); k[:16] = np.repeat(end, 4); l[:16] = np.tile(end, 4)
                    s[np.maximum(l, rng.integers(0, 16, P)), h] = s[l, h]
                    j[k, h] = (s[l, h] & -8) + rng.integers(0, 8, P)
                    j[np.maximum(k, rng.integers(0, 16, P)), h] = j[k, h]
                if v == 4:
                    s[:] = W - 1; j[:] = W - 1; s[:, :P // 2] = 0; j[:, :P // 2] = 0
                    s[1:, P // 2:3 * P // 4] = W - 21; j[1:, P // 2:3 * P // 4] = W - 3
                f[a, g][:, 0::2] = s; f[a, g][:, 1::2] = j
            elif v == 5:
                r = rng.integers(64, 192, (16, 1)); x[a, g] = r; lm[a, g] = 0
                off = np.argsort(rng.random((16, C)), axis=0) >= rng.integers(Q - 2, Q + 2, C)[None, :]
                z[a, g] = r + np.where(off, rng.choice(np.array([-40, -4, 4, 40]), (16, C)), 0)
            elif v == 6:
                f[a, g] = (W - 1) * rng.integers(0, 2, (16, C)); w[a, g] = 15 * rng.integers(0, 2, (16, 1)); lm[a, g] = LM * rng.integers(0, 2, (16, 1))
            else:
                w[a, g, 0] = 15; w[a, g, 1] = 1; z[a, g][:, ::2] = 0; z[a, g, 0, ::2] = 136; z[a, g, 1, ::2] = 7; f[a, g][:, ::4] = W - 1
                for i, n, u, m in ((2, W - 3, 2037, 0), (6, W - 15, 2039, 2)):
                    z[a, g, 0, i::8] = 135; z[a, g, 1, i::8] = u - 2025; f[a, g][:, i::8] = n
                    x[a, g][:, (((n * (2 * u + 1)) >> (5 + m)) + n + 613 * m + 37 * np.arange(16)) & (W - 1)] = z[a, g][:, i][:, None]
    return pack(x, f, z, w, lm)
def setup_inputs_ends(rng):
    x, f, z, w, lm = parts(rng)
    x = 255 * np.where(rng.random((N, 8, 1, W)) < 0.4, rng.integers(0, 2, (N, 8, 1, W)), rng.integers(0, 2, (N, 8, 16, W)))
    z = 255 * np.where(rng.random((N, 8, 1, C)) < 0.4, rng.integers(0, 2, (N, 8, 1, C)), rng.integers(0, 2, (N, 8, 16, C)))
    f = (W - 1) * rng.integers(0, 2, f.shape); w = 15 * rng.integers(0, 2, w.shape); lm = LM * rng.integers(0, 2, lm.shape)
    for a, g in ((N - 1, 7), (0, 0)):
        w[a, g] = 15; z[a, g][:, [0, C - 2, C - 1]] = 255; z[a, g][:, [3, C - 3]] = 0
        z[a, g][:, [5, C - 4]] = rng.permutation(np.array([255] * 9 + [26] + [0] * 6))[:, None]
        f[a, g, 15][[0, 3, 5, C - 4, C - 3, C - 2, C - 1]] = W - 1
        for u in ((16 * 15 * 255) & 2047, 0):
            x[a, g][:, ((((W - 1) * (2 * u + 1)) >> (5 + np.arange(M))) + W - 1 + 613 * np.arange(M) + 37 * 15) & (W - 1)] = 0
    return pack(x, f, z, w, lm)
def setup_inputs_full(rng):
    x, f, z, w, lm = parts(rng); P = C // 2; h = np.arange(P); n = W // C
    b = int(rng.integers(0, N)); g = int(rng.integers(0, 8)); rest = [q for q in range(N) if q not in (b, (b - D) % N)]; a = rest[int(rng.integers(0, len(rest)))]
    for q in range(N):
        if q != a:
            x[q, g] = rng.integers(200, 256, (16, W)); z[q, g] = rng.integers(0, 61, (16, C)); lm[q, g] = 0
            f[q, g] = n * rng.permutation(C)[None, :] + rng.integers(0, n, (16, C))
    i = np.array([P - 1, 0, P // 2])[:int(rng.integers(1, 4))]
    f[b, g, 15, 2 * i + 1] = (f[b, g, rng.integers(0, 16, len(i)), 2 * i] & -8) + rng.integers(0, 8, len(i))
    x[a] = rng.integers(200, 256, (8, 16, W)); z[a] = rng.integers(0, 61, (8, 16, C)); lm[a] = rng.integers(80, 121, (8, 16, 1))
    k = rng.integers(0, 16, (8, P)); l = rng.integers(0, 16, (8, P)); gr = np.arange(8)[:, None]; fa = f[a]
    fa[gr, k, 2 * h + 1] = (fa[gr, l, 2 * h] & -8) + rng.integers(0, 8, (8, P))
    o = [int(c) for c in rng.permutation(8)]
    f[a, o[0]] = 0; w[a, o[0]] = 0
    f[a, o[1]] = W - 1; w[a, o[1]] = 0; w[a, o[1], 0] = W >> 9; z[a, o[1], 0] = 32
    return pack(x, f, z, w, lm)
def setup_inputs_spread(rng):
    x = np.minimum((np.exp2(8 * rng.random((N, 8, 1, W))) * rng.random((N, 8, 16, W))).astype(np.int64), 255)
    z = np.minimum((np.exp2(8 * rng.random((N, 8, 1, C))) * rng.random((N, 8, 16, C))).astype(np.int64), 255)
    f = np.minimum((W * rng.random((N, 8, 16, C)) ** 3).astype(np.int64), W - 1)
    return pack(x, f, z, rng.integers(0, 16, (N, 8, 16, 1)), np.minimum((128 * rng.random((N, 8, 16, 1)) ** 2).astype(np.int64), LM))
def check_inputs(d):
    bad = []
    for k, hi in (("rock", 255), ("front", W - 1), ("vein", 255), ("w", 15), ("lim", LM)):
        v = np.asarray(d[k]).astype(np.float64)
        if not (np.min(v) >= 0 and np.max(v) <= hi): bad.append("range of " + k)
        elif np.any(v != np.floor(v)): bad.append("whole numbers in " + k)
    return bad
def reference(rock, front, vein, w, lim):
    x = rock.astype(np.float32).astype(np.int64).reshape(N, 8, 16, W)
    f = front.astype(np.int64).reshape(N, 8, 16, C)
    z = vein.astype(np.float32).astype(np.int64).reshape(N, 8, 16, C)
    wt = w.astype(np.int64).reshape(N, 8, 16, 1); lm = lim.astype(np.int64).reshape(N, 8, 16, 1)
    place = np.arange(16)[:, None]; ci = np.arange(C); met = np.zeros(N, np.int64)
    for t in range(V):
        if t > 0:
            f = np.roll(f, D, axis=0); z = np.roll(z, D, axis=0)
        u = np.add.reduce(wt * z, axis=2) & 2047
        dig = np.add.reduce(z, axis=2) & 15
        top = (lm + (met & 3)[:, None, None, None])[..., None]
        for m in range(M):
            c = (((f * (2 * u[:, :, None, :] + 1)) >> (5 + m)) + f + 613 * m + 37 * place) & (W - 1)
            v = np.take_along_axis(x, c.reshape(N, 8, 1, 16 * C), 3).reshape(N, 8, 16, 16, C)
            dif = np.abs(v - z[:, :, :, None, :])
            score = np.add.reduce(dif, axis=2); near = np.count_nonzero(dif <= top, axis=2)
            if m == 0:
                bs, bc, bn = score, c, near
            else:
                less = score < bs; bs = np.where(less, score, bs); bc = np.where(less, c, bc); bn = np.where(less, near, bn)
        f = np.where(bn >= Q, bc, f)
        sen = ci[((ci >> t) & 1) == 0]; jun = sen + (1 << t)
        fs = f[..., sen]; fj = f[..., jun]
        eq = ((fj[:, :, :, None, :] >> 3) == (fs[:, :, None, :, :] >> 3)).reshape(N, 8, 256, C // 2)
        meet = np.any(eq, axis=2)[:, :, None, :]; first = np.argmax(eq, axis=2)[:, :, None, :]
        k = first >> 4; l = first & 15
        met = np.count_nonzero(meet, axis=(1, 2, 3))
        src = place - l + k
        ns = np.where(meet & (place > l) & (src <= 15), np.take_along_axis(fj, np.minimum(np.maximum(src, 0), 15), 2), fs)
        nj = np.where(meet & (place >= k), (((fj * fs) >> 5) + fj + u[..., jun][:, :, None, :]) & (W - 1), fj)
        f = f.copy(); f[..., sen] = ns; f[..., jun] = nj
        e = np.take_along_axis(f, dig[:, :, None, :], 2)
        old = np.take_along_axis(x, e, 3)
        lo = np.full((N, 8, W), C)
        np.minimum.at(lo, (np.arange(N)[:, None, None], np.arange(8)[None, :, None], e[:, :, 0]), np.broadcast_to(ci, (N, 8, C)))
        zl = np.take_along_axis(z, np.minimum(lo, C - 1)[:, :, None, :], 3)
        x = np.where((lo < C)[:, :, None, :], np.maximum(x - (zl >> 2), 0), x)
        z = (z + old) >> 1
    return {"yx": x.reshape(N, 128, W).astype(np.float32).astype(BF), "yf": f.reshape(N, 128, C).astype(np.float32), "yz": z.reshape(N, 128, C).astype(np.float32).astype(BF)}

@@ -1,0 +1,576 @@
+import math
+from concourse.mybir import AluOpType as A, ActivationFunctionType as AF, AxisListType
+
+NV = 5
+NEARV = ((0, 1, 2, 3), (0, 1, 2, 3))
+SG = (0,)
+ZXV = (16, 0)
+SCRATCH = {
+    "PI": ("sbuf", [128, 8], "int32"), "RF": ("sbuf", [128, 16], "float32"),
+    "ONES": ("sbuf", [128, 160], "bfloat16"), "IEB": ("sbuf", [128, 160], "bfloat16"),
+    "IEH": ("sbuf", [128, 160], "float16"), "I32": ("sbuf", [128, 128], "float32"),
+    "GR": ("sbuf", [128, 128], "float32"), "CR": ("sbuf", [128, 128], "float32"),
+    "XR": ("sbuf", [128, 144], "float32"), "T32": ("sbuf", [128, 128], "float32"),
+    "BLK": ("sbuf", [128, 128], "bfloat16"), "BLH": ("sbuf", [128, 128], "float16"),
+    "R256": ("sbuf", [128, 144], "bfloat16"), "R05": ("sbuf", [128, 144], "bfloat16"), "R1B": ("sbuf", [128, 144], "bfloat16"),
+    "R1H": ("sbuf", [128, 144], "float16"), "R2H": ("sbuf", [128, 144], "float16"), "NI": ("sbuf", [128, 128], "bfloat16"),
+    "EX": ("sbuf", [128, 1024], "bfloat16"), "EX1": ("sbuf", [128, 512], "bfloat16"), "ZT": ("sbuf", [128, 2, 128], "bfloat16"),
+    "XG0": ("sbuf", [128, 1024], "bfloat16"), "XG1": ("sbuf", [128, 1024], "bfloat16"),
+    "KM16": ("sbuf", [128, 16], "float32"), "KT": ("sbuf", [128, 16], "float32"),
+    "P4": ("sbuf", [128, 16], "float32"), "P4C": ("sbuf", [128, 1], "float32"),
+    "EL": ("sbuf", [128, 16 * 128], "bfloat16"), "NEG": ("sbuf", [128, 128], "bfloat16"), "PL": ("sbuf", [128, 16 * 128], "bfloat16"),
+    "SLB": ("sbuf", [128, 128], "bfloat16"), "Q2": ("sbuf", [128, 128], "bfloat16"),
+    "UPI": ("sbuf", [128, 128], "bfloat16"), "S15": ("sbuf", [128, 128], "bfloat16"),
+    "ALLC": ("sbuf", [128, 128], "bfloat16"), "K1": ("sbuf", [128, 2, 256], "bfloat16"),
+    "BB": ("sbuf", [128, 4], "float32"), "PCH": ("sbuf", [128, 2], "float16"),
+    "DUMP": ("sbuf", [128, 8], "float32"), "MK": ("sbuf", [128, 5 * 256], "float16"),
+    "PRW": ("sbuf", [128, 5 * 64], "float32"), "JCI": ("sbuf", [128, 16], "int32"),
+    "PCI": ("sbuf", [128, 5 * 4], "int32"), "PTI": ("sbuf", [128, 5 * 4], "int32"),
+    "PCF": ("sbuf", [128, 5 * 4], "float32"),
+    "W2": ("sbuf", [128, 128], "bfloat16"), "WI": ("sbuf", [128, 2], "int32"),
+    "WF": ("sbuf", [128, 2], "float32"), "LIM": ("sbuf", [128, 1], "float32"),
+    "TOP": ("sbuf", [128, 8], "float32"), "CN": ("sbuf", [128, 4], "float32"), "CI": ("sbuf", [128, 4], "int32"),
+    "FI": ("sbuf", [128, 128], "int32"),
+    "F": ("sbuf", [128, NV * 128], "float32"), "FO": ("sbuf", [128, NV * 128], "float32"),
+    "Z": ("sbuf", [128, NV * 128], "bfloat16"), "ZO": ("sbuf", [128, NV * 128], "bfloat16"),
+    "ROCK": ("sbuf", [128, 4096 + 128], "bfloat16"),
+    "YF": ("sbuf", [128, 128], "float32"), "YZ": ("sbuf", [128, 128], "bfloat16"),
+    "MF": ("sbuf", [128, 128], "float16"), "RN": ("sbuf", [128, 128], "bfloat16"),
+    "OF": ("sbuf", [128, 8], "uint16"), "LO": ("sbuf", [128, 8], "float32"),
+}
+for _n, _w, _d in (("UA", 128, "int32"), ("UI", 64, "int32"), ("SI", 64, "int32"), ("QI", 64, "int32"),
+                   ("HM", 256, "int32"), ("C4", 256, "int32"), ("DN", 256, "float32"),
+                   ("UF", 32, "float32"), ("SM", 64, "float32"), ("ZB", 64, "bfloat16"), ("Z5", 64, "float32"),
+                   ("Z4", 64, "bfloat16"), ("KS", 128, "float32"), ("KM", 128, "float32"),
+                   ("KB", 64, "int32"), ("KC", 64, "int32"), ("PR", 256, "float32"), ("HF", 64, "float16"), ("JC", 64, "float16"),
+                   ("NS", 64, "float32"), ("S2", 64, "float32"), ("EQB", 512, "bfloat16"),
+                   ("PM", 32, "bfloat16"), ("LN", 64, "float32"), ("JM", 32, "bfloat16"), ("XX", 64, "float16"),
+                   ("JG", 32, "float32"), ("CD", 96, "bfloat16"), ("JI", 32, "int32"),
+                   ("JU", 32, "int32"), ("DJ", 32, "float32"), ("FC", 64, "float32"),
+                   ("EF", 8, "float32"), ("SU", 64, "float32"), ("Y1", 64, "int32"), ("RR", 64, "float32"),
+                   ("DU", 512, "bfloat16"), ("OT", 8, "float32"), ("D", 4096, "bfloat16"), ("NR", 4096, "bfloat16")):
+    SCRATCH[_n] = ("sbuf", [128, 2, _w], _d)
+for _h in "01":
+    for _n, _w, _d in (("CO", 256, "uint16"), ("ZX", 1024, "bfloat16"), ("HW", 1024, "float32"), ("LS", 2, "uint16"), ("E16", 4, "uint16")):
+        SCRATCH[_n + _h] = ("sbuf", [128, _w], _d)
+BANKS = ["X0", "X1", "K0", "K1b", "EQ", "HA", "HB", "MM"]
+for _n in BANKS:
+    SCRATCH[_n] = ("psum", [128, 512], "float32")
+
+LOADS = ["wi", "li", "fr", "v0", "v1", "r0", "r1", "r2", "r3"]
+SEMAPHORES = (["sv", "ss", "st", "sg", "sl"] + ["ld_" + n for n in LOADS] + ["od_f", "od_z", "od_x"] +
+              ["ar%s%d%d" % (k, t, h) for k in "fz" for t in range(1, NV) for h in range(2)])
+QSEM = {"v": "sv", "s": "ss", "t": "st", "g": "sg"}
+ZXP = (1, 1)
+BIAS = {'e1': 0.5, 'm0s': 1.0, 'i0t': -2.5, 'e1t': -5.0, 'c1v': -0.5, 'c0s': -1.0, 'c0t': 13.5, 'm0t': -6.5, 'c0v': -1.0, 'i1t': -6.5,
+        'e1v': -2.0, 'e1s': 4.0, 'e0v': 0.5, 'm1': -2.0, 'c1t': -6.5, 'e0': 0.5, 'i1s': 3.5, 'm1s': -2.0, 'm1v': 0.5, 'c0': 1.0,
+        'e0t': -4.0, 'i0s': -3.5, 'm1t': -1.5, 'e0s': 6.5}
+LOOK = 0.0
+LOV = ((), (1, 3))
+CYC = 0.00104
+PEC = 0.0003
+LAT = 0.15
+SFIX = 78
+
+
+def add(S, q, cost, reads, writes, fn, sig=None, lat=0.0):
+    i = len(S["ops"])
+    deps = {}
+
+    def dep(j, sem):
+        if j != i:
+            deps[j] = deps.get(j, False) or sem
+    for k in reads + writes:
+        if k in BANKS:
+            for q2, (j, wr) in S["b"].setdefault(k, {}).items():
+                dep(j, q2 != q or (wr and k in reads))
+    for k in reads:
+        if k not in BANKS:
+            for j in S["w"].get(k, []):
+                dep(j, True)
+    for k in writes:
+        if k not in BANKS:
+            for j in S["w"].get(k, []) + S["r"].get(k, []):
+                dep(j, True)
+    for k in reads + writes:
+        if k in BANKS:
+            acc = S["b"][k]
+            acc[q] = (i, k in writes or (q in acc and acc[q][1] and k not in reads))
+        elif k in writes:
+            S["w"][k] = [i]
+            S["r"][k] = []
+    for k in reads:
+        if k not in BANKS and k not in writes:
+            S["r"].setdefault(k, []).append(i)
+    S["ops"].append({"q": q, "cost": cost, "deps": deps, "fn": fn, "sig": sig, "lat": lat, "st": S.get("st", ""), "nm": " ".join(writes)})
+    return i
+
+
+def plan(S):
+    ops = S["ops"]
+    n = len(ops)
+    succ = [[] for _ in range(n)]
+    for i, o in enumerate(ops):
+        for j in o["deps"]:
+            succ[j].append(i)
+    pri = [0.0] * n
+    for i in range(n - 1, -1, -1):
+        o = ops[i]
+        b = 0.0
+        for k in succ[i]:
+            b = max(b, pri[k] + (o["lat"] if o["sig"] else (LAT if ops[k]["deps"][i] else 0.0)))
+        pri[i] = b + o["cost"]
+    pri = [p + BIAS.get(o["st"], 0.0) + BIAS.get(o["st"] + o["q"], 0.0) for p, o in zip(pri, ops)]
+    left = [len(o["deps"]) for o in ops]
+    ready = {}
+    est = [0.0] * n
+    free = {}
+    for i in range(n):
+        if left[i] == 0:
+            ready.setdefault(ops[i]["q"], []).append(i)
+    order = []
+    end = 0.0
+    while len(order) < n:
+        best = None
+        for q, lst in ready.items():
+            if lst:
+                st = max(free.get(q, 0.0), min(est[i] for i in lst))
+                if best is None or st < best[0]:
+                    best = (st, q)
+        st, q = best
+        lst = ready[q]
+        c = max((i for i in lst if est[i] <= st + 1e-9), key=lambda i: (pri[i], -i))
+        for i in lst:
+            if pri[i] > pri[c] and est[i] < st + LOOK * ops[c]["cost"]:
+                c = i
+        st = max(st, est[c])
+        lst.remove(c)
+        o = ops[c]
+        fin = st + o["cost"]
+        free[q] = fin
+        o["start"] = st
+        end = max(end, fin + o["lat"])
+        order.append(c)
+        for k in succ[c]:
+            d = ops[k]["deps"][c]
+            l = o["lat"] if o["sig"] else (LAT if d else 0.0)
+            est[k] = max(est[k], fin + l if d else st)
+            left[k] -= 1
+            if left[k] == 0:
+                ready.setdefault(ops[k]["q"], []).append(k)
+    S["end"] = end
+    return order
+
+
+def issue(S, order, eng, T):
+    ops = S["ops"]
+    cnt = {}
+    known = {q: {} for q in eng}
+    for i in order:
+        o = ops[i]
+        q = o["q"]
+        kn = known[q]
+        need = {}
+        for j, sem in o["deps"].items():
+            if sem:
+                s, val = ops[j]["done"]
+                if kn.get(s, 0) < val:
+                    need[s] = max(need.get(s, 0), val)
+        for s in sorted(need):
+            eng[q].wait_ge(T.sem[s], need[s])
+        for j, sem in o["deps"].items():
+            if sem:
+                for s, val in ops[j]["clock"].items():
+                    if kn.get(s, 0) < val:
+                        kn[s] = val
+        if o["sig"]:
+            o["fn"]()
+            o["done"] = o["sig"]
+        else:
+            s = QSEM[q]
+            cnt[s] = cnt.get(s, 0) + 1
+            o["fn"]().then_inc(T.sem[s], 1)
+            o["done"] = (s, cnt[s])
+        o["clock"] = dict(kn)
+        o["clock"][o["done"][0]] = o["done"][1]
+    return cnt
+
+
+def record(g, core, T, topo):
+    rank = T.rank_of(core)
+    S = {"ops": [], "w": {}, "r": {}, "b": {}, "sends": 0}
+    v, sc, te = g.vector, g.scalar, g.tensor
+
+    def seq(calls):
+        def fn():
+            for c in calls:
+                x = c()
+            return x
+        return fn
+
+    def V(cyc, R, W, *calls):
+        return add(S, "v", max(cyc, 64 * len(calls)) * CYC, R, W, seq(calls))
+
+    def SC(cyc, R, W, *calls):
+        return add(S, "s", (cyc + SFIX * len(calls)) * CYC, R, W, seq(calls))
+
+    def PE(cyc, R, W, mms):
+        return add(S, "t", cyc * PEC, R, W, seq([(lambda m: lambda: te.matmul(*m))(m) for m in mms]))
+
+    def G(cost, R, W, call):
+        return add(S, "g", cost, R, W, call)
+
+    def ts(out, in0, s1, s2, op0, op1=None):
+        if op1 is None:
+            return lambda: v.tensor_scalar(out, in0, s1, None, op0)
+        return lambda: v.tensor_scalar(out, in0, s1, s2, op0, op1)
+
+    def tt(out, a, b, op):
+        return lambda: v.tensor_tensor(out, a, b, op)
+
+    def cp(out, a):
+        return lambda: v.tensor_copy(out, a)
+
+    def ac(out, a, f, **kw):
+        return lambda: sc.activation(out, a, f, **kw)
+
+    def ms(ap, c):
+        return lambda: v.memset(ap, c)
+
+    def load(q, name, out, in_, W, lat):
+        e = g.sync if q == "y" else g.scalar
+        add(S, q, 0.06, [], W, lambda: e.dma_start(out, in_).then_inc(T.sem["ld_" + name], 16), ("ld_" + name, 16), lat)
+
+    load("y", "fr", T.FI[:], T.front[:], ["FI"], 2.2)
+    load("s", "v0", T.Z[:, 0:64], T.vein[:, 0:64], ["Z00"], 2.2)
+    load("y", "wi", T.WI[:, 0:1], T.w[:], ["WI0"], 2.2)
+    load("y", "li", T.WI[:, 1:2], T.lim[:], ["WI1"], 2.2)
+    load("s", "v1", T.Z[:, 64:128], T.vein[:, 64:128], ["Z01"], 2.2)
+    for b in range(4):
+        load("y", "r%d" % b, T.ROCK[:, 1024 * b:1024 * b + 1024], T.rock[:, 1024 * b:1024 * b + 1024], ["ROCK%d" % b], 5.0)
+    RK = ["ROCK%d" % b for b in range(4)]
+
+    def ioF(ap, pat, base, cm):
+        return lambda: g.iota(ap, pat, base, cm, allow_small_or_imprecise_dtypes=True)
+
+    def ioI(ap, pat, base, cm):
+        return lambda: g.iota(ap, pat, base, cm)
+    G(0.15, [], ["PI"], ioI(T.PI[:, 0:1], [[1, 1]], 0, 1))
+    G(0.35, [], ["GR"], ioF(T.GR[:], [[1, 8], [0, 16]], 0, 0))
+    G(0.35, [], ["XR"], ioF(T.XR[:, 0:143], [[1, 143]], -15, 0))
+    V(64, [], ["ONES"], ms(T.ONES[:], 1.0))
+    G(0.45, ["ONES"], ["IEB"], lambda: g.affine_select(T.IEB[:, 0:158], T.ONES[:, 0:158], [[-1, 158]], A.is_equal, 0.0, 15, 1))
+    G(0.35, [], ["CR"], ioF(T.CR[:], [[0, 8], [1, 16]], 0, 0))
+    G(0.2, [], ["KM0"], ioF(T.KM16[:], [[1, 16]], 0, 0))
+    V(64, ["PI"], ["PIr"], ts(T.PI[:, 1:2], T.PI[:, 0:1], 15, None, A.bitwise_and))
+    V(64, ["PI"], ["PIg"], ts(T.PI[:, 2:3], T.PI[:, 0:1], 4, None, A.arith_shift_right))
+    V(64, ["PIr"], ["r"], cp(T.RF[:, 0:1], T.PI[:, 1:2]))
+    V(64, ["PIg"], ["gp"], cp(T.RF[:, 1:2], T.PI[:, 2:3]))
+    r = T.RF[:, 0:1]
+    gp = T.RF[:, 1:2]
+    V(64, ["gp"], ["gp16"], ts(T.RF[:, 2:3], gp, 16.0, None, A.mult))
+    V(128, ["GR", "gp"], ["BLK"], ts(T.BLK[:], T.GR[:], gp, None, A.is_equal))
+    V(64, ["BLK"], ["BLH"], cp(T.BLH[:], T.BLK[:]))
+    V(64, ["WI0"], ["WF0"], ts(T.WF[:, 0:1], T.WI[:, 0:1], 2.0, None, A.mult))
+    V(64, ["WI1"], ["LIM"], ts(T.LIM[:], T.WI[:, 1:2], 0.5, None, A.add))
+    V(64, ["LIM"], ["TOP0"], cp(T.TOP[:, 0:1], T.LIM[:]))
+    V(64, ["BLK", "WF0"], ["W2"], ts(T.W2[:], T.BLK[:], T.WF[:, 0:1], None, A.mult))
+    V(128, ["FI"], ["F00", "F01"], cp(T.F[:, 0:128], T.FI[:]))
+    V(4 * 64, ["r"], ["BB"], *[ts(T.BB[:, m:m + 1], r, 37.0 * 2 ** (4 + m), 613.0 * m * 2 ** (4 + m), A.mult, A.add) for m in range(4)])
+    V(64, ["r"], ["c1"], ts(T.RF[:, 4:5], r, -1.0, 1039.0, A.mult, A.add))
+    V(64, ["r"], ["c2"], ts(T.RF[:, 5:6], r, -1.0, 1054.0, A.mult, A.add))
+    V(64, ["PIr"], ["PIs"], ts(T.PI[:, 3:4], T.PI[:, 1:2], 1.0, None, A.add))
+    V(64, ["PIs"], ["PIt"], ts(T.PI[:, 4:5], T.PI[:, 3:4], 15, None, A.bitwise_and))
+    V(64, ["PIt"], ["rp1"], cp(T.RF[:, 3:4], T.PI[:, 4:5]))
+    V(64, [], ["q25"], ms(T.RF[:, 6:7], 0.25))
+    V(64, [], ["b129"], ms(T.RF[:, 8:9], 129.5))
+    V(64, ["IEB"], ["NI"], ts(T.NI[:], T.IEB[:, 15:143], -1.0, None, A.mult))
+    for n, c in (("R256", 256.0), ("R05", 0.5), ("R1B", 1.0), ("R1H", 1.0), ("R2H", 2.0)):
+        V(143, ["XR", "gp16"], [n], ts(T[n][:, 0:143], T.XR[:, 0:143], T.RF[:, 2:3], c, A.is_equal, A.mult))
+    V(64, [], ["ALLC"], ms(T.ALLC[:], 1.0 / 128))
+    for h in range(2):
+        for m in range(4):
+            G(0.28, ["ONES"], ["K1%d%d" % (h, m)], (lambda h, m: lambda: g.affine_select(T.K1[:, h, 64 * m:64 * m + 64], T.ONES[:, 0:64], [[0, 64]], A.is_gt, 64.0 * m + (23 if m in NEARV[h] else 31), 0, 0))(h, m))
+    V(80, ["IEB"], ["IEH"], cp(T.IEH[:, 0:158], T.IEB[:, 0:158]))
+    V(128, ["IEB"], ["I32"], cp(T.I32[:], T.IEB[:, 15:143]))
+    V(64, ["KM0", "r"], ["KT"], ts(T.KT[:], T.KM16[:], r, None, A.is_equal))
+    V(512, [], ["W1"], ms(T.EX1[:], 1.0))
+    for b in range(2):
+        G(1.05, ["W1"], ["EX%d" % b], (lambda b: lambda: g.affine_select(T.EX[:, 512 * b:512 * b + 512], T.EX1[:], [[-1, 32], [0, 16]], A.is_equal, 0.0, -32 * b, 1))(b))
+    V(64, [], ["NEG"], ms(T.NEG[:], -1.0))
+    for l in range(16):
+        G(0.4, ["NEG"], ["EL%d" % l], (lambda l: lambda: g.affine_select(T.EL[:, 128 * l:128 * l + 128], T.NEG[:], [[-16, 8], [0, 16]], A.is_equal, 0.0, -l, 1))(l))
+        G(0.18, ["q25"], ["P4%d" % l], (lambda l: lambda: g.affine_select(T.P4[:, l:l + 1], T.RF[:, 6:7], [[0, 1]], A.is_gt, 4.0 ** l, 0, 0))(l))
+    V(64, ["P4%d" % l for l in range(16)] + ["KT"], ["P4b"], tt(T.P4[:], T.P4[:], T.KT[:], A.mult))
+    V(64, ["P4b"], ["P4C"], lambda: v.tensor_reduce(T.P4C[:], T.P4[:], AxisListType.X, A.add))
+    V(64, ["BLK", "P4C"], ["Q2"], ts(T.Q2[:], T.BLK[:], T.P4C[:, 0:1], None, A.mult))
+    V(128, ["CR", "r"], ["T32"], ts(T.T32[:], T.CR[:], r, -(2.0 ** 40), A.is_gt, A.mult))
+    V(256, ["T32", "BLK"], ["SLB"], tt(T.SLB[:], T.T32[:], T.BLK[:], A.mult))
+    for l in range(16):
+        G(0.4, ["SLB"], ["PL%d" % l], (lambda l: lambda: g.affine_select(T.PL[:, 128 * l:128 * l + 128], T.SLB[:], [[-1, 128]], A.not_equal, 4.0 ** (15 - l), 0, 1))(l))
+    V(128, ["CR", "r"], ["T32"], ts(T.T32[:], T.CR[:], r, None, A.is_ge))
+    V(256, ["T32", "BLK"], ["UPI"], tt(T.UPI[:], T.T32[:], T.BLK[:], A.mult))
+    V(64, ["ONES", "KT"], ["S15"], ts(T.S15[:], T.ONES[:, 0:128], T.KT[:, 15:16], None, A.mult))
+    G(0.2, [], ["JCI0"], ioI(T.JCI[:, 0:8], [[16, 8]], 0, 0))
+    V(64, ["JCI0", "r"], ["JCI1"], ts(T.JCI[:, 8:16], T.JCI[:, 0:8], r, None, A.add))
+    V(64, ["JCI1"], ["PCH"], cp(T.PCH[:], T.JCI[:, 8:10]))
+    V(64, ["JCI1"], ["DUMP"], ts(T.DUMP[:], T.JCI[:, 8:16], 4096.0, None, A.add))
+    V(128, [], ["HWz0", "HWz1"], ms(T.HW0[:, 0:32], 0.0), ms(T.HW1[:, 0:32], 0.0))
+    for t in range(NV):
+        a = t + 1
+        G(0.25, [], ["PRW%d" % t], ioF(T.PRW[:, 64 * t:64 * t + 64], [[1, 2 ** a], [2 ** a, 2 ** (6 - a)]], 0, 0))
+        pc, pt, pf = T.PCI[:, 4 * t:4 * t + 4], T.PTI[:, 4 * t:4 * t + 4], T.PCF[:, 4 * t:4 * t + 4]
+        V(64, ["JCI1"], ["PCI%d" % t], ts(pc, T.JCI[:, 8:12], 2 ** (6 - a) - 1, None, A.bitwise_and))
+        V(64, ["JCI1"], ["PTI%d" % t], ts(pt, T.JCI[:, 8:12], 6 - a, None, A.arith_shift_right))
+        V(64, ["PCI%d" % t], ["PCF%d" % t], ts(pf, pc, float(2 ** a), None, A.mult))
+        V(64, ["PCF%d" % t, "PTI%d" % t], ["PCG%d" % t], tt(pf, pf, pt, A.add))
+        V(256, ["PRW%d" % t, "PCG%d" % t], ["MK%d" % t],
+          *[ts(T.MK[:, 256 * t + 64 * c:256 * t + 64 * c + 64], T.PRW[:, 64 * t:64 * t + 64], T.PCF[:, 4 * t + c:4 * t + c + 1], 8192.0, A.is_ge, A.mult) for c in range(4)])
+    SC(0, ["q25"], ["lnw"], ac(T.RF[:, 7:8], T.RF[:, 6:7], AF.Ln))
+
+    MM, EQ = T.MM, T.EQ
+    IH = T.IEH[:, 15:143]
+    PLK = ["PL%d" % l for l in range(16)]
+
+    def claims(t, h):
+        k, H, xk = "%d%d" % (t, h), str(h), "X%d" % h
+        o = (2 * t + h) * 64
+        F, Z, X = T.F[:, o:o + 64], T.Z[:, o:o + 64], T[xk]
+        CO, ZX = T["CO" + H], T["ZX" + H]
+        nX = X[:, 384:448]
+        SC(5 * 64, ["F" + k, "BB"], [xk], ac(nX, F, AF.Copy),
+           *[ac(X[:, 128 + 64 * m:192 + 64 * m], F, AF.Identity, bias=T.BB[:, m:m + 1], scale=float(2 ** (4 + m))) for m in range(4)])
+        PE(128, ["Z" + k, "W2", "BLK"], [xk], [(X[:, 0:64], T.W2[:], Z, True, True), (X[:, 64:128], T.BLK[:], Z, True, True)])
+        hh, u1 = T.UA[:, h, 0:64], T.UI[:, h, :]
+        V(128, [xk], ["UA" + H], ts(T.UA[:, h, :], X[:, 0:128], 1.0, None, A.add))
+        V(64, ["UA" + H], ["UI" + H], ts(u1, hh, 4095, None, A.bitwise_and))
+        V(64, [xk, "UI" + H], ["QI" + H], tt(T.QI[:, h, :], nX, u1, A.mult))
+        V(64, ["QI" + H], ["UAh" + H], ts(hh, T.QI[:, h, :], 1, None, A.arith_shift_right))
+        V(256, [xk, "UAh" + H], ["HM" + H], *[tt(T.HM[:, h, 64 * m:64 * m + 64], X[:, 128 + 64 * m:192 + 64 * m], hh, A.add) for m in range(4)])
+        V(256, ["HM" + H], ["C4" + H], *[ts(T.C4[:, h, 64 * m:64 * m + 64], T.HM[:, h, 64 * m:64 * m + 64], 4 + m, 4095, A.arith_shift_right, A.bitwise_and) for m in range(4)])
+        V(256, ["C4" + H], ["CO" + H], cp(CO[:], T.C4[:, h, :]))
+        if ZXP[h]:
+            PE(128, ["Z" + k, "IEB"], ["HA"], [(T.HA[0:64, 0:128], Z, T.IEB[:, 15:143], True, True)])
+            SC(128, ["HA"], ["ZT" + H], ac(T.ZT[0:64, h, :], T.HA[0:64, 0:128], AF.Copy))
+            for b, bk in ((0, "HB"), (1, "HA")):
+                PE(512, ["ZT" + H, "EX0", "EX1"], [bk], [(T[bk][:], T.ZT[0:64, h, :], T.EX[0:64, 512 * b:512 * b + 512], True, True)])
+                SC(512, [bk], ["ZX%s%d" % (H, 8 * b), "ZX%s%d" % (H, 8 * b + 4)], ac(ZX[:, 512 * b:512 * b + 512], T[bk][:], AF.Copy))
+        else:
+            for b in range(0, 16, 4):
+                if b < ZXV[h]:
+                    V(256, ["Z" + k], ["ZX%s%d" % (H, b)], *[cp(ZX[:, p:1024:16], Z) for p in range(b, b + 4)])
+                else:
+                    SC(256, ["Z" + k], ["ZX%s%d" % (H, b)], *[ac(ZX[:, p:1024:16], Z, AF.Copy) for p in range(b, b + 4)])
+        V(64, ["UA" + H], ["SI" + H], ts(T.SI[:, h, :], T.UA[:, h, 64:128], 15, None, A.bitwise_and))
+        V(256, [xk, "C4" + H], ["DN" + H], *[tt(T.DN[:, h, 64 * m:64 * m + 64], T.C4[:, h, 64 * m:64 * m + 64], nX, A.subtract) for m in range(4)])
+        V(64, ["UI" + H], ["UF" + H], ts(T.UF[:, h, :], T.UI[:, h, 1:64:2], -1.0, 0.5, A.add, A.mult))
+        V(128, ["SI" + H, "rp1"], ["SM" + H], *[ts(T.SM[:, h, 32 * b:32 * b + 32], T.SI[:, h, b:64:2], T.RF[:, 3:4], None, A.is_equal) for b in range(2)])
+        zb = T.ZB[:, h, :]
+        SC(64, ["Z" + k], ["ZB" + H], *[ac(T.ZB[:, h, 32 * b:32 * b + 32], T.Z[:, o + b:o + 64:2], AF.Copy) for b in range(2)])
+        SC(64, ["ZB" + H], ["Z5" + H], ac(T.Z5[:, h, :], zb, AF.Copy, bias=-0.5))
+        SC(64, ["ZB" + H], ["Z4" + H], ac(T.Z4[:, h, :], zb, AF.Copy, scale=0.25, bias=129 - 0.375))
+        PE(128, ["ZB" + H, "Z4" + H, "IEB"], [xk], [(X[:, 0:64], T.IEB[:, 15:143], T.Z4[:, h, :], True, False), (X[:, 0:64], T.IEB[:, 15:143], zb, False, True)])
+        PE(256, ["F" + k, "I32"], [xk], [(X[:, 448:512], T.I32[:], F, True, False)])
+
+    def moves(t, h):
+        k, H = "%d%d" % (t, h), str(h)
+        kk = BANKS[2 + h]
+        KK = T[kk]
+        CO, ZX = T["CO" + H], T["ZX" + H]
+        o = (2 * t + h) * 64
+        for m in range(4):
+            d, n = "D%d%d" % (h, m), "N%d%d" % (h, m)
+            dm, nm = T.D[:, h, 1024 * m:1024 * m + 1024], T.NR[:, h, 1024 * m:1024 * m + 1024]
+            zk = ["ZX%s%d" % (H, b) for b in range(0, 16, 4)]
+            win = T.ROCK[:, 0:4096].indirect(CO[:, 64 * m:64 * m + 64])
+            if m in SG:
+                xg = T["XG" + H]
+                SC(1536, RK + ["CO" + H], ["XG" + H], ac(xg[:], win, AF.Copy))
+                for b, bk in ((0, "HA"), (1, "HB")):
+                    PE(1024, ["XG" + H, "IEB", "NI"] + zk, [bk], [(T[bk][:], T.IEB[:, 15:143], xg[:, 512 * b:512 * b + 512], True, False),
+                                                                (T[bk][:], T.NI[:], ZX[:, 512 * b:512 * b + 512], False, True)])
+                    SC(512, [bk], [d + "ab"[b]], ac(T.D[:, h, 1024 * m + 512 * b:1024 * m + 512 * b + 512], T[bk][:], AF.Abs))
+            else:
+                V(60 + 1536, RK + ["CO" + H] + zk, [d + "a", d + "b"], tt(dm, win, ZX[:], A.subtract))
+                SC(1024, [d + "a", d + "b"], [d + "a", d + "b"], ac(dm, dm, AF.Abs))
+            if m in NEARV[h]:
+                V(512, [d + "a", d + "b", "TOP%d" % t], [n + "a", n + "b"], ts(nm, dm, T.TOP[:, t:t + 1], None, A.is_le))
+            else:
+                SC(1024, [d + "a", d + "b", "TOP%d" % t], [n + "a", n + "b"], ac(nm, dm, AF.Sign, bias=T.TOP[:, t:t + 1], scale=-1.0))
+
+        def keys(m, near):
+            w, src, b = (("R1B" if m in NEARV[h] else "R05"), T.NR, "N") if near else ("R256", T.D, "D")
+            PE(1024, ["%s%d%d%s" % (b, h, m, x) for x in "ab"] + [w], [kk], [(KK[:, 64 * m:64 * m + 64], T[w][:, 15 - p:143 - p], src[:, h, 1024 * m + p:1024 * m + 1024:16], False, near and m % 2 == 1 and p == 15) for p in range(16)])
+        for b in (0, 1):
+            PE(128, ["ALLC"] + ["K1%d%d" % (h, m) for m in range(4)], [kk], [(KK[:, 128 * b:128 * b + 128], T.ALLC[:], T.K1[:, h, 128 * b:128 * b + 128], True, False)])
+            for m, near in ((0, 0), (1, 0), (0, 1), (1, 1)):
+                keys(2 * b + m, bool(near))
+            if b == 0:
+                SC(128, [kk], ["KS" + H], ac(T.KS[:, h, :], KK[:, 0:128], AF.Copy))
+        V(128, [kk, "KS" + H], ["KM" + H], tt(T.KM[:, h, :], KK[:, 128:256], T.KS[:, h, :], A.min))
+        V(128, ["KM" + H], ["KB" + H], tt(T.KB[:, h, :], T.KM[:, h, 0:64], T.KM[:, h, 64:128], A.min))
+        V(64, ["KB" + H], ["KC" + H], ts(T.KC[:, h, :], T.KB[:, h, :], 255, 5, A.bitwise_and, A.arith_shift_right))
+        V(256, ["KC" + H], [kk], *[ts(KK[:, 256 + 64 * m:320 + 64 * m], T.KC[:, h, :], float(2 * m + 1), None, A.is_equal) for m in range(4)])
+        V(256, [kk, "DN" + H], ["PR" + H], tt(T.PR[:, h, :], KK[:, 256:512], T.DN[:, h, :], A.mult))
+        X = T["X" + H]
+        PE(4 * 256, ["PR" + H, "I32"], ["X" + H], [(X[:, 448:512], T.I32[:], T.PR[:, h, 64 * m:64 * m + 64], False, m == 3) for m in range(4)])
+
+    def meetings(t, h):
+        k, H = "%d%d" % (t, h), str(h)
+        o = (2 * t + h) * 64
+        kk, xk = BANKS[2 + h], "X" + H
+        KK, NP = T[kk], T[xk][:, 448:512]
+        HW, LS, FO = T["HW" + H], T["LS" + H], T.FO
+        SS, JJ = T.NS[:, h, 0:64:2], T.NS[:, h, 1:64:2]
+        V(64, [xk], ["HF" + H], ts(T.HF[:, h, :], NP, 0.125, 1025 - 0.4375, A.mult, A.add))
+        V(64, [xk], ["JC" + H], ts(T.JC[:, h, 0:32], T[xk][:, 449:512:2], -2048.0, None, A.add))
+        V(64, [xk], ["JS" + H], ts(T.JC[:, h, 32:64], T[xk][:, 448:512:2], -1.0, 2048.0, A.mult, A.add))
+        SC(64, [xk], ["NS" + H], ac(T.NS[:, h, :], NP, AF.Copy))
+        SC(64, ["NS" + H], ["S2" + H], ac(T.S2[:, h, :], T.NS[:, h, :], AF.Copy, bias=-2048.0))
+        for b, bk in ((0, "EQ"), (1, "MM")):
+            mm = []
+            for l in range(8):
+                dd = T[bk][:, 32 * l:32 * l + 32]
+                mm.append((dd, IH, T.HF[:, h, 1:64:2], True, False))
+                mm.append((dd, T.EL[:, 128 * (8 * b + l):128 * (8 * b + l) + 128], T.HF[:, h, 0:64:2], False, True))
+            PE(16 * 64, ["HF" + H, "IEH"] + ["EL%d" % l for l in range(16)], [bk], mm)
+            V(256, [bk], ["EQB%s%d" % (H, b)], ts(T.EQB[:, h, 256 * b:256 * b + 256], T[bk][:, 0:256], 0.0, None, A.is_equal))
+            PE(512, ["EQB%s%d" % (H, b)] + PLK, [kk], [(KK[:, 256:288], T.PL[:, 128 * l:128 * l + 128], T.EQB[:, h, 32 * l:32 * l + 32], l == 0, l == 15) for l in range(8 * b, 8 * b + 8)])
+        pm = T.PM[:, h, :]
+        for bk, s0, s1 in [("HA" if x < 16 else "HB", max(x, 1), x + 4) for x in range(0, 32, 4)]:
+            mm = []
+            for s in range(s0, s1):
+                dd = T[bk][:, 32 * (s % 16):32 * (s % 16) + 32]
+                mm += [(dd, T.IEH[:, s - 1:s + 127], T.JC[:, h, 0:32], True, False), (dd, IH, T.JC[:, h, 32:64], False, True)]
+            PE(64 * len(mm), ["JC" + H, "JS" + H, "IEH"], [bk], mm)
+        V(64, [kk], ["PM" + H], ts(pm, KK[:, 256:288], 0.0, None, A.max))
+        PE(192, ["PM" + H, "Q2", "BLK", "UPI"], [kk], [(KK[:, 288:320], T.Q2[:], pm, True, True), (KK[:, 320:352], T.BLK[:], pm, True, True),
+                                                       (KK[:, 352:384], T.UPI[:], pm, True, True)])
+        SC(64, [kk, "lnw"], ["LN" + H], ac(T.LN[:, h, :], KK[:, 288:352], AF.Ln, bias=T.RF[:, 6:7]))
+        SC(480, ["HA"], ["HWa" + H], ac(HW[:, 32:512], T.HA[:, 32:512], AF.Copy))
+        SC(512, ["HB"], ["HWb" + H], ac(HW[:, 512:1024], T.HB[:, 0:512], AF.Copy))
+        V(64, ["LN" + H], ["XX" + H], ts(T.XX[:, h, :], T.LN[:, h, :], 1.0 / math.log(4.0), 1024.0, A.mult, A.add))
+        V(64, [kk], ["JM" + H], ts(T.JM[:, h, :], KK[:, 352:384], 0.0, None, A.is_gt))
+        PE(17 * 64, ["XX" + H, "R2H", "PCH", "IEH"], [kk], [(KK[:, 128:130], IH, T.PCH[:], True, False)] +
+           [(KK[:, 128:130], T.R2H[:, 15 - p:143 - p], T.XX[:, h, p:32:16], False, p == 15) for p in range(16)])
+        ji, ju, dj = T.JI[:, h, :], T.JU[:, h, :], T.DJ[:, h, :]
+        V(64, ["NS" + H], ["JI" + H], tt(ji, JJ, SS, A.mult))
+        V(64, ["NS" + H, "UF" + H], ["JU" + H], tt(ju, JJ, T.UF[:, h, :], A.add))
+        V(64, ["JI" + H], ["JI" + H], ts(ji, ji, 5, None, A.arith_shift_right))
+        V(64, ["JI" + H, "JU" + H], ["JU" + H], tt(ju, ji, ju, A.add))
+        V(64, ["JU" + H], ["JU" + H], ts(ju, ju, 4095, None, A.bitwise_and))
+        V(64, ["JU" + H, "NS" + H], ["DJ" + H], tt(dj, ju, JJ, A.subtract))
+        V(64, ["DJ" + H, "JM" + H], ["DJ" + H], tt(dj, dj, T.JM[:, h, :], A.mult))
+        V(64, ["DJ" + H, "S2" + H], ["FCj" + H], tt(T.FC[:, h, 32:64], dj, T.S2[:, h, 1:64:2], A.add))
+        SC(32, ["FCj" + H], ["FOj" + k], ac(FO[:, o + 32:o + 64], T.FC[:, h, 32:64], AF.Copy, bias=2048.0))
+        jg = T.JG[:, h, :]
+        V(64, ["XX" + H, "c1"], ["CDa" + H], ts(T.CD[:, h, 0:32], T.XX[:, h, 32:64], T.RF[:, 4:5], None, A.is_gt))
+        V(64, ["XX" + H, "c2"], ["CDb" + H], ts(T.CD[:, h, 32:64], T.XX[:, h, 0:32], T.RF[:, 5:6], None, A.is_le))
+        V(64, ["CDa" + H, "CDb" + H], ["CD" + H], tt(T.CD[:, h, 64:96], T.CD[:, h, 0:32], T.CD[:, h, 32:64], A.mult))
+        V(64, [kk], ["LS" + H], ts(LS[:], KK[:, 128:130], -32.0 * 1023, None, A.add))
+        V(110, ["LS" + H, "CD" + H, "HWz" + H, "HWa" + H, "HWb" + H], ["JG" + H], tt(jg, HW[:].indirect(LS[:]), T.CD[:, h, 64:96], A.mult))
+        V(64, ["JG" + H, "S2" + H], ["FCs" + H], tt(T.FC[:, h, 0:32], jg, T.S2[:, h, 0:64:2], A.add))
+        SC(32, ["FCs" + H], ["FOs" + k], ac(FO[:, o:o + 32], T.FC[:, h, 0:32], AF.Copy, bias=2048.0))
+
+    def send(kind, t, h, R):
+        if t == NV - 1:
+            return
+        dst = T.cores[(rank + 3) % 8]
+        rid, pid, _ = topo.addr(dst)
+        n, mask = len(topo.engines(core, dst)), topo.mask(core, dst)
+        o = (2 * t + h) * 64
+        src, out = (T.FO, T.F) if kind == "f" else (T.ZO, T.Z)
+        sem = "ar%s%d%d" % (kind, t + 1, h)
+        add(S, "g", 0.1, R, [("F" if kind == "f" else "Z") + "%d%d" % (t + 1, h)],
+            lambda: g.remote_dma(out[:, o + 128:o + 192], src[:, o:o + 64], T.sem[sem], T.sem.sl, pid, rid, mask), (sem, n), 2.2)
+        S["sends"] += n
+
+    def mining(t, h):
+        k, H = "%d%d" % (t, h), str(h)
+        o = (2 * t + h) * 64
+        MF, E16 = T.MF, T["E16" + H]
+        ef = T.EF[:, h, 0:4]
+        send("f", t, h, ["FOj" + k, "FOs" + k])
+        V(128, ["FCj" + H, "FCs" + H, "SM" + H], ["MF" + H], tt(MF[:, 64 * h:64 * h + 64], T.FC[:, h, :], T.SM[:, h, :], A.mult))
+        kk, bk = BANKS[2 + h], ("MM", "EQ")[h]
+        KK, DD = T[kk], T[bk]
+        PE(1024, ["MF" + H, "R1H"], [kk], [(KK[:, 160:164], T.R1H[:, 15 - p:143 - p], MF[:, 64 * h + p:64 * h + 64:16], p == 0, p == 15) for p in range(16)])
+        V(64, [kk], ["E16" + H], ts(E16[:], KK[:, 160:164], 2048.0, None, A.add))
+        V(64, [kk], ["EF" + H], cp(ef, KK[:, 160:164]))
+        SC(4, [kk], ["EG" + H], ac(T.EF[:, h, 4:8], KK[:, 160:164], AF.Copy, bias=2048.0))
+        su = T.SU[:, h, :]
+        V(156, RK + ["E16" + H, "Z5" + H], ["SU" + H], tt(su, T.ROCK[:, 0:4096].indirect(E16[:]), T.Z5[:, h, :], A.add))
+        V(64, ["SU" + H], ["Y1" + H], ts(T.Y1[:, h, :], su, 0.5, None, A.mult))
+        V(64, ["Y1" + H], ["ZO" + k], cp(T.ZO[:, o:o + 64], T.Y1[:, h, :]))
+        send("z", t, h, ["ZO" + k])
+        w = 64 + 64 * h
+        mm = []
+        for c in range(4):
+            mm.append((DD[:, c * w:c * w + w], T.BLH[:], MF[:, 0:w], True, False))
+            mm.append((DD[:, c * w + w - 64:c * w + w], IH, T.MK[:, 256 * t + 64 * c:256 * t + 64 * c + 64], False, True))
+        PE(4 * w + 256, ["MF0", "MF" + H, "MK%d" % t, "BLH", "IEH"], [bk], mm)
+        for c in range(4):
+            du = T.DU[:, h, c * w:c * w + w]
+            V(w, [bk, "EF" + H], ["DU%s%d" % (H, c)], ts(du, DD[:, c * w:c * w + w], T.EF[:, h, c:c + 1], 8192.0, A.is_equal, A.mult))
+            j = 4 * h + c
+            lo = T.LO[:, j:j + 1]
+            if c in LOV[h]:
+                V(w, ["DU%s%d" % (H, c)], ["LO%s%d" % (H, c)], (lambda lo, du: lambda: v.tensor_reduce(lo, du, AxisListType.X, A.add))(lo, du))
+            else:
+                SC(w + 24, ["DU%s%d" % (H, c)], ["DU%s%d" % (H, c), "LO%s%d" % (H, c)], ac(du, du, AF.Copy, accum_out=lo))
+            V(64, ["LO%s%d" % (H, c), "DUMP", "EG" + H], ["OF%d" % j], ts(T.OF[:, j:j + 1], lo, T.DUMP[:, j:j + 1], T.EF[:, h, 4 + c:5 + c], A.min, A.max))
+        V(64, ["SU" + H, "X" + H], ["RR" + H], tt(T.RR[:, h, :], su, T["X" + H][:, 0:64], A.subtract))
+        SC(64, ["RR" + H, "b129"], ["RN" + H], ac(T.RN[:, 64 * h:64 * h + 64], T.RR[:, h, :], AF.Relu, bias=T.RF[:, 8:9]))
+
+    names = [(claims, "c"), (moves, "m"), (meetings, "e"), (mining, "i")]
+
+    def stage(f, t, h):
+        S["st"] = [n for f2, n in names if f2 == f][0] + str(h)
+        f(t, h)
+        S["st"] = ""
+
+    for t in range(NV):
+        stage(claims, t, 0)
+        if t == 0:
+            stage(claims, t, 1)
+        stage(moves, t, 0)
+        if t > 0:
+            stage(claims, t, 1)
+        stage(moves, t, 1)
+        stage(meetings, t, 0)
+        stage(meetings, t, 1)
+        stage(mining, t, 0)
+        stage(mining, t, 1)
+        V(60 + 128 * 3.8, ["OF%d" % j for j in range(8)] + ["RN0", "RN1"], RK, cp(T.ROCK[:].indirect(T.OF[:]), T.RN[:]))
+        if t < NV - 1:
+            PE(128, ["JM0", "JM1", "S15"], ["MM"], [(MM[:, 256 + 32 * h:288 + 32 * h], T.S15[:], T.JM[:, h, :], True, True) for h in range(2)])
+            V(64, ["MM"], ["CN"], lambda: v.tensor_reduce(T.CN[:, 0:1], MM[:, 256:320], AxisListType.X, A.add))
+            V(64, ["CN"], ["CI0"], cp(T.CI[:, 0:1], T.CN[:, 0:1]))
+            V(64, ["CI0"], ["CI1"], ts(T.CI[:, 1:2], T.CI[:, 0:1], 3, None, A.bitwise_and))
+            V(64, ["CI1", "LIM"], ["TOP%d" % (t + 1)], ts(T.TOP[:, t + 1:t + 2], T.CI[:, 1:2], T.LIM[:, 0:1], None, A.add))
+    t = NV - 1
+    for h in range(2):
+        o = (2 * t + h) * 64
+        for b in range(2):
+            c = 64 * h + 32 * b
+            SC(32, ["FOj%d%d" % (t, h), "FOs%d%d" % (t, h)], ["YF%d%d" % (h, b)], ac(T.YF[:, c:c + 32], T.FO[:, o + b:o + 64:2], AF.Copy))
+            SC(32, ["ZO%d%d" % (t, h)], ["YZ%d%d" % (h, b)], ac(T.YZ[:, c:c + 32], T.ZO[:, o + b:o + 64:2], AF.Copy))
+    hb = ["00", "01", "10", "11"]
+    add(S, "y", 0.06, ["YF" + x for x in hb], ["oF"], lambda: g.sync.dma_start(T.yf[:], T.YF[:]).then_inc(T.sem.od_f, 16), ("od_f", 16), 2.0)
+    add(S, "y", 0.06, ["YZ" + x for x in hb], ["oZ"], lambda: g.sync.dma_start(T.yz[:], T.YZ[:]).then_inc(T.sem.od_z, 16), ("od_z", 16), 2.0)
+    add(S, "y", 0.06, RK, ["oX"], lambda: g.sync.dma_start(T.yx[:], T.ROCK[:, 0:4096]).then_inc(T.sem.od_x, 16), ("od_x", 16), 5.0)
+    return S
+
+
+def rank_program(g, core, T, topo):
+    if T.rank_of(core) is None:
+        return
+    S = record(g, core, T, topo)
+    order = plan(S)
+    eng = {"v": g.vector, "s": g.scalar, "t": g.tensor, "g": g, "y": g.sync}
+    cnt = issue(S, order, eng, T)
+    for s in sorted(cnt):
+        g.wait_ge(T.sem[s], cnt[s])
+    for s in ("od_f", "od_z", "od_x"):
+        g.wait_ge(T.sem[s], 16)
+    g.wait_ge(T.sem.sl, S["sends"])

@@ -1,76 +1,75 @@
-import math
 from concourse.mybir import AluOpType as A, ActivationFunctionType as AF, AxisListType
 
 NV = 5
-NEARV = ((0, 1, 2, 3), (0, 1, 2, 3))
-SG = (0,)
-ZXV = (16, 0)
+NG = 32
+INT = True
 SCRATCH = {
     "PI": ("sbuf", [128, 8], "int32"), "RF": ("sbuf", [128, 16], "float32"),
-    "ONES": ("sbuf", [128, 160], "bfloat16"), "IEB": ("sbuf", [128, 160], "bfloat16"),
-    "IEH": ("sbuf", [128, 160], "float16"), "I32": ("sbuf", [128, 128], "float32"),
-    "GR": ("sbuf", [128, 128], "float32"), "CR": ("sbuf", [128, 128], "float32"),
-    "XR": ("sbuf", [128, 144], "float32"), "T32": ("sbuf", [128, 128], "float32"),
-    "BLK": ("sbuf", [128, 128], "bfloat16"), "BLH": ("sbuf", [128, 128], "float16"),
-    "R256": ("sbuf", [128, 144], "bfloat16"), "R05": ("sbuf", [128, 144], "bfloat16"), "R1B": ("sbuf", [128, 144], "bfloat16"),
-    "R1H": ("sbuf", [128, 144], "float16"), "R2H": ("sbuf", [128, 144], "float16"), "NI": ("sbuf", [128, 128], "bfloat16"),
-    "EX": ("sbuf", [128, 1024], "bfloat16"), "EX1": ("sbuf", [128, 512], "bfloat16"), "ZT": ("sbuf", [128, 2, 128], "bfloat16"),
-    "XG0": ("sbuf", [128, 1024], "bfloat16"), "XG1": ("sbuf", [128, 1024], "bfloat16"),
-    "KM16": ("sbuf", [128, 16], "float32"), "KT": ("sbuf", [128, 16], "float32"),
-    "P4": ("sbuf", [128, 16], "float32"), "P4C": ("sbuf", [128, 1], "float32"),
-    "EL": ("sbuf", [128, 16 * 128], "bfloat16"), "NEG": ("sbuf", [128, 128], "bfloat16"), "PL": ("sbuf", [128, 16 * 128], "bfloat16"),
-    "SLB": ("sbuf", [128, 128], "bfloat16"), "Q2": ("sbuf", [128, 128], "bfloat16"),
-    "UPI": ("sbuf", [128, 128], "bfloat16"), "S15": ("sbuf", [128, 128], "bfloat16"),
-    "ALLC": ("sbuf", [128, 128], "bfloat16"), "K1": ("sbuf", [128, 2, 256], "bfloat16"),
-    "BB": ("sbuf", [128, 4], "float32"), "PCH": ("sbuf", [128, 2], "float16"),
-    "DUMP": ("sbuf", [128, 8], "float32"), "MK": ("sbuf", [128, 5 * 256], "float16"),
-    "PRW": ("sbuf", [128, 5 * 64], "float32"), "JCI": ("sbuf", [128, 16], "int32"),
-    "PCI": ("sbuf", [128, 5 * 4], "int32"), "PTI": ("sbuf", [128, 5 * 4], "int32"),
-    "PCF": ("sbuf", [128, 5 * 4], "float32"),
-    "W2": ("sbuf", [128, 128], "bfloat16"), "WI": ("sbuf", [128, 2], "int32"),
-    "WF": ("sbuf", [128, 2], "float32"), "LIM": ("sbuf", [128, 1], "float32"),
-    "TOP": ("sbuf", [128, 8], "float32"), "CN": ("sbuf", [128, 4], "float32"), "CI": ("sbuf", [128, 4], "int32"),
-    "FI": ("sbuf", [128, 128], "int32"),
-    "F": ("sbuf", [128, NV * 128], "float32"), "FO": ("sbuf", [128, NV * 128], "float32"),
-    "Z": ("sbuf", [128, NV * 128], "bfloat16"), "ZO": ("sbuf", [128, NV * 128], "bfloat16"),
-    "ROCK": ("sbuf", [128, 4096 + 128], "bfloat16"),
-    "YF": ("sbuf", [128, 128], "float32"), "YZ": ("sbuf", [128, 128], "bfloat16"),
-    "MF": ("sbuf", [128, 128], "float16"), "RN": ("sbuf", [128, 128], "bfloat16"),
-    "OF": ("sbuf", [128, 8], "uint16"), "LO": ("sbuf", [128, 8], "float32"),
+    "ONES": ("sbuf", [128, 128], "bfloat16"), "NEG": ("sbuf", [128, 128], "bfloat16"), "IB": ("sbuf", [128, 128], "bfloat16"),
+    "I32": ("sbuf", [128, 128], "float32"), "NI32": ("sbuf", [128, 128], "float32"), "ONE32": ("sbuf", [128, 128], "float32"),
+    "PERM": ("sbuf", [128, 128], "float32"),
+    "GR": ("sbuf", [128, 128], "bfloat16"), "CR": ("sbuf", [128, 128], "bfloat16"), "G4": ("sbuf", [128, 128], "bfloat16"),
+    "XR": ("sbuf", [128, 144], "bfloat16"), "RW": ("sbuf", [128, 144], "bfloat16"), "BLK": ("sbuf", [128, 128], "bfloat16"),
+    "T1": ("sbuf", [128, 128], "float32"), "T2": ("sbuf", [128, 128], "float32"), "T3": ("sbuf", [128, 128], "bfloat16"),
+    "T4": ("sbuf", [128, 128], "bfloat16"), "TI": ("sbuf", [128, 128], "int32"), "P4": ("sbuf", [128, 128], "float32"),
+    "KT": ("sbuf", [128, 16], "float32"), "NKT": ("sbuf", [128, 16], "float32"), "KH": ("sbuf", [128, 8], "float32"),
+    "SCM": ("sbuf", [128, 4, 128], "bfloat16"), "L3": ("sbuf", [128, 128], "bfloat16"), "R3": ("sbuf", [128, 320], "bfloat16"),
+    "WD": ("sbuf", [128, 16], "bfloat16"), "CM": ("sbuf", [128, 256], "bfloat16"), "RS": ("sbuf", [128, 128], "bfloat16"),
+    "XK": ("sbuf", [128, 144], "bfloat16"), "RK": ("sbuf", [128, 2, 144], "bfloat16"), "NIB": ("sbuf", [128, 128], "bfloat16"),
+    "R1": ("sbuf", [128, 32], "bfloat16"), "CJ": ("sbuf", [128, 32], "bfloat16"),
+    "EL": ("sbuf", [128, 16, 128], "bfloat16"), "PL": ("sbuf", [128, 16, 128], "bfloat16"), "CS": ("sbuf", [128, 16, 128], "bfloat16"),
+    "SLB": ("sbuf", [128, 128], "bfloat16"), "QQ": ("sbuf", [128, 3, 128], "bfloat16"), "WX": ("sbuf", [128, 3, 128], "bfloat16"),
+    "S15": ("sbuf", [128, 128], "bfloat16"), "I32B": ("sbuf", [128, 128], "bfloat16"), "HB": ("sbuf", [128, 3, 128], "bfloat16"),
+    "SEL": ("sbuf", [128, 4, 128], "bfloat16"), "GS": ("sbuf", [128, 8, 128], "bfloat16"), "BK": ("sbuf", [128, 4, 128], "bfloat16"),
+    "CL": ("sbuf", [128, NV, 128], "bfloat16"), "MK": ("sbuf", [128, NV, 128], "bfloat16"), "DUMP": ("sbuf", [128, 8], "float32"),
+    "QR": ("sbuf", [128, 128], "bfloat16"),
+    "WI": ("sbuf", [128, 2], "int32"), "WL": ("sbuf", [128, 2], "bfloat16"), "W2": ("sbuf", [128, 2, 128], "bfloat16"),
+    "LIM": ("sbuf", [128, 2], "float32"), "TOP": ("sbuf", [128, 2, 8], "float32"), "CN": ("sbuf", [128, 4], "float32"),
+    "CI": ("sbuf", [128, 4], "int32"),
+    "FI": ("sbuf", [128, 2, 64], "int32"),
+    "F": ("sbuf", [128, 2 * NV, 64], "float16"), "FO": ("sbuf", [128, 2 * NV, 64], "float16"),
+    "Z": ("sbuf", [128, 2 * NV, 64], "bfloat16"), "ZO": ("sbuf", [128, 2 * NV, 64], "bfloat16"),
+    "YF": ("sbuf", [128, 2, 64], "float32"), "YZ": ("sbuf", [128, 2, 64], "bfloat16"),
 }
-for _n, _w, _d in (("UA", 128, "int32"), ("UI", 64, "int32"), ("SI", 64, "int32"), ("QI", 64, "int32"),
-                   ("HM", 256, "int32"), ("C4", 256, "int32"), ("DN", 256, "float32"),
-                   ("UF", 32, "float32"), ("SM", 64, "float32"), ("ZB", 64, "bfloat16"), ("Z5", 64, "float32"),
-                   ("Z4", 64, "bfloat16"), ("KS", 128, "float32"), ("KM", 128, "float32"),
-                   ("KB", 64, "int32"), ("KC", 64, "int32"), ("PR", 256, "float32"), ("HF", 64, "float16"), ("JC", 64, "float16"),
-                   ("NS", 64, "float32"), ("S2", 64, "float32"), ("EQB", 512, "bfloat16"),
-                   ("PM", 32, "bfloat16"), ("LN", 64, "float32"), ("JM", 32, "bfloat16"), ("XX", 64, "float16"),
-                   ("JG", 32, "float32"), ("CD", 96, "bfloat16"), ("JI", 32, "int32"),
-                   ("JU", 32, "int32"), ("DJ", 32, "float32"), ("FC", 64, "float32"),
-                   ("EF", 8, "float32"), ("SU", 64, "float32"), ("Y1", 64, "int32"), ("RR", 64, "float32"),
-                   ("DU", 512, "bfloat16"), ("OT", 8, "float32"), ("D", 4096, "bfloat16"), ("NR", 4096, "bfloat16")):
+for _n, _w, _d in (("UA", 128, "int32"), ("UI", 320, "int32"), ("SI", 64, "int32"), ("QI", 64, "int32"), ("HM", 320, "int32"),
+                   ("C4", 256, "int32"), ("UF", 32, "float32"), ("Z4", 64, "bfloat16"), ("KE", 128, "float32"),
+                   ("KS", 256, "int32" if INT else "float32"),
+                   ("KB", 64, "int32"), ("KC", 64, "int32"), ("NB", 64, "int32"), ("PR", 320, "float32"), ("HF", 64, "float16"),
+                   ("JC", 64, "float16"), ("NS", 64, "float32"), ("EQB", 512, "bfloat16"), ("PM", 32, "bfloat16"),
+                   ("MS", 128, "bfloat16"), ("SX", 32, "float32"), ("JI", 32, "float32"), ("JU", 32, "int32"), ("JX", 32, "int32"),
+                   ("DF", 64, "float32"), ("DM", 64, "float32"), ("MF", 128, "float16"), ("EF", 8, "float32"), ("YA", 128, "bfloat16"),
+                   ("LO", 4, "float32"), ("LX", 32, "bfloat16"), ("OT", 8, "float32"), ("RN", 128, "bfloat16"),
+                   ("D", 4096, "bfloat16"), ("NR", 4096, "bfloat16")):
     SCRATCH[_n] = ("sbuf", [128, 2, _w], _d)
-for _h in "01":
-    for _n, _w, _d in (("CO", 256, "uint16"), ("ZX", 1024, "bfloat16"), ("HW", 1024, "float32"), ("LS", 2, "uint16"), ("E16", 4, "uint16")):
-        SCRATCH[_n + _h] = ("sbuf", [128, _w], _d)
-BANKS = ["X0", "X1", "K0", "K1b", "EQ", "HA", "HB", "MM"]
+for _s in "01":
+    for _n, _w, _d in (("ROCK", 4096 + 128, "bfloat16"), ("CO", 256, "uint16"), ("ZX", 16 * NG, "bfloat16"), ("HW", 512, "float32"),
+                       ("LS", 2, "uint16"), ("E16", 8, "uint16"), ("OF", 8, "uint16")):
+        SCRATCH[_n + _s] = ("sbuf", [128, _w], _d)
+BANKS = ["X0", "X1", "K0", "K1", "KX", "EQ", "HT", "MM"]
 for _n in BANKS:
     SCRATCH[_n] = ("psum", [128, 512], "float32")
 
-LOADS = ["wi", "li", "fr", "v0", "v1", "r0", "r1", "r2", "r3"]
-SEMAPHORES = (["sv", "ss", "st", "sg", "sl"] + ["ld_" + n for n in LOADS] + ["od_f", "od_z", "od_x"] +
-              ["ar%s%d%d" % (k, t, h) for k in "fz" for t in range(1, NV) for h in range(2)])
+LOADS = ["wi", "li"] + [n + s + a for n in "fvr" for s in "01" for a in "01"]
+STORES = [n + s + a for n in "fzx" for s in "01" for a in "01"]
+SEMAPHORES = (["sv", "ss", "st", "sg", "sl"] + ["ld_" + n for n in LOADS] + ["od_" + n for n in STORES] +
+              ["ar%s%d%d" % (k, t, s) for k in "fz" for t in range(1, NV) for s in range(2)])
 QSEM = {"v": "sv", "s": "ss", "t": "st", "g": "sg"}
-ZXP = (1, 1)
-BIAS = {'e1': 0.5, 'm0s': 1.0, 'i0t': -2.5, 'e1t': -5.0, 'c1v': -0.5, 'c0s': -1.0, 'c0t': 13.5, 'm0t': -6.5, 'c0v': -1.0, 'i1t': -6.5,
-        'e1v': -2.0, 'e1s': 4.0, 'e0v': 0.5, 'm1': -2.0, 'c1t': -6.5, 'e0': 0.5, 'i1s': 3.5, 'm1s': -2.0, 'm1v': 0.5, 'c0': 1.0,
-        'e0t': -4.0, 'i0s': -3.5, 'm1t': -1.5, 'e0s': 6.5}
-LOOK = 0.0
-LOV = ((), (1, 3))
-CYC = 0.00104
-PEC = 0.0003
-LAT = 0.15
-SFIX = 78
+CYC = 0.00085
+PEC = 0.00043
+LAT = 0.28
+DML = 1.8
+GAT = 1.56
+SCA = 3.8
+SFIX = 70
+BIAS = {}
+SGRP = 2
+VP = 2
+LOOK = 0.4
+ZV = 4
+ABS = (6, 8, 10, 12)
+NPC = 512
+OPT = {"lx": "v", "rn": "s", "ya": "v", "ke": "s", "ef": "v"}
+PLANS = {}
 
 
 def add(S, q, cost, reads, writes, fn, sig=None, lat=0.0):
@@ -82,8 +81,8 @@ def add(S, q, cost, reads, writes, fn, sig=None, lat=0.0):
             deps[j] = deps.get(j, False) or sem
     for k in reads + writes:
         if k in BANKS:
-            for q2, (j, wr) in S["b"].setdefault(k, {}).items():
-                dep(j, q2 != q or (wr and k in reads))
+            for q2, j in S["b"].setdefault(k, {}).items():
+                dep(j, q2 != q)
     for k in reads:
         if k not in BANKS:
             for j in S["w"].get(k, []):
@@ -94,8 +93,7 @@ def add(S, q, cost, reads, writes, fn, sig=None, lat=0.0):
                 dep(j, True)
     for k in reads + writes:
         if k in BANKS:
-            acc = S["b"][k]
-            acc[q] = (i, k in writes or (q in acc and acc[q][1] and k not in reads))
+            S["b"][k][q] = i
         elif k in writes:
             S["w"][k] = [i]
             S["r"][k] = []
@@ -114,13 +112,20 @@ def plan(S):
         for j in o["deps"]:
             succ[j].append(i)
     pri = [0.0] * n
-    for i in range(n - 1, -1, -1):
+    left = [len(x) for x in succ]
+    back = [i for i in range(n) if left[i] == 0]
+    for i in back:
+        for j in ops[i]["deps"]:
+            left[j] -= 1
+            if left[j] == 0:
+                back.append(j)
+    for i in back:
         o = ops[i]
         b = 0.0
         for k in succ[i]:
             b = max(b, pri[k] + (o["lat"] if o["sig"] else (LAT if ops[k]["deps"][i] else 0.0)))
         pri[i] = b + o["cost"]
-    pri = [p + BIAS.get(o["st"], 0.0) + BIAS.get(o["st"] + o["q"], 0.0) for p, o in zip(pri, ops)]
+    pri = [p + BIAS.get(o["st"][:1] + o["q"] + o["nm"][:2], 0.0) for p, o in zip(pri, ops)]
     left = [len(o["deps"]) for o in ops]
     ready = {}
     est = [0.0] * n
@@ -198,7 +203,7 @@ def issue(S, order, eng, T):
 
 def record(g, core, T, topo):
     rank = T.rank_of(core)
-    S = {"ops": [], "w": {}, "r": {}, "b": {}, "sends": 0}
+    S = {"ops": [], "w": {}, "r": {}, "b": {}, "sends": 0, "last": {}}
     v, sc, te = g.vector, g.scalar, g.tensor
 
     def seq(calls):
@@ -217,8 +222,8 @@ def record(g, core, T, topo):
     def PE(cyc, R, W, mms):
         return add(S, "t", cyc * PEC, R, W, seq([(lambda m: lambda: te.matmul(*m))(m) for m in mms]))
 
-    def G(cost, R, W, call):
-        return add(S, "g", cost, R, W, call)
+    def G(n, R, W, *calls):
+        return add(S, "g", (0.17 + 2 * n * CYC) * len(calls), R, W, seq(calls))
 
     def ts(out, in0, s1, s2, op0, op1=None):
         if op1 is None:
@@ -237,328 +242,430 @@ def record(g, core, T, topo):
     def ms(ap, c):
         return lambda: v.memset(ap, c)
 
-    def load(q, name, out, in_, W, lat):
-        e = g.sync if q == "y" else g.scalar
-        add(S, q, 0.06, [], W, lambda: e.dma_start(out, in_).then_inc(T.sem["ld_" + name], 16), ("ld_" + name, 16), lat)
-
-    load("y", "fr", T.FI[:], T.front[:], ["FI"], 2.2)
-    load("s", "v0", T.Z[:, 0:64], T.vein[:, 0:64], ["Z00"], 2.2)
-    load("y", "wi", T.WI[:, 0:1], T.w[:], ["WI0"], 2.2)
-    load("y", "li", T.WI[:, 1:2], T.lim[:], ["WI1"], 2.2)
-    load("s", "v1", T.Z[:, 64:128], T.vein[:, 64:128], ["Z01"], 2.2)
-    for b in range(4):
-        load("y", "r%d" % b, T.ROCK[:, 1024 * b:1024 * b + 1024], T.rock[:, 1024 * b:1024 * b + 1024], ["ROCK%d" % b], 5.0)
-    RK = ["ROCK%d" % b for b in range(4)]
+    def scan(out, d0, d1, init, op0, op1):
+        return lambda: v.tensor_tensor_scan(out, d0, d1, init, op0, op1)
 
     def ioF(ap, pat, base, cm):
         return lambda: g.iota(ap, pat, base, cm, allow_small_or_imprecise_dtypes=True)
 
     def ioI(ap, pat, base, cm):
         return lambda: g.iota(ap, pat, base, cm)
-    G(0.15, [], ["PI"], ioI(T.PI[:, 0:1], [[1, 1]], 0, 1))
-    G(0.35, [], ["GR"], ioF(T.GR[:], [[1, 8], [0, 16]], 0, 0))
-    G(0.35, [], ["XR"], ioF(T.XR[:, 0:143], [[1, 143]], -15, 0))
+
+    def sel(out, a, pat, op, fill, base, cm):
+        return lambda: g.affine_select(out, a, pat, op, fill, base, cm)
+
+    def dma(q, sem, out, in_, R, W, lat):
+        e = g.sync if q == "y" else g.scalar
+        add(S, q, 0.06, R, W, lambda: e.dma_start(out, in_).then_inc(T.sem[sem], 16), (sem, 16), lat)
+
+    def rows(s):
+        return slice(64 * s, 64 * s + 64)
+    for s in range(2):
+        for a in range(2):
+            n = "%d%d" % (s, a)
+            dma("y", "ld_f" + n, T.FI[rows(a), s, :], T.front[rows(s), rows(a)], [], ["FI" + n], 2.2)
+            dma("s", "ld_v" + n, T.Z[rows(a), s, :], T.vein[rows(s), rows(a)], [], ["Zl" + n], 2.2)
+        if s == 0:
+            dma("s", "ld_wi", T.WI[:, 0:1], T.w[:], [], ["WI0"], 2.2)
+            dma("s", "ld_li", T.WI[:, 1:2], T.lim[:], [], ["WI1"], 2.2)
+        for a in range(2):
+            n = "%d%d" % (s, a)
+            dma("y", "ld_r" + n, T["ROCK%d" % s][rows(a), 0:4096], T.rock[rows(s), :], [], ["ROCK" + n], 5.0 + 3.5 * s)
+
+    S["st"] = "k"
+    G(1, [], ["PI"], ioI(T.PI[:, 0:1], [[1, 1]], 0, 1))
+    G(128, [], ["GR"], ioF(T.GR[:], [[1, 8], [0, 16]], 0, 0))
+    G(128, [], ["CR"], ioF(T.CR[:], [[0, 8], [1, 16]], 0, 0))
     V(64, [], ["ONES"], ms(T.ONES[:], 1.0))
-    G(0.45, ["ONES"], ["IEB"], lambda: g.affine_select(T.IEB[:, 0:158], T.ONES[:, 0:158], [[-1, 158]], A.is_equal, 0.0, 15, 1))
-    G(0.35, [], ["CR"], ioF(T.CR[:], [[0, 8], [1, 16]], 0, 0))
-    G(0.2, [], ["KM0"], ioF(T.KM16[:], [[1, 16]], 0, 0))
+    V(64, [], ["NEG"], ms(T.NEG[:], -1.0))
+    V(128, [], ["ONE32"], ms(T.ONE32[:], 1.0))
+    G(128, ["ONES"], ["IB"], sel(T.IB[:], T.ONES[:], [[-1, 128]], A.is_equal, 0.0, 0, 1))
+    for a in range(2):
+        G(128, ["ONES"], ["SEL%d" % a], sel(T.SEL[:, a, :], T.ONES[:], [[0, 2], [-1, 64]], A.is_equal, 0.0, -64 * a, 1))
+        V(64, ["SEL%d" % a], ["NSEL%d" % a], ts(T.SEL[:, 2 + a, :], T.SEL[:, a, :], -1.0, None, A.mult))
     V(64, ["PI"], ["PIr"], ts(T.PI[:, 1:2], T.PI[:, 0:1], 15, None, A.bitwise_and))
     V(64, ["PI"], ["PIg"], ts(T.PI[:, 2:3], T.PI[:, 0:1], 4, None, A.arith_shift_right))
-    V(64, ["PIr"], ["r"], cp(T.RF[:, 0:1], T.PI[:, 1:2]))
-    V(64, ["PIg"], ["gp"], cp(T.RF[:, 1:2], T.PI[:, 2:3]))
-    r = T.RF[:, 0:1]
-    gp = T.RF[:, 1:2]
-    V(64, ["gp"], ["gp16"], ts(T.RF[:, 2:3], gp, 16.0, None, A.mult))
-    V(128, ["GR", "gp"], ["BLK"], ts(T.BLK[:], T.GR[:], gp, None, A.is_equal))
-    V(64, ["BLK"], ["BLH"], cp(T.BLH[:], T.BLK[:]))
-    V(64, ["WI0"], ["WF0"], ts(T.WF[:, 0:1], T.WI[:, 0:1], 2.0, None, A.mult))
-    V(64, ["WI1"], ["LIM"], ts(T.LIM[:], T.WI[:, 1:2], 0.5, None, A.add))
-    V(64, ["LIM"], ["TOP0"], cp(T.TOP[:, 0:1], T.LIM[:]))
-    V(64, ["BLK", "WF0"], ["W2"], ts(T.W2[:], T.BLK[:], T.WF[:, 0:1], None, A.mult))
-    V(128, ["FI"], ["F00", "F01"], cp(T.F[:, 0:128], T.FI[:]))
-    V(4 * 64, ["r"], ["BB"], *[ts(T.BB[:, m:m + 1], r, 37.0 * 2 ** (4 + m), 613.0 * m * 2 ** (4 + m), A.mult, A.add) for m in range(4)])
-    V(64, ["r"], ["c1"], ts(T.RF[:, 4:5], r, -1.0, 1039.0, A.mult, A.add))
-    V(64, ["r"], ["c2"], ts(T.RF[:, 5:6], r, -1.0, 1054.0, A.mult, A.add))
-    V(64, ["PIr"], ["PIs"], ts(T.PI[:, 3:4], T.PI[:, 1:2], 1.0, None, A.add))
-    V(64, ["PIs"], ["PIt"], ts(T.PI[:, 4:5], T.PI[:, 3:4], 15, None, A.bitwise_and))
-    V(64, ["PIt"], ["rp1"], cp(T.RF[:, 3:4], T.PI[:, 4:5]))
-    V(64, [], ["q25"], ms(T.RF[:, 6:7], 0.25))
-    V(64, [], ["b129"], ms(T.RF[:, 8:9], 129.5))
-    V(64, ["IEB"], ["NI"], ts(T.NI[:], T.IEB[:, 15:143], -1.0, None, A.mult))
-    for n, c in (("R256", 256.0), ("R05", 0.5), ("R1B", 1.0), ("R1H", 1.0), ("R2H", 2.0)):
-        V(143, ["XR", "gp16"], [n], ts(T[n][:, 0:143], T.XR[:, 0:143], T.RF[:, 2:3], c, A.is_equal, A.mult))
-    V(64, [], ["ALLC"], ms(T.ALLC[:], 1.0 / 128))
-    for h in range(2):
-        for m in range(4):
-            G(0.28, ["ONES"], ["K1%d%d" % (h, m)], (lambda h, m: lambda: g.affine_select(T.K1[:, h, 64 * m:64 * m + 64], T.ONES[:, 0:64], [[0, 64]], A.is_gt, 64.0 * m + (23 if m in NEARV[h] else 31), 0, 0))(h, m))
-    V(80, ["IEB"], ["IEH"], cp(T.IEH[:, 0:158], T.IEB[:, 0:158]))
-    V(128, ["IEB"], ["I32"], cp(T.I32[:], T.IEB[:, 15:143]))
-    V(64, ["KM0", "r"], ["KT"], ts(T.KT[:], T.KM16[:], r, None, A.is_equal))
-    V(512, [], ["W1"], ms(T.EX1[:], 1.0))
-    for b in range(2):
-        G(1.05, ["W1"], ["EX%d" % b], (lambda b: lambda: g.affine_select(T.EX[:, 512 * b:512 * b + 512], T.EX1[:], [[-1, 32], [0, 16]], A.is_equal, 0.0, -32 * b, 1))(b))
-    V(64, [], ["NEG"], ms(T.NEG[:], -1.0))
+    V(64, ["PI"], ["PIm"], ts(T.PI[:, 3:4], T.PI[:, 0:1], 4, 3, A.arith_shift_right, A.bitwise_and))
+    V(64, ["PI"], ["PIa"], ts(T.PI[:, 4:5], T.PI[:, 0:1], 6, None, A.arith_shift_right))
+    V(64, ["PIr", "PIg", "PIm", "PIa"], ["r"], cp(T.RF[:, 0:4], T.PI[:, 1:5]))
+    r, gp, mi, ha = T.RF[:, 0:1], T.RF[:, 1:2], T.RF[:, 2:3], T.RF[:, 3:4]
+    V(64, ["GR", "r"], ["BLK"], ts(T.BLK[:], T.GR[:], gp, None, A.is_equal))
+    V(64, ["WI0", "WI1"], ["WL"], cp(T.WL[:], T.WI[:]))
+    PE(128, ["WL", "SEL0", "SEL1"], ["MM"], [(T.MM[:, 2 * s:2 * s + 2], T.SEL[:, s, :], T.WL[:], True, True) for s in range(2)])
+    for s in range(2):
+        V(64, ["MM", "BLK"], ["W2%d" % s], ts(T.W2[:, s, :], T.BLK[:], T.MM[:, 2 * s:2 * s + 1], 2.0, A.mult, A.mult))
+    V(64, ["MM"], ["LIM"], ts(T.LIM[:], T.MM[:, 1:4:2], 0.5, None, A.add))
+    V(64, ["LIM"], ["TOP0"], cp(T.TOP[:, :, 0], T.LIM[:]))
+    for s in range(2):
+        V(64, ["FI%d0" % s, "FI%d1" % s], ["F0%d" % s], ts(T.F[:, s, :], T.FI[:, s, :], -2048.0, None, A.add))
+    pw = [32, 32, 64, 128] if INT else [32, 64, 128, 256]
+    for m in range(4):
+        V(64, ["IB"], ["SCM%d" % m], ts(T.SCM[:, m, :], T.IB[:], float(pw[m]), None, A.mult))
+    V(64, ["IB"], ["NIB"], ts(T.NIB[:], T.IB[:], -1.0, None, A.mult))
+    V(64, [], ["L3z"], ms(T.L3[:], 1.0))
+    V(64, ["L3z", "CR"], ["L3"], cp(T.L3[0:1, :], T.CR[0:1, :]))
+    V(160, [], ["R3z"], ms(T.R3[:], 0.0))
+    fills = []
+    for m in range(4):
+        c = (2048 + 613 * m) * 2 ** (5 + m) - 2 ** 23
+        if INT and m:
+            c -= (2048 + 613 * (m - 1)) * 2 ** (4 + m) - 2 ** 23
+        hi = (c >> 16) << 16
+        lo1 = ((c - hi) >> 8) << 8
+        for row, x in ((0, 37 * pw[m]), (32, hi), (64, lo1), (96, c - hi - lo1)):
+            if x:
+                fills.append(ms(T.R3[row:row + 1, 1 + m:320:5], float(x)))
+    fills.append(ms(T.R3[32:33, 0:320:5], 2048.0))
+    V(64, ["R3z"], ["R3"], *fills)
+    V(64, ["PIr"], ["PIs"], ts(T.PI[:, 5:6], T.PI[:, 1:2], 1.0, None, A.add))
+    V(64, ["PIs"], ["PIt"], ts(T.PI[:, 6:7], T.PI[:, 5:6], 15, None, A.bitwise_and))
+    V(64, ["r"], ["h100"], ts(T.RF[:, 4:5], ha, 100.0, None, A.mult), ts(T.RF[:, 5:6], ha, -100.0, 100.0, A.mult, A.add))
+    V(128, ["PIt", "h100"], ["rp1"], *[ts(T.RF[:, 6 + a:7 + a], T.PI[:, 6:7], T.RF[:, 4 + a:5 + a], None, A.add) for a in range(2)])
+    V(128, ["BLK"], ["WD"], ts(T.WD[:, 0:8], T.BLK[:, 0:128:16], 256.0, None, A.mult), cp(T.WD[:, 8:16], T.BLK[:, 0:128:16]))
+    G(128, [], ["CM"], ioF(T.CM[0:1, 0:4 * NG], [[64, 4], [0, NG]], 23, 0), ioF(T.CM[0:1, 4 * NG:256], [[0, 64 - NG], [64, 4]], 23, 0))
+    G(NG, ["ONE32"], ["PERM"], *([sel(T.PERM[:, m:4 * NG:4], T.ONE32[:, 0:NG], [[-1, NG]], A.is_equal, 0.0, -NG * m, 1) for m in range(4)] +
+                                 ([sel(T.PERM[:, 4 * NG:128], T.ONE32[:, 4 * NG:128], [[-1, 128 - 4 * NG]], A.is_equal, 0.0, -4 * NG, 1)] if NG < 32 else [])))
+    V(128, ["IB"], ["I32"], cp(T.I32[:], T.IB[:]))
+    V(128, ["IB"], ["NI32"], ts(T.NI32[:], T.IB[:], -1.0, None, A.mult))
+    V(64, [], ["RSz"], ms(T.RS[:], 0.0))
+    V(64, ["RSz"], ["RS"], ms(T.RS[:, 0:128:4], float(2 ** 22)))
+    G(144, [], ["XK"], ioF(T.XK[:], [[1, 144]], -15, 0))
+    V(64, ["r"], ["g16"], ts(T.RF[:, 13:14], gp, 16.0, None, A.mult))
+    V(144, ["XK", "g16"], ["RK"], *[ts(T.RK[:, x, :], T.XK[:], T.RF[:, 13:14], (256.0, 1.0)[x], A.is_equal, A.mult) for x in range(2)])
+    if INT:
+        for s in range(2):
+            V(320, [], ["UIa%d" % s], ms(T.UI[:, s, :], 1))
+            V(64, ["UIa%d" % s], ["UI%d" % s], ms(T.UI[:, s, 0:320:5], 0))
+    V(64, ["CR", "r"], ["KT"], ts(T.KT[:], T.CR[:, 0:16], r, None, A.is_equal))
+    V(64, ["KT"], ["NKT"], ts(T.NKT[:], T.KT[:], -1.0, None, A.mult))
+    for l in range(0, 16, 4):
+        V(256, ["BLK", "NKT"], ["EL%d" % l], *[ts(T.EL[:, x, :], T.BLK[:], T.NKT[:, x:x + 1], None, A.mult) for x in range(l, l + 4)])
+    V(64, ["CR", "r"], ["T3"], ts(T.T3[:], T.CR[:], r, -(2.0 ** 40), A.is_gt, A.mult))
+    V(128, ["T3", "BLK"], ["SLB"], tt(T.SLB[:], T.T3[:], T.BLK[:], A.mult))
     for l in range(16):
-        G(0.4, ["NEG"], ["EL%d" % l], (lambda l: lambda: g.affine_select(T.EL[:, 128 * l:128 * l + 128], T.NEG[:], [[-16, 8], [0, 16]], A.is_equal, 0.0, -l, 1))(l))
-        G(0.18, ["q25"], ["P4%d" % l], (lambda l: lambda: g.affine_select(T.P4[:, l:l + 1], T.RF[:, 6:7], [[0, 1]], A.is_gt, 4.0 ** l, 0, 0))(l))
-    V(64, ["P4%d" % l for l in range(16)] + ["KT"], ["P4b"], tt(T.P4[:], T.P4[:], T.KT[:], A.mult))
-    V(64, ["P4b"], ["P4C"], lambda: v.tensor_reduce(T.P4C[:], T.P4[:], AxisListType.X, A.add))
-    V(64, ["BLK", "P4C"], ["Q2"], ts(T.Q2[:], T.BLK[:], T.P4C[:, 0:1], None, A.mult))
-    V(128, ["CR", "r"], ["T32"], ts(T.T32[:], T.CR[:], r, -(2.0 ** 40), A.is_gt, A.mult))
-    V(256, ["T32", "BLK"], ["SLB"], tt(T.SLB[:], T.T32[:], T.BLK[:], A.mult))
-    for l in range(16):
-        G(0.4, ["SLB"], ["PL%d" % l], (lambda l: lambda: g.affine_select(T.PL[:, 128 * l:128 * l + 128], T.SLB[:], [[-1, 128]], A.not_equal, 4.0 ** (15 - l), 0, 1))(l))
-    V(128, ["CR", "r"], ["T32"], ts(T.T32[:], T.CR[:], r, None, A.is_ge))
-    V(256, ["T32", "BLK"], ["UPI"], tt(T.UPI[:], T.T32[:], T.BLK[:], A.mult))
-    V(64, ["ONES", "KT"], ["S15"], ts(T.S15[:], T.ONES[:, 0:128], T.KT[:, 15:16], None, A.mult))
-    G(0.2, [], ["JCI0"], ioI(T.JCI[:, 0:8], [[16, 8]], 0, 0))
-    V(64, ["JCI0", "r"], ["JCI1"], ts(T.JCI[:, 8:16], T.JCI[:, 0:8], r, None, A.add))
-    V(64, ["JCI1"], ["PCH"], cp(T.PCH[:], T.JCI[:, 8:10]))
-    V(64, ["JCI1"], ["DUMP"], ts(T.DUMP[:], T.JCI[:, 8:16], 4096.0, None, A.add))
-    V(128, [], ["HWz0", "HWz1"], ms(T.HW0[:, 0:32], 0.0), ms(T.HW1[:, 0:32], 0.0))
+        G(128, ["SLB"], ["PL%d" % l], sel(T.PL[:, l, :], T.SLB[:], [[-1, 128]], A.not_equal, 4.0 ** (15 - l), 0, 1))
+    V(256, ["CR"], ["T1", "T2"], ts(T.T1[:], T.CR[:], 0.0, 4.0, A.is_gt, A.mult), ts(T.T2[:], T.CR[:], 0.0, 4.0 ** -16, A.is_equal, A.mult))
+    V(128, ["T1", "T2"], ["P4"], scan(T.P4[:], T.T1[:], T.T2[:], 0.0, A.mult, A.add))
+    V(256, ["P4", "BLK"], ["QA"], tt(T.QQ[:, 0, :], T.P4[:], T.BLK[:], A.mult))
+    V(64, ["P4", "KT"], ["T1"], tt(T.T1[:, 0:16], T.P4[:, 0:16], T.KT[:], A.mult))
+    V(64, ["T1"], ["p4c"], lambda: v.tensor_reduce(T.RF[:, 8:9], T.T1[:, 0:16], AxisListType.X, A.add))
+    V(64, ["QA", "p4c"], ["QB"], ts(T.QQ[:, 1, :], T.QQ[:, 0, :], T.RF[:, 8:9], 4.0, A.mult, A.mult))
+    V(64, ["CR", "r"], ["T3"], ts(T.T3[:], T.CR[:], r, None, A.is_ge))
+    V(128, ["T3", "BLK"], ["QC"], tt(T.QQ[:, 2, :], T.T3[:], T.BLK[:], A.mult))
+    V(128, ["KT"], ["KH"], ts(T.KH[:, 0:1], T.KT[:, 15:16], -512.0, None, A.mult), ts(T.KH[:, 1:2], T.KT[:, 15:16], 512.0, -32.0, A.mult, A.add))
+    V(192, ["BLK", "KH"], ["WX"], ts(T.WX[:, 0, :], T.BLK[:], 32.0, None, A.mult), ts(T.WX[:, 1, :], T.BLK[:], T.KH[:, 0:1], None, A.mult),
+      ts(T.WX[:, 2, :], T.BLK[:], T.KH[:, 1:2], None, A.mult))
+    G(32, [], ["T4j"], ioF(T.T4[:, 0:32], [[1, 32]], 0, 0))
+    V(64, ["CR", "r"], ["T3"], ts(T.T3[:, 0:32], T.CR[:, 0:32], r, -2048.0, A.not_equal, A.mult))
+    V(64, ["T3", "T4j"], ["CJ"], tt(T.CJ[:], T.T3[:, 0:32], T.T4[:, 0:32], A.add))
+    V(64, ["CR"], ["R1"], ts(T.R1[:], T.CR[:, 0:32], 0.0, None, A.is_gt))
+    G(128, [], ["TI"], ioI(T.TI[:], [[-1, 128]], 128, 1))
+    V(128, ["TI"], ["TI"], ts(T.TI[:], T.TI[:], 15, None, A.bitwise_and))
+    V(64, ["BLK"], ["T3"], ts(T.T3[:], T.BLK[:], -100.0, 100.0, A.mult, A.add))
+    V(256, ["TI", "T3", "T4j", "CJ"], ["T4"], tt(T.T4[:], T.TI[:], T.T3[:], A.add))
+    for l in range(0, 16, 4):
+        V(256, ["T4"], ["CS%d" % l], *[ts(T.CS[:, x, :], T.T4[:], float((x + 1) % 16), None, A.is_equal) for x in range(l, l + 4)])
+    V(64, ["IB"], ["I32B"], ts(T.I32B[:], T.IB[:], 32.0, None, A.mult))
+    V(64, ["ONES", "KT"], ["S15"], ts(T.S15[:], T.ONES[:], T.KT[:, 15:16], None, A.mult))
+    V(64, [], ["XRz"], ms(T.XR[:], -1.0))
+    G(128, ["XRz"], ["XR"], ioF(T.XR[:, 15:143], [[0, 2], [1, 64]], 0, 0))
+    V(64, ["r"], ["m16"], ts(T.RF[:, 9:10], mi, 16.0, None, A.mult))
+    V(72, ["XR", "m16"], ["RW"], ts(T.RW[:], T.XR[:], T.RF[:, 9:10], None, A.is_equal))
+    V(128, ["r"], ["hh"], ts(T.RF[:, 10:11], ha, -0.5, 0.5, A.mult, A.add), ts(T.RF[:, 11:12], ha, 0.5, None, A.mult))
+    V(192, ["IB", "hh"], ["HB"], ts(T.HB[:, 0, :], T.IB[:], T.RF[:, 10:11], None, A.mult), ts(T.HB[:, 1, :], T.IB[:], T.RF[:, 11:12], None, A.mult),
+      ts(T.HB[:, 2, :], T.IB[:], 0.5, None, A.mult))
+    V(64, [], ["QR"], ms(T.QR[0:1, :], -0.25))
+    V(256, ["r"], ["KM"], *[ts(T.KH[:, 4 + x:5 + x], mi, float(x), None, A.is_equal) for x in range(4)])
+    for x in range(4):
+        V(128, ["ONES", "NEG", "KM"], ["GS%d" % x], ts(T.GS[:, x, :], T.ONES[:], T.KH[:, 4 + x:5 + x], None, A.mult),
+          ts(T.GS[:, 4 + x, :], T.NEG[:], T.KH[:, 4 + x:5 + x], None, A.mult))
+    G(128, [], ["G4"], ioF(T.G4[:], [[0, 2], [1, 4], [0, 16]], 0, 0))
+    V(64, ["CR", "r"], ["T3"], ts(T.T3[:], T.CR[:], r, 100.0, A.not_equal, A.mult))
+    V(128, ["T3", "G4"], ["G4"], tt(T.G4[:], T.G4[:], T.T3[:], A.add))
+    V(256, ["G4"], ["BK"], *[ts(T.BK[:, x, :], T.G4[:], float(x), 8192.0, A.is_equal, A.mult) for x in range(4)])
+    G(8, [], ["DUMPa"], ioF(T.DUMP[:], [[16, 8]], 4096, 0))
+    V(64, ["DUMPa", "r"], ["DUMP"], ts(T.DUMP[:], T.DUMP[:], r, None, A.add))
     for t in range(NV):
         a = t + 1
-        G(0.25, [], ["PRW%d" % t], ioF(T.PRW[:, 64 * t:64 * t + 64], [[1, 2 ** a], [2 ** a, 2 ** (6 - a)]], 0, 0))
-        pc, pt, pf = T.PCI[:, 4 * t:4 * t + 4], T.PTI[:, 4 * t:4 * t + 4], T.PCF[:, 4 * t:4 * t + 4]
-        V(64, ["JCI1"], ["PCI%d" % t], ts(pc, T.JCI[:, 8:12], 2 ** (6 - a) - 1, None, A.bitwise_and))
-        V(64, ["JCI1"], ["PTI%d" % t], ts(pt, T.JCI[:, 8:12], 6 - a, None, A.arith_shift_right))
-        V(64, ["PCI%d" % t], ["PCF%d" % t], ts(pf, pc, float(2 ** a), None, A.mult))
-        V(64, ["PCF%d" % t, "PTI%d" % t], ["PCG%d" % t], tt(pf, pf, pt, A.add))
-        V(256, ["PRW%d" % t, "PCG%d" % t], ["MK%d" % t],
-          *[ts(T.MK[:, 256 * t + 64 * c:256 * t + 64 * c + 64], T.PRW[:, 64 * t:64 * t + 64], T.PCF[:, 4 * t + c:4 * t + c + 1], 8192.0, A.is_ge, A.mult) for c in range(4)])
-    SC(0, ["q25"], ["lnw"], ac(T.RF[:, 7:8], T.RF[:, 6:7], AF.Ln))
+        G(128, [], ["CL%d" % t], ioF(T.CL[0:1, t, :], [[64, 2], [1, 2 ** a], [2 ** a, 2 ** (6 - a)]], 0, 0))
+        PE(256, ["CL%d" % t, "ONES", "NEG"], ["EQ"], [(T.EQ[:, 0:128], T.ONES[0:1, :], T.CL[0:1, t, :], True, False),
+                                                      (T.EQ[:, 0:128], T.CL[0:1, t, :], T.NEG[0:1, :], False, True)])
+        V(128, ["EQ"], ["MK%d" % t], ts(T.MK[:, t, :], T.EQ[:, 0:128], 0.0, 8192.0, A.is_ge, A.mult))
+    V(64, [], ["b128"], ms(T.RF[:, 12:13], 129.0))
+    S["st"] = ""
 
-    MM, EQ = T.MM, T.EQ
-    IH = T.IEH[:, 15:143]
-    PLK = ["PL%d" % l for l in range(16)]
+    MM, EQ, KX, HT = T.MM, T.EQ, T.KX, T.HT
+    IB = T.IB[:]
 
-    def claims(t, h):
-        k, H, xk = "%d%d" % (t, h), str(h), "X%d" % h
-        o = (2 * t + h) * 64
-        F, Z, X = T.F[:, o:o + 64], T.Z[:, o:o + 64], T[xk]
-        CO, ZX = T["CO" + H], T["ZX" + H]
-        nX = X[:, 384:448]
-        SC(5 * 64, ["F" + k, "BB"], [xk], ac(nX, F, AF.Copy),
-           *[ac(X[:, 128 + 64 * m:192 + 64 * m], F, AF.Identity, bias=T.BB[:, m:m + 1], scale=float(2 ** (4 + m))) for m in range(4)])
-        PE(128, ["Z" + k, "W2", "BLK"], [xk], [(X[:, 0:64], T.W2[:], Z, True, True), (X[:, 64:128], T.BLK[:], Z, True, True)])
-        hh, u1 = T.UA[:, h, 0:64], T.UI[:, h, :]
-        V(128, [xk], ["UA" + H], ts(T.UA[:, h, :], X[:, 0:128], 1.0, None, A.add))
-        V(64, ["UA" + H], ["UI" + H], ts(u1, hh, 4095, None, A.bitwise_and))
-        V(64, [xk, "UI" + H], ["QI" + H], tt(T.QI[:, h, :], nX, u1, A.mult))
-        V(64, ["QI" + H], ["UAh" + H], ts(hh, T.QI[:, h, :], 1, None, A.arith_shift_right))
-        V(256, [xk, "UAh" + H], ["HM" + H], *[tt(T.HM[:, h, 64 * m:64 * m + 64], X[:, 128 + 64 * m:192 + 64 * m], hh, A.add) for m in range(4)])
-        V(256, ["HM" + H], ["C4" + H], *[ts(T.C4[:, h, 64 * m:64 * m + 64], T.HM[:, h, 64 * m:64 * m + 64], 4 + m, 4095, A.arith_shift_right, A.bitwise_and) for m in range(4)])
-        V(256, ["C4" + H], ["CO" + H], cp(CO[:], T.C4[:, h, :]))
-        if ZXP[h]:
-            PE(128, ["Z" + k, "IEB"], ["HA"], [(T.HA[0:64, 0:128], Z, T.IEB[:, 15:143], True, True)])
-            SC(128, ["HA"], ["ZT" + H], ac(T.ZT[0:64, h, :], T.HA[0:64, 0:128], AF.Copy))
-            for b, bk in ((0, "HB"), (1, "HA")):
-                PE(512, ["ZT" + H, "EX0", "EX1"], [bk], [(T[bk][:], T.ZT[0:64, h, :], T.EX[0:64, 512 * b:512 * b + 512], True, True)])
-                SC(512, [bk], ["ZX%s%d" % (H, 8 * b), "ZX%s%d" % (H, 8 * b + 4)], ac(ZX[:, 512 * b:512 * b + 512], T[bk][:], AF.Copy))
+    def zk(t, s):
+        return ["Zl%d0" % s, "Zl%d1" % s] if t == 0 else ["Z%d%d" % (t, s)]
+
+    def rk(s):
+        return ["ROCK%d0" % s, "ROCK%d1" % s]
+
+    def follow(q, i):
+        if q in S["last"]:
+            S["ops"][i]["deps"].setdefault(S["last"][q], False)
+        S["last"][q] = i
+
+    def claims(t, s):
+        k, H, xk = "%d%d" % (t, s), str(s), "X%d" % s
+        o = 2 * t + s
+        X, CO, ZX = T[xk], T["CO" + H], T["ZX" + H]
+        nX = X[:, 128:448:5]
+        mm = [(X[:, 128:448], T.L3[0:97, :], T.R3[0:97, :], True, False)]
+        for m in range(5):
+            for b in range(2):
+                mm.append((X[:, 128 + 160 * b + m:288 + 160 * b:5], T.SCM[:, m - 1, :] if m else IB, T.F[:, o, b:64:2], False, m == 4 and b == 1))
+        PE(320 + 640, ["F" + k, "L3", "R3", "IB"] + ["SCM%d" % m for m in range(4)], [xk], mm)
+        for x in range(2):
+            PE(128, zk(t, s) + ["W2" + H, "BLK"], [xk], [(X[:, 64 * x + 32 * b:64 * x + 32 * b + 32], (T.W2[:, s, :], T.BLK[:])[x], T.Z[:, o, b:64:2], True, True)
+                                                        for b in range(2)])
+        u1 = T.UI[:, s, 1:320:5]
+        V(128, [xk], ["UA" + H], ts(T.UA[:, s, :], X[:, 0:128], 1.0, None, A.add))
+        V(64, ["UA" + H], ["UI" + H], ts(u1, T.UA[:, s, 0:64], 4095, None, A.bitwise_and))
+        if INT:
+            V(320, [xk, "UI" + H], ["HM%s%d" % (H, m) for m in range(4)], scan(T.HM[:, s, :], T.UI[:, s, :], X[:, 128:448], 0.0, A.mult, A.add))
         else:
-            for b in range(0, 16, 4):
-                if b < ZXV[h]:
-                    V(256, ["Z" + k], ["ZX%s%d" % (H, b)], *[cp(ZX[:, p:1024:16], Z) for p in range(b, b + 4)])
-                else:
-                    SC(256, ["Z" + k], ["ZX%s%d" % (H, b)], *[ac(ZX[:, p:1024:16], Z, AF.Copy) for p in range(b, b + 4)])
-        V(64, ["UA" + H], ["SI" + H], ts(T.SI[:, h, :], T.UA[:, h, 64:128], 15, None, A.bitwise_and))
-        V(256, [xk, "C4" + H], ["DN" + H], *[tt(T.DN[:, h, 64 * m:64 * m + 64], T.C4[:, h, 64 * m:64 * m + 64], nX, A.subtract) for m in range(4)])
-        V(64, ["UI" + H], ["UF" + H], ts(T.UF[:, h, :], T.UI[:, h, 1:64:2], -1.0, 0.5, A.add, A.mult))
-        V(128, ["SI" + H, "rp1"], ["SM" + H], *[ts(T.SM[:, h, 32 * b:32 * b + 32], T.SI[:, h, b:64:2], T.RF[:, 3:4], None, A.is_equal) for b in range(2)])
-        zb = T.ZB[:, h, :]
-        SC(64, ["Z" + k], ["ZB" + H], *[ac(T.ZB[:, h, 32 * b:32 * b + 32], T.Z[:, o + b:o + 64:2], AF.Copy) for b in range(2)])
-        SC(64, ["ZB" + H], ["Z5" + H], ac(T.Z5[:, h, :], zb, AF.Copy, bias=-0.5))
-        SC(64, ["ZB" + H], ["Z4" + H], ac(T.Z4[:, h, :], zb, AF.Copy, scale=0.25, bias=129 - 0.375))
-        PE(128, ["ZB" + H, "Z4" + H, "IEB"], [xk], [(X[:, 0:64], T.IEB[:, 15:143], T.Z4[:, h, :], True, False), (X[:, 0:64], T.IEB[:, 15:143], zb, False, True)])
-        PE(256, ["F" + k, "I32"], [xk], [(X[:, 448:512], T.I32[:], F, True, False)])
-
-    def moves(t, h):
-        k, H = "%d%d" % (t, h), str(h)
-        kk = BANKS[2 + h]
-        KK = T[kk]
-        CO, ZX = T["CO" + H], T["ZX" + H]
-        o = (2 * t + h) * 64
+            V(64, [xk, "UI" + H], ["QI" + H], tt(T.QI[:, s, :], nX, u1, A.mult))
+            for m in range(4):
+                V(64, [xk, "QI" + H], ["HM%s%d" % (H, m)], tt(T.HM[:, s, 1 + m:320:5], X[:, 129 + m:448:5], T.QI[:, s, :], A.add))
         for m in range(4):
-            d, n = "D%d%d" % (h, m), "N%d%d" % (h, m)
-            dm, nm = T.D[:, h, 1024 * m:1024 * m + 1024], T.NR[:, h, 1024 * m:1024 * m + 1024]
-            zk = ["ZX%s%d" % (H, b) for b in range(0, 16, 4)]
-            win = T.ROCK[:, 0:4096].indirect(CO[:, 64 * m:64 * m + 64])
-            if m in SG:
-                xg = T["XG" + H]
-                SC(1536, RK + ["CO" + H], ["XG" + H], ac(xg[:], win, AF.Copy))
-                for b, bk in ((0, "HA"), (1, "HB")):
-                    PE(1024, ["XG" + H, "IEB", "NI"] + zk, [bk], [(T[bk][:], T.IEB[:, 15:143], xg[:, 512 * b:512 * b + 512], True, False),
-                                                                (T[bk][:], T.NI[:], ZX[:, 512 * b:512 * b + 512], False, True)])
-                    SC(512, [bk], [d + "ab"[b]], ac(T.D[:, h, 1024 * m + 512 * b:1024 * m + 512 * b + 512], T[bk][:], AF.Abs))
+            V(64, ["HM%s%d" % (H, m)], ["C4%s%d" % (H, m)], ts(T.C4[:, s, m:256:4], T.HM[:, s, 1 + m:320:5], 5 + m, 4095, A.arith_shift_right, A.bitwise_and))
+        V(256 - 4 * NG, ["C4%s%d" % (H, m) for m in range(4)], ["COs" + H], cp(CO[:, 4 * NG:256], T.C4[:, s, 4 * NG:256]))
+        for m in range(4):
+            V(64, ["C4%s%d" % (H, m)], ["COv%s%d" % (H, m)], cp(CO[:, NG * m:NG * m + NG], T.C4[:, s, m:4 * NG:4]))
+        for p in range(16):
+            if p < ZV:
+                V(64, zk(t, s), ["ZX%s%d" % (H, p)], cp(ZX[:, p:16 * NG:16], T.Z[:, o, 0:2 * NG:2]))
             else:
-                V(60 + 1536, RK + ["CO" + H] + zk, [d + "a", d + "b"], tt(dm, win, ZX[:], A.subtract))
-                SC(1024, [d + "a", d + "b"], [d + "a", d + "b"], ac(dm, dm, AF.Abs))
-            if m in NEARV[h]:
-                V(512, [d + "a", d + "b", "TOP%d" % t], [n + "a", n + "b"], ts(nm, dm, T.TOP[:, t:t + 1], None, A.is_le))
-            else:
-                SC(1024, [d + "a", d + "b", "TOP%d" % t], [n + "a", n + "b"], ac(nm, dm, AF.Sign, bias=T.TOP[:, t:t + 1], scale=-1.0))
+                G(NG, zk(t, s), ["ZX%s%d" % (H, p)], sel(ZX[:, p:16 * NG:16], T.Z[:, o, 0:2 * NG:2], [[0, NG]], A.is_ge, 0.0, 0, 0))
+        V(64, ["UA" + H], ["SI" + H], ts(T.SI[:, s, :], T.UA[:, s, 64:128], 15, None, A.bitwise_and))
+        V(64, ["UI" + H], ["UF" + H], ts(T.UF[:, s, :], T.UI[:, s, 161:320:5], 16.0, 65536.0 - 16 - 2 ** 18, A.mult, A.add))
+        V(128, ["SI" + H, "rp1"], [xk, "SM" + H], *[ts(X[:, 64 * a:64 * a + 64], T.SI[:, s, :], T.RF[:, 6 + a:7 + a], None, A.is_equal) for a in range(2)])
+        V(64, zk(t, s), ["Z4" + H], ts(T.Z4[:, s, :], T.Z[:, o, :], 0.25, 129 - 0.375, A.mult, A.add))
 
-        def keys(m, near):
-            w, src, b = (("R1B" if m in NEARV[h] else "R05"), T.NR, "N") if near else ("R256", T.D, "D")
-            PE(1024, ["%s%d%d%s" % (b, h, m, x) for x in "ab"] + [w], [kk], [(KK[:, 64 * m:64 * m + 64], T[w][:, 15 - p:143 - p], src[:, h, 1024 * m + p:1024 * m + 1024:16], False, near and m % 2 == 1 and p == 15) for p in range(16)])
-        for b in (0, 1):
-            PE(128, ["ALLC"] + ["K1%d%d" % (h, m) for m in range(4)], [kk], [(KK[:, 128 * b:128 * b + 128], T.ALLC[:], T.K1[:, h, 128 * b:128 * b + 128], True, False)])
-            for m, near in ((0, 0), (1, 0), (0, 1), (1, 1)):
-                keys(2 * b + m, bool(near))
-            if b == 0:
-                SC(128, [kk], ["KS" + H], ac(T.KS[:, h, :], KK[:, 0:128], AF.Copy))
-        V(128, [kk, "KS" + H], ["KM" + H], tt(T.KM[:, h, :], KK[:, 128:256], T.KS[:, h, :], A.min))
-        V(128, ["KM" + H], ["KB" + H], tt(T.KB[:, h, :], T.KM[:, h, 0:64], T.KM[:, h, 64:128], A.min))
-        V(64, ["KB" + H], ["KC" + H], ts(T.KC[:, h, :], T.KB[:, h, :], 255, 5, A.bitwise_and, A.arith_shift_right))
-        V(256, ["KC" + H], [kk], *[ts(KK[:, 256 + 64 * m:320 + 64 * m], T.KC[:, h, :], float(2 * m + 1), None, A.is_equal) for m in range(4)])
-        V(256, [kk, "DN" + H], ["PR" + H], tt(T.PR[:, h, :], KK[:, 256:512], T.DN[:, h, :], A.mult))
-        X = T["X" + H]
-        PE(4 * 256, ["PR" + H, "I32"], ["X" + H], [(X[:, 448:512], T.I32[:], T.PR[:, h, 64 * m:64 * m + 64], False, m == 3) for m in range(4)])
+    def moves(t, s):
+        H = str(s)
+        o = 2 * t + s
+        CO, ZX, RO = T["CO" + H], T["ZX" + H], T["ROCK" + H]
+        nv = 64 * NG
+        run = []
+        for c0 in list(range(NG, 32, SGRP)) + list(range(32, 64, SGRP)):
+            calls = []
+            run.append(len(S["ops"]))
+            for c in range(c0, c0 + SGRP):
+                z = 2 * c if c < 32 else 2 * (c - 32) + 1
+                calls.append(ac(T.D[:, s, 64 * c:64 * c + 64], RO[:, 0:4096].indirect(CO[:, 4 * c:4 * c + 4]), AF.Abs, bias=T.Z[:, o, z:z + 1], scale=-1.0))
+            SC(SGRP * (64 * GAT + 5), rk(s) + zk(t, s) + ["COs" + H], ["D%s_%d" % (H, c) for c in range(c0, c0 + SGRP)], *calls)
+        for m in range(4):
+            dm = T.D[:, s, 16 * NG * m:16 * NG * (m + 1)]
+            n = NG // VP
+            before = list(S["r"].get("E%s_%d" % (H, m), []))
+            for x in range(VP):
+                e0 = 16 * (NG * m + n * x)
+                V(57 + GAT * 16 * n, rk(s) + ["COv%s%d" % (H, m), "E%s_%d" % (H, m)] + ["ZX%s%d" % (H, b) for b in range(16)], ["G%s_%d_%d" % (H, m, x)],
+                  tt(T.D[:, s, e0:e0 + 16 * n], RO[:, 0:4096].indirect(CO[:, NG * m + n * x:NG * m + n * x + n]), ZX[:, 16 * n * x:16 * n * (x + 1)], A.subtract))
+                for j in before:
+                    S["ops"][-1]["deps"][j] = True
+                follow("v", len(S["ops"]) - 1)
+            run.insert(ABS[m] + m, SC(16 * NG, ["G%s_%d_%d" % (H, m, x) for x in range(VP)], ["E%s_%d" % (H, m)], ac(dm, dm, AF.Abs)))
+        for i in run:
+            follow("s", i)
 
-    def meetings(t, h):
-        k, H = "%d%d" % (t, h), str(h)
-        o = (2 * t + h) * 64
-        kk, xk = BANKS[2 + h], "X" + H
-        KK, NP = T[kk], T[xk][:, 448:512]
-        HW, LS, FO = T["HW" + H], T["LS" + H], T.FO
-        SS, JJ = T.NS[:, h, 0:64:2], T.NS[:, h, 1:64:2]
-        V(64, [xk], ["HF" + H], ts(T.HF[:, h, :], NP, 0.125, 1025 - 0.4375, A.mult, A.add))
-        V(64, [xk], ["JC" + H], ts(T.JC[:, h, 0:32], T[xk][:, 449:512:2], -2048.0, None, A.add))
-        V(64, [xk], ["JS" + H], ts(T.JC[:, h, 32:64], T[xk][:, 448:512:2], -1.0, 2048.0, A.mult, A.add))
-        SC(64, [xk], ["NS" + H], ac(T.NS[:, h, :], NP, AF.Copy))
-        SC(64, ["NS" + H], ["S2" + H], ac(T.S2[:, h, :], T.NS[:, h, :], AF.Copy, bias=-2048.0))
-        for b, bk in ((0, "EQ"), (1, "MM")):
+        def parts(a, b):
+            return (["E%s_%d" % (H, m) for m in range(4) if 16 * NG * m < b and 16 * NG * (m + 1) > a] +
+                    ["D%s_%d" % (H, c) for c in range(NG, 64) if 64 * c < b and 64 * c + 64 > a])
+        cuts = {0: [16 * NG * m for m in range(5)] + ([2048] if NG < 32 else []), 1: list(range(2048, 4097, NPC))}
+        for ch in (0, 1):
+            for a, b in zip(cuts[ch][:-1], cuts[ch][1:]):
+                V((b - a) // 2, parts(a, b) + ["TOP%d" % t], ["N%s_%d" % (H, a)], ts(T.NR[:, s, a:b], T.D[:, s, a:b], T.TOP[:, s, t:t + 1], None, A.is_le))
+        K0, K1 = T.K0, T.K1
+        for p0 in range(0, 16, 4):
+            PE(256 + 128 * (p0 == 0), parts(0, 2048) + ["WD", "CM", "ONES"], ["K0"], [(K0[:, 0:128], T.CM[0:1, 0:128], T.ONES[0:1, :], True, False)][:p0 == 0] +
+               [(K0[:, p:128:16], T.D[:, s, p:2048:16], T.WD[:, 0:8], False, False) for p in range(p0, p0 + 4)])
+        for p0 in range(0, 16, 4):
+            PE(256, ["N%s_%d" % (H, a) for a in cuts[0][:-1]] + ["WD"], ["K0"],
+               [(K0[:, p:128:16], T.NR[:, s, p:2048:16], T.WD[:, 8:16], False, p == 15) for p in range(p0, p0 + 4)])
+        ke = T.KE[:, s, 0:128]
+        if OPT["ke"] == "s":
+            SC(128, ["K0"], ["KE" + H], ac(ke, K0[:, 0:128], AF.Copy))
+        else:
+            V(128, ["K0"], ["KE" + H], cp(ke, K0[:, 0:128]))
+        PE(512, ["KE" + H, "PERM"], ["KX"], [(KX[:, 0:128], ke, T.PERM[:], True, True)])
+        V(128, ["KX", "RS"], ["KS%s0" % H], scan(T.KS[:, s, 0:128], T.RS[:], KX[:, 0:128], 0.0, A.add, A.min))
+        for x in range(2):
+            a0, kk = 2048 + 1024 * x, K1[:, 64 * x:64 * x + 64]
+            for p0 in range(0, 16, 4):
+                first = x == 0 and p0 == 0
+                PE(256 + 128 * first, parts(a0, a0 + 1024) + ["RK", "CM", "ONES"], ["K1"], [(K1[:, 0:128], T.ONES[0:1, :], T.CM[0:1, 128:256], True, False)][:first] +
+                   [(kk, T.RK[:, 0, 15 - p:143 - p], T.D[:, s, a0 + p:a0 + 1024:16], False, False) for p in range(p0, p0 + 4)])
+            for p0 in range(0, 16, 4):
+                PE(256, ["N%s_%d" % (H, a) for a in cuts[1][:-1] if a0 <= a < a0 + 1024] + ["RK"], ["K1"],
+                   [(kk, T.RK[:, 1, 15 - p:143 - p], T.NR[:, s, a0 + p:a0 + 1024:16], False, x == 1 and p == 15) for p in range(p0, p0 + 4)])
+        V(128, ["K1", "RS"], ["KS%s1" % H], scan(T.KS[:, s, 128:256], T.RS[:], K1[:, 0:128], 0.0, A.add, A.min))
+
+    def choice(t, s):
+        k, H, xk = "%d%d" % (t, s), str(s), "X%d" % s
+        o = 2 * t + s
+        X = T[xk]
+        if INT:
+            kb, kn = T.KS[:, s, 3:256:4], ["KS%s0" % H, "KS%s1" % H]
+        else:
+            kb, kn = T.KB[:, s, :], ["KB" + H]
+            V(64, ["KS%s0" % H, "KS%s1" % H], kn, cp(kb, T.KS[:, s, 3:256:4]))
+        V(64, kn, ["KC" + H], ts(T.KC[:, s, :], kb, 255, 5, A.bitwise_and, A.arith_shift_right))
+        V(64, kn, ["NB" + H], ts(T.NB[:, s, :], kb, 5, 1, A.arith_shift_right, A.bitwise_and))
+        V(64, ["NB" + H, xk], ["PRn" + H], tt(T.PR[:, s, 256:320], X[:, 128:448:5], T.NB[:, s, :], A.mult))
+        NP = X[:, 448:512]
+        PE(256 + 128, ["PRn" + H, "NI32", "F" + k, "IB"], [xk], [(NP, T.NI32[:], T.PR[:, s, 256:320], True, False)] +
+           [(X[:, 448 + 32 * b:480 + 32 * b], IB, T.F[:, o, b:64:2], False, False) for b in range(2)])
+        for m in range(4):
+            V(64, ["KC" + H], ["KX", "KM%d" % m], ts(KX[:, 256 + 64 * m:320 + 64 * m], T.KC[:, s, :], float(2 * m + 1), None, A.is_equal))
+        for m in range(4):
+            V(64, ["KX", "KM%d" % m, "C4%s%d" % (H, m)], ["PR%s%d" % (H, m)],
+              tt(T.PR[:, s, 64 * m:64 * m + 64], KX[:, 256 + 64 * m:320 + 64 * m], T.C4[:, s, m:256:4], A.mult))
+            PE(256, ["PR%s%d" % (H, m), "I32"], [xk], [(NP, T.I32[:], T.PR[:, s, 64 * m:64 * m + 64], False, m == 3)])
+
+    def meetings(t, s):
+        k, H, xk = "%d%d" % (t, s), str(s), "X%d" % s
+        o = 2 * t + s
+        X = T[xk]
+        NP = X[:, 448:512]
+        HW, LS = T["HW" + H], T["LS" + H]
+        SS, JJ = T.NS[:, s, 0:32], T.NS[:, s, 32:64]
+        V(64, [xk], ["HF" + H], ts(T.HF[:, s, :], NP, 0.125, 1281 - 0.4375, A.mult, A.add))
+        V(64, [xk], ["JC" + H], cp(T.JC[:, s, :], NP))
+        SC(64, [xk], ["NS" + H], ac(T.NS[:, s, :], NP, AF.Copy, bias=2048.0))
+        for b, bk in ((0, "EQ"), (1, "KX")):
             mm = []
             for l in range(8):
                 dd = T[bk][:, 32 * l:32 * l + 32]
-                mm.append((dd, IH, T.HF[:, h, 1:64:2], True, False))
-                mm.append((dd, T.EL[:, 128 * (8 * b + l):128 * (8 * b + l) + 128], T.HF[:, h, 0:64:2], False, True))
-            PE(16 * 64, ["HF" + H, "IEH"] + ["EL%d" % l for l in range(16)], [bk], mm)
-            V(256, [bk], ["EQB%s%d" % (H, b)], ts(T.EQB[:, h, 256 * b:256 * b + 256], T[bk][:, 0:256], 0.0, None, A.is_equal))
-            PE(512, ["EQB%s%d" % (H, b)] + PLK, [kk], [(KK[:, 256:288], T.PL[:, 128 * l:128 * l + 128], T.EQB[:, h, 32 * l:32 * l + 32], l == 0, l == 15) for l in range(8 * b, 8 * b + 8)])
-        pm = T.PM[:, h, :]
-        for bk, s0, s1 in [("HA" if x < 16 else "HB", max(x, 1), x + 4) for x in range(0, 32, 4)]:
+                mm.append((dd, IB, T.HF[:, s, 32:64], True, False))
+                mm.append((dd, T.EL[:, 8 * b + l, :], T.HF[:, s, 0:32], False, True))
+            PE(16 * 64, ["HF" + H, "IB", "EL%d" % (8 * b), "EL%d" % (8 * b + 4)], [bk], mm)
+            V(256, [bk], ["EQB%s%d" % (H, b)], ts(T.EQB[:, s, 256 * b:256 * b + 256], T[bk][:, 0:256], 0.0, None, A.is_equal))
+        for b in range(2):
+            PE(512, ["EQB%s%d" % (H, b)] + ["PL%d" % l for l in range(8 * b, 8 * b + 8)], ["MM"],
+               [(MM[:, 0:32], T.PL[:, l, :], T.EQB[:, s, 32 * l:32 * l + 32], l == 0, l == 15) for l in range(8 * b, 8 * b + 8)])
+        for x in range(0, 16, 2):
             mm = []
-            for s in range(s0, s1):
-                dd = T[bk][:, 32 * (s % 16):32 * (s % 16) + 32]
-                mm += [(dd, T.IEH[:, s - 1:s + 127], T.JC[:, h, 0:32], True, False), (dd, IH, T.JC[:, h, 32:64], False, True)]
-            PE(64 * len(mm), ["JC" + H, "JS" + H, "IEH"], [bk], mm)
-        V(64, [kk], ["PM" + H], ts(pm, KK[:, 256:288], 0.0, None, A.max))
-        PE(192, ["PM" + H, "Q2", "BLK", "UPI"], [kk], [(KK[:, 288:320], T.Q2[:], pm, True, True), (KK[:, 320:352], T.BLK[:], pm, True, True),
-                                                       (KK[:, 352:384], T.UPI[:], pm, True, True)])
-        SC(64, [kk, "lnw"], ["LN" + H], ac(T.LN[:, h, :], KK[:, 288:352], AF.Ln, bias=T.RF[:, 6:7]))
-        SC(480, ["HA"], ["HWa" + H], ac(HW[:, 32:512], T.HA[:, 32:512], AF.Copy))
-        SC(512, ["HB"], ["HWb" + H], ac(HW[:, 512:1024], T.HB[:, 0:512], AF.Copy))
-        V(64, ["LN" + H], ["XX" + H], ts(T.XX[:, h, :], T.LN[:, h, :], 1.0 / math.log(4.0), 1024.0, A.mult, A.add))
-        V(64, [kk], ["JM" + H], ts(T.JM[:, h, :], KK[:, 352:384], 0.0, None, A.is_gt))
-        PE(17 * 64, ["XX" + H, "R2H", "PCH", "IEH"], [kk], [(KK[:, 128:130], IH, T.PCH[:], True, False)] +
-           [(KK[:, 128:130], T.R2H[:, 15 - p:143 - p], T.XX[:, h, p:32:16], False, p == 15) for p in range(16)])
-        ji, ju, dj = T.JI[:, h, :], T.JU[:, h, :], T.DJ[:, h, :]
-        V(64, ["NS" + H], ["JI" + H], tt(ji, JJ, SS, A.mult))
-        V(64, ["NS" + H, "UF" + H], ["JU" + H], tt(ju, JJ, T.UF[:, h, :], A.add))
-        V(64, ["JI" + H], ["JI" + H], ts(ji, ji, 5, None, A.arith_shift_right))
-        V(64, ["JI" + H, "JU" + H], ["JU" + H], tt(ju, ji, ju, A.add))
-        V(64, ["JU" + H], ["JU" + H], ts(ju, ju, 4095, None, A.bitwise_and))
-        V(64, ["JU" + H, "NS" + H], ["DJ" + H], tt(dj, ju, JJ, A.subtract))
-        V(64, ["DJ" + H, "JM" + H], ["DJ" + H], tt(dj, dj, T.JM[:, h, :], A.mult))
-        V(64, ["DJ" + H, "S2" + H], ["FCj" + H], tt(T.FC[:, h, 32:64], dj, T.S2[:, h, 1:64:2], A.add))
-        SC(32, ["FCj" + H], ["FOj" + k], ac(FO[:, o + 32:o + 64], T.FC[:, h, 32:64], AF.Copy, bias=2048.0))
-        jg = T.JG[:, h, :]
-        V(64, ["XX" + H, "c1"], ["CDa" + H], ts(T.CD[:, h, 0:32], T.XX[:, h, 32:64], T.RF[:, 4:5], None, A.is_gt))
-        V(64, ["XX" + H, "c2"], ["CDb" + H], ts(T.CD[:, h, 32:64], T.XX[:, h, 0:32], T.RF[:, 5:6], None, A.is_le))
-        V(64, ["CDa" + H, "CDb" + H], ["CD" + H], tt(T.CD[:, h, 64:96], T.CD[:, h, 0:32], T.CD[:, h, 32:64], A.mult))
-        V(64, [kk], ["LS" + H], ts(LS[:], KK[:, 128:130], -32.0 * 1023, None, A.add))
-        V(110, ["LS" + H, "CD" + H, "HWz" + H, "HWa" + H, "HWb" + H], ["JG" + H], tt(jg, HW[:].indirect(LS[:]), T.CD[:, h, 64:96], A.mult))
-        V(64, ["JG" + H, "S2" + H], ["FCs" + H], tt(T.FC[:, h, 0:32], jg, T.S2[:, h, 0:64:2], A.add))
-        SC(32, ["FCs" + H], ["FOs" + k], ac(FO[:, o:o + 32], T.FC[:, h, 0:32], AF.Copy, bias=2048.0))
+            for i in (x, x + 1):
+                mm += [(HT[:, 32 * i:32 * i + 32], T.CS[:, i, :], T.JC[:, s, 32:64], True, False), (HT[:, 32 * i:32 * i + 32], T.NIB[:], T.JC[:, s, 0:32], False, True)]
+            PE(256, ["JC" + H, "CS%d" % (x // 4 * 4), "NIB"], ["HT"], mm)
+        SC(512, ["HT"], ["HW" + H], ac(HW[:], HT[:], AF.Copy))
+        PE(256 + 64, ["JC" + H, "UF" + H, "I32", "I32B"], [xk], [(X[:, 128:160], T.I32[:], T.UF[:, s, :], True, False), (X[:, 128:160], T.I32B[:], T.JC[:, s, 32:64], False, True)])
+        pm = T.PM[:, s, :]
+        V(64, ["MM"], ["PM" + H], ts(pm, MM[:, 0:32], 0.0, None, A.max))
+        PE(192, ["PM" + H, "QA", "QB", "QC"], ["MM"], [(MM[:, 32 + 32 * x:64 + 32 * x], T.QQ[:, x, :], pm, True, True) for x in range(3)])
+        V(96, ["MM"], ["MS" + H], ts(T.MS[:, s, 0:96], MM[:, 32:128], 0.5, None, A.is_ge))
+        PE(256, ["MS" + H, "WX", "CJ", "IB"], ["MM"], [(MM[:, 128:160], IB, T.CJ[:], True, False)] +
+           [(MM[:, 128:160], T.WX[:, x, :], T.MS[:, s, 32 * x:32 * x + 32], False, x == 2) for x in range(3)])
+        V(64, ["MM", "R1"], ["SX" + H], scan(T.SX[:, s, :], T.R1[:], MM[:, 128:160], 0.0, A.mult, A.max))
+        V(64, ["SX" + H], ["LS" + H], cp(LS[:], T.SX[:, s, 15:32:16]))
+        V(64, ["MS" + H], ["CD" + H], tt(T.MS[:, s, 96:128], T.MS[:, s, 0:32], T.MS[:, s, 32:64], A.subtract))
+        V(57 + 32 * GAT, ["LS" + H, "HW" + H, "CD" + H], ["DMs" + H], tt(T.DM[:, s, 0:32], HW[:].indirect(LS[:]), T.MS[:, s, 96:128], A.mult))
+        V(64, ["NS" + H], ["JI" + H], tt(T.JI[:, s, :], JJ, SS, A.mult))
+        V(64, ["JI" + H, xk], ["JU" + H], tt(T.JU[:, s, :], X[:, 128:160], T.JI[:, s, :], A.add))
+        V(64, ["JU" + H], ["JX" + H], ts(T.JX[:, s, :], T.JU[:, s, :], 5, 4095, A.arith_shift_right, A.bitwise_and))
+        V(64, ["JX" + H, "NS" + H], ["DFj" + H], tt(T.DF[:, s, 32:64], T.JX[:, s, :], JJ, A.subtract))
+        V(64, ["DFj" + H, "MS" + H], ["DMj" + H], tt(T.DM[:, s, 32:64], T.DF[:, s, 32:64], T.MS[:, s, 64:96], A.mult))
+        V(64, ["DMs" + H, "DMj" + H, xk], ["FO" + k], tt(T.FO[:, o, :], NP, T.DM[:, s, :], A.add))
 
-    def send(kind, t, h, R):
-        if t == NV - 1:
-            return
+    def send(kind, t, s, R):
         dst = T.cores[(rank + 3) % 8]
         rid, pid, _ = topo.addr(dst)
         n, mask = len(topo.engines(core, dst)), topo.mask(core, dst)
-        o = (2 * t + h) * 64
+        o = 2 * t + s
         src, out = (T.FO, T.F) if kind == "f" else (T.ZO, T.Z)
-        sem = "ar%s%d%d" % (kind, t + 1, h)
-        add(S, "g", 0.1, R, [("F" if kind == "f" else "Z") + "%d%d" % (t + 1, h)],
-            lambda: g.remote_dma(out[:, o + 128:o + 192], src[:, o:o + 64], T.sem[sem], T.sem.sl, pid, rid, mask), (sem, n), 2.2)
+        sem = "ar%s%d%d" % (kind, t + 1, s)
+        add(S, "g", 0.1, R, [("F" if kind == "f" else "Z") + "%d%d" % (t + 1, s)],
+            lambda: g.remote_dma(out[:, o + 2, :], src[:, o, :], T.sem[sem], T.sem.sl, pid, rid, mask), (sem, n), DML)
         S["sends"] += n
 
-    def mining(t, h):
-        k, H = "%d%d" % (t, h), str(h)
-        o = (2 * t + h) * 64
-        MF, E16 = T.MF, T["E16" + H]
-        ef = T.EF[:, h, 0:4]
-        send("f", t, h, ["FOj" + k, "FOs" + k])
-        V(128, ["FCj" + H, "FCs" + H, "SM" + H], ["MF" + H], tt(MF[:, 64 * h:64 * h + 64], T.FC[:, h, :], T.SM[:, h, :], A.mult))
-        kk, bk = BANKS[2 + h], ("MM", "EQ")[h]
-        KK, DD = T[kk], T[bk]
-        PE(1024, ["MF" + H, "R1H"], [kk], [(KK[:, 160:164], T.R1H[:, 15 - p:143 - p], MF[:, 64 * h + p:64 * h + 64:16], p == 0, p == 15) for p in range(16)])
-        V(64, [kk], ["E16" + H], ts(E16[:], KK[:, 160:164], 2048.0, None, A.add))
-        V(64, [kk], ["EF" + H], cp(ef, KK[:, 160:164]))
-        SC(4, [kk], ["EG" + H], ac(T.EF[:, h, 4:8], KK[:, 160:164], AF.Copy, bias=2048.0))
-        su = T.SU[:, h, :]
-        V(156, RK + ["E16" + H, "Z5" + H], ["SU" + H], tt(su, T.ROCK[:, 0:4096].indirect(E16[:]), T.Z5[:, h, :], A.add))
-        V(64, ["SU" + H], ["Y1" + H], ts(T.Y1[:, h, :], su, 0.5, None, A.mult))
-        V(64, ["Y1" + H], ["ZO" + k], cp(T.ZO[:, o:o + 64], T.Y1[:, h, :]))
-        send("z", t, h, ["ZO" + k])
-        w = 64 + 64 * h
-        mm = []
-        for c in range(4):
-            mm.append((DD[:, c * w:c * w + w], T.BLH[:], MF[:, 0:w], True, False))
-            mm.append((DD[:, c * w + w - 64:c * w + w], IH, T.MK[:, 256 * t + 64 * c:256 * t + 64 * c + 64], False, True))
-        PE(4 * w + 256, ["MF0", "MF" + H, "MK%d" % t, "BLH", "IEH"], [bk], mm)
-        for c in range(4):
-            du = T.DU[:, h, c * w:c * w + w]
-            V(w, [bk, "EF" + H], ["DU%s%d" % (H, c)], ts(du, DD[:, c * w:c * w + w], T.EF[:, h, c:c + 1], 8192.0, A.is_equal, A.mult))
-            j = 4 * h + c
-            lo = T.LO[:, j:j + 1]
-            if c in LOV[h]:
-                V(w, ["DU%s%d" % (H, c)], ["LO%s%d" % (H, c)], (lambda lo, du: lambda: v.tensor_reduce(lo, du, AxisListType.X, A.add))(lo, du))
+    def mining(t, s):
+        k, H, xk = "%d%d" % (t, s), str(s), "X%d" % s
+        o = 2 * t + s
+        X, E16, OF, RO = T[xk], T["E16" + H], T["OF" + H], T["ROCK" + H]
+        last = t == NV - 1
+        if not last:
+            send("f", t, s, ["FO" + k])
+        mf = T.MF[:, s, :]
+        V(128, ["FO" + k, xk, "SM" + H], ["MF" + H], *[tt(T.MF[:, s, 64 * a:64 * a + 64], X[:, 64 * a:64 * a + 64], T.FO[:, o, :], A.mult) for a in range(2)])
+        EL, VV = MM[:, 160:168], MM[:, 168:176]
+        PE(1024, ["MF" + H, "RW"], ["MM"], [(EL, T.RW[:, 15 - p:143 - p], T.MF[:, s, p:128:16], p == 0, p == 15) for p in range(16)])
+        V(64, ["MM"], ["E16" + H], ts(E16[:], EL, 2048.0, None, A.add))
+        if OPT["ef"] == "s":
+            SC(8, ["MM"], ["EF" + H], ac(T.EF[:, s, :], EL, AF.Copy, bias=2048.0))
+        else:
+            V(64, ["MM"], ["EF" + H], ts(T.EF[:, s, :], EL, 2048.0, None, A.add))
+        ya = T.YA[:, s, :]
+        if OPT["ya"] == "s":
+            SC(128 * GAT + 5, rk(s) + ["E16" + H], ["YA" + H], ac(ya, RO[:, 0:4096].indirect(E16[:]), AF.Copy))
+        else:
+            V(128 * GAT + 57, rk(s) + ["E16" + H], ["YA" + H], cp(ya, RO[:, 0:4096].indirect(E16[:])))
+        for x in range(4):
+            bk = "EQ"
+            dd = EQ[:, 128 * x:128 * x + 128]
+            PE(384, ["MF" + H, "MK%d" % t, "IB", "GS%d" % x], [bk], [(dd, IB, T.MK[:, t, :], True, False), (dd, T.GS[:, x, :], mf, False, False),
+                                                                    (dd, mf, T.GS[:, 4 + x, :], False, True)])
+        zz = HT[:, 0:64]
+        PE(64 * 3, zk(t, s) + ["QR", "ONES", "HB"], ["HT"], [(zz, T.QR[0:1, :], T.ONES[0:1, 0:64], True, False)] +
+           [(HT[:, 32 * b:32 * b + 32], T.HB[:, 2, :], T.Z[:, o, b:64:2], False, False) for b in range(2)])
+        PE(128, ["YA" + H, "HB"], ["HT"], [(zz, T.HB[:, a, :], T.YA[:, s, 64 * a:64 * a + 64], False, a == 1) for a in range(2)])
+        big = 1.5 * 2 ** 23
+        if last:
+            V(128, ["HT"], ["YZ" + H], *[ts(T.YZ[:, s, 32 * b:32 * b + 32], HT[:, b:64:2], big, big, A.add, A.subtract) for b in range(2)])
+            V(128, ["FO" + k], ["YF" + H], *[ts(T.YF[:, s, 32 * b:32 * b + 32], T.FO[:, o, b:64:2], 2048.0, None, A.add) for b in range(2)])
+        else:
+            V(64, ["HT"], ["ZO" + k], ts(T.ZO[:, o, :], zz, big, big, A.add, A.subtract))
+            send("z", t, s, ["ZO" + k])
+        PE(128 + 256, ["YA" + H, "Z4" + H, "IB", "NSEL0", "NSEL1"], ["HT"], [(HT[:, 128:256], IB, ya, True, False)] +
+           [(HT[:, 128 + 64 * a + 32 * b:160 + 64 * a + 32 * b], T.SEL[:, 2 + a, :], T.Z4[:, s, b:64:2], False, a + b == 2) for a in range(2) for b in range(2)])
+        if OPT["rn"] == "s":
+            SC(128, ["HT", "b128"], ["RN" + H], ac(T.RN[:, s, :], HT[:, 128:256], AF.Relu, bias=T.RF[:, 12:13]))
+        else:
+            V(128, ["HT"], ["RN" + H], ts(T.RN[:, s, :], HT[:, 128:256], 129.0, 0.0, A.add, A.max))
+        PE(256, ["DUMP", "I32"], ["MM"], [(VV, T.I32[:], T.DUMP[:], True, False)])
+        for x in range(4):
+            bk = "EQ"
+            dd = EQ[:, 128 * x:128 * x + 128]
+            lo, lx = T.LO[:, s, x:x + 1], T.LX[:, s, 8 * x:8 * x + 8]
+            V(128, [bk], ["LO%s%d" % (H, x)], (lambda lo, dd: lambda: v.tensor_reduce(lo, dd, AxisListType.X, A.min, negate=True, apply_absolute_value=True))(lo, dd))
+            if OPT["lx"] == "s":
+                SC(8, ["LO%s%d" % (H, x), "WD"], ["LX%s%d" % (H, x)], ac(lx, T.WD[:, 8:16], AF.Copy, scale=lo))
             else:
-                SC(w + 24, ["DU%s%d" % (H, c)], ["DU%s%d" % (H, c), "LO%s%d" % (H, c)], ac(du, du, AF.Copy, accum_out=lo))
-            V(64, ["LO%s%d" % (H, c), "DUMP", "EG" + H], ["OF%d" % j], ts(T.OF[:, j:j + 1], lo, T.DUMP[:, j:j + 1], T.EF[:, h, 4 + c:5 + c], A.min, A.max))
-        V(64, ["SU" + H, "X" + H], ["RR" + H], tt(T.RR[:, h, :], su, T["X" + H][:, 0:64], A.subtract))
-        SC(64, ["RR" + H, "b129"], ["RN" + H], ac(T.RN[:, 64 * h:64 * h + 64], T.RR[:, h, :], AF.Relu, bias=T.RF[:, 8:9]))
+                V(64, ["LO%s%d" % (H, x), "WD"], ["LX%s%d" % (H, x)], ts(lx, T.WD[:, 8:16], lo, None, A.mult))
+            PE(64, ["LX%s%d" % (H, x), "BK"], ["MM"], [(VV, T.BK[:, x, :], lx, False, x == 3)])
+        V(64, ["MM", "EF" + H], ["OT" + H], tt(T.OT[:, s, :], VV, T.EF[:, s, :], A.max))
+        V(64, ["OT" + H], ["OF" + H], cp(OF[:], T.OT[:, s, :]))
+        V(57 + 128 * SCA, ["OF" + H, "RN" + H], rk(s), cp(RO[:].indirect(OF[:]), T.RN[:, s, :]))
+        if last:
+            for a in range(2):
+                n = "%d%d" % (s, a)
+                dma("y", "od_f" + n, T.yf[rows(s), rows(a)], T.YF[rows(a), s, :], ["YF" + H], ["of" + n], 2.0)
+                dma("y", "od_z" + n, T.yz[rows(s), rows(a)], T.YZ[rows(a), s, :], ["YZ" + H], ["oz" + n], 2.0)
+            for a in range(2):
+                n = "%d%d" % (s, a)
+                dma("ys"[a * s], "od_x" + n, T.yx[rows(s), 2048 * a:2048 * a + 2048], RO[rows(a), 2048 * a:2048 * a + 2048], rk(s), ["ox" + n], 3.5)
 
-    names = [(claims, "c"), (moves, "m"), (meetings, "e"), (mining, "i")]
-
-    def stage(f, t, h):
-        S["st"] = [n for f2, n in names if f2 == f][0] + str(h)
-        f(t, h)
-        S["st"] = ""
+    def count(t):
+        PE(128, ["MS0", "MS1", "S15"], ["HT"], [(HT[:, 256:288], T.S15[:], T.MS[:, s, 64:96], s == 0, s == 1) for s in range(2)])
+        V(64, ["HT"], ["CN"], lambda: v.tensor_reduce(T.CN[:, 0:1], HT[:, 256:288], AxisListType.X, A.add))
+        V(64, ["CN"], ["CI0"], cp(T.CI[:, 0:1], T.CN[:, 0:1]))
+        V(64, ["CI0"], ["CI1"], ts(T.CI[:, 1:2], T.CI[:, 0:1], 3, None, A.bitwise_and))
+        V(128, ["CI1", "LIM"], ["TOP%d" % (t + 1)], *[ts(T.TOP[:, s, t + 1:t + 2], T.CI[:, 1:2], T.LIM[:, s:s + 1], None, A.add) for s in range(2)])
 
     for t in range(NV):
-        stage(claims, t, 0)
-        if t == 0:
-            stage(claims, t, 1)
-        stage(moves, t, 0)
-        if t > 0:
-            stage(claims, t, 1)
-        stage(moves, t, 1)
-        stage(meetings, t, 0)
-        stage(meetings, t, 1)
-        stage(mining, t, 0)
-        stage(mining, t, 1)
-        V(60 + 128 * 3.8, ["OF%d" % j for j in range(8)] + ["RN0", "RN1"], RK, cp(T.ROCK[:].indirect(T.OF[:]), T.RN[:]))
-        if t < NV - 1:
-            PE(128, ["JM0", "JM1", "S15"], ["MM"], [(MM[:, 256 + 32 * h:288 + 32 * h], T.S15[:], T.JM[:, h, :], True, True) for h in range(2)])
-            V(64, ["MM"], ["CN"], lambda: v.tensor_reduce(T.CN[:, 0:1], MM[:, 256:320], AxisListType.X, A.add))
-            V(64, ["CN"], ["CI0"], cp(T.CI[:, 0:1], T.CN[:, 0:1]))
-            V(64, ["CI0"], ["CI1"], ts(T.CI[:, 1:2], T.CI[:, 0:1], 3, None, A.bitwise_and))
-            V(64, ["CI1", "LIM"], ["TOP%d" % (t + 1)], ts(T.TOP[:, t + 1:t + 2], T.CI[:, 1:2], T.LIM[:, 0:1], None, A.add))
-    t = NV - 1
-    for h in range(2):
-        o = (2 * t + h) * 64
-        for b in range(2):
-            c = 64 * h + 32 * b
-            SC(32, ["FOj%d%d" % (t, h), "FOs%d%d" % (t, h)], ["YF%d%d" % (h, b)], ac(T.YF[:, c:c + 32], T.FO[:, o + b:o + 64:2], AF.Copy))
-            SC(32, ["ZO%d%d" % (t, h)], ["YZ%d%d" % (h, b)], ac(T.YZ[:, c:c + 32], T.ZO[:, o + b:o + 64:2], AF.Copy))
-    hb = ["00", "01", "10", "11"]
-    add(S, "y", 0.06, ["YF" + x for x in hb], ["oF"], lambda: g.sync.dma_start(T.yf[:], T.YF[:]).then_inc(T.sem.od_f, 16), ("od_f", 16), 2.0)
-    add(S, "y", 0.06, ["YZ" + x for x in hb], ["oZ"], lambda: g.sync.dma_start(T.yz[:], T.YZ[:]).then_inc(T.sem.od_z, 16), ("od_z", 16), 2.0)
-    add(S, "y", 0.06, RK, ["oX"], lambda: g.sync.dma_start(T.yx[:], T.ROCK[:, 0:4096]).then_inc(T.sem.od_x, 16), ("od_x", 16), 5.0)
+        for s in range(2):
+            for f, n in ((claims, "c"), (moves, "m"), (choice, "s"), (meetings, "e")):
+                S["st"] = n + str(s)
+                f(t, s)
+            if s == 1 and t < NV - 1:
+                S["st"] = "n"
+                count(t)
+            S["st"] = "i" + str(s)
+            mining(t, s)
     return S
 
 
@@ -566,11 +673,12 @@ def rank_program(g, core, T, topo):
     if T.rank_of(core) is None:
         return
     S = record(g, core, T, topo)
-    order = plan(S)
+    if "order" not in PLANS:
+        PLANS["order"] = plan(S)
     eng = {"v": g.vector, "s": g.scalar, "t": g.tensor, "g": g, "y": g.sync}
-    cnt = issue(S, order, eng, T)
+    cnt = issue(S, PLANS["order"], eng, T)
     for s in sorted(cnt):
         g.wait_ge(T.sem[s], cnt[s])
-    for s in ("od_f", "od_z", "od_x"):
-        g.wait_ge(T.sem[s], 16)
+    for s in STORES:
+        g.wait_ge(T.sem["od_" + s], 16)
     g.wait_ge(T.sem.sl, S["sends"])

@@ -2,7 +2,9 @@ from concourse.mybir import AluOpType as A, ActivationFunctionType as AF, AxisLi
 
 NV = 5
 NG = 32
-INT = True
+U16S = True
+U16B = False
+U16T = True
 SCRATCH = {
     "PI": ("sbuf", [128, 8], "int32"), "RF": ("sbuf", [128, 16], "float32"),
     "ONES": ("sbuf", [128, 128], "bfloat16"), "NEG": ("sbuf", [128, 128], "bfloat16"), "IB": ("sbuf", [128, 128], "bfloat16"),
@@ -13,7 +15,7 @@ SCRATCH = {
     "T1": ("sbuf", [128, 128], "float32"), "T2": ("sbuf", [128, 128], "float32"), "T3": ("sbuf", [128, 128], "bfloat16"),
     "T4": ("sbuf", [128, 128], "bfloat16"), "TI": ("sbuf", [128, 128], "int32"), "P4": ("sbuf", [128, 128], "float32"),
     "KT": ("sbuf", [128, 16], "float32"), "NKT": ("sbuf", [128, 16], "float32"), "KH": ("sbuf", [128, 8], "float32"),
-    "SCM": ("sbuf", [128, 4, 128], "bfloat16"), "L3": ("sbuf", [128, 128], "bfloat16"), "R3": ("sbuf", [128, 320], "bfloat16"),
+    "SCM": ("sbuf", [128, 4, 128], "bfloat16"), "L3": ("sbuf", [128, 128], "bfloat16"), "R3": ("sbuf", [128, 512], "bfloat16"),
     "WD": ("sbuf", [128, 16], "bfloat16"), "CM": ("sbuf", [128, 256], "bfloat16"), "RS": ("sbuf", [128, 128], "bfloat16"),
     "XK": ("sbuf", [128, 144], "bfloat16"), "RK": ("sbuf", [128, 2, 144], "bfloat16"), "NIB": ("sbuf", [128, 128], "bfloat16"),
     "R1": ("sbuf", [128, 32], "bfloat16"), "CJ": ("sbuf", [128, 32], "bfloat16"),
@@ -22,28 +24,26 @@ SCRATCH = {
     "S15": ("sbuf", [128, 128], "bfloat16"), "I32B": ("sbuf", [128, 128], "bfloat16"), "HB": ("sbuf", [128, 3, 128], "bfloat16"),
     "SEL": ("sbuf", [128, 4, 128], "bfloat16"), "GS": ("sbuf", [128, 8, 128], "bfloat16"), "BK": ("sbuf", [128, 4, 128], "bfloat16"),
     "CL": ("sbuf", [128, NV, 128], "bfloat16"), "MK": ("sbuf", [128, NV, 128], "bfloat16"), "DUMP": ("sbuf", [128, 8], "float32"),
-    "QR": ("sbuf", [128, 128], "bfloat16"),
+    "QR": ("sbuf", [128, 128], "bfloat16"), "QS": ("sbuf", [128, 64], "bfloat16"),
     "WI": ("sbuf", [128, 2], "int32"), "WL": ("sbuf", [128, 2], "bfloat16"), "W2": ("sbuf", [128, 2, 128], "bfloat16"),
-    "LIM": ("sbuf", [128, 2], "float32"), "TOP": ("sbuf", [128, 2, 8], "float32"), "CN": ("sbuf", [128, 4], "float32"),
-    "CI": ("sbuf", [128, 4], "int32"),
+    "LIM": ("sbuf", [128, 2], "float32"), "TOP": ("sbuf", [128, NV, 70], "float32"), "CN": ("sbuf", [128, 2, 70], "float32"),
     "FI": ("sbuf", [128, 2, 64], "int32"),
     "F": ("sbuf", [128, 2 * NV, 64], "float16"), "FO": ("sbuf", [128, 2 * NV, 64], "float16"),
     "Z": ("sbuf", [128, 2 * NV, 64], "bfloat16"), "ZO": ("sbuf", [128, 2 * NV, 64], "bfloat16"),
     "YF": ("sbuf", [128, 2, 64], "float32"), "YZ": ("sbuf", [128, 2, 64], "bfloat16"),
 }
-for _n, _w, _d in (("UA", 128, "int32"), ("UI", 320, "int32"), ("SI", 64, "int32"), ("QI", 64, "int32"), ("HM", 320, "int32"),
+for _n, _w, _d in (("UA", 64, "int32"), ("UI", 512, "float32"), ("SI", 64, "int32"), ("HM", 512, "int32"),
                    ("C4", 256, "int32"), ("UF", 32, "float32"), ("Z4", 64, "bfloat16"), ("KE", 128, "float32"),
-                   ("KS", 256, "int32" if INT else "float32"),
-                   ("KB", 64, "int32"), ("KC", 64, "int32"), ("NB", 64, "int32"), ("PR", 320, "float32"), ("HF", 64, "float16"),
+                   ("KS", 256, "int32"), ("KC", 64, "int32"), ("NB", 64, "int32"), ("PR", 320, "float32"), ("HF", 64, "float16"),
                    ("JC", 64, "float16"), ("NS", 64, "float32"), ("EQB", 512, "bfloat16"), ("PM", 32, "bfloat16"),
-                   ("MS", 128, "bfloat16"), ("SX", 32, "float32"), ("JI", 32, "float32"), ("JU", 32, "int32"), ("JX", 32, "int32"),
+                   ("MS", 128, "bfloat16"), ("SX", 32, "float32"), ("JU", 64, "int32"), ("JX", 32, "int32"),
                    ("DF", 64, "float32"), ("DM", 64, "float32"), ("MF", 128, "float16"), ("EF", 8, "float32"), ("YA", 128, "bfloat16"),
                    ("LO", 4, "float32"), ("LX", 32, "bfloat16"), ("OT", 8, "float32"), ("RN", 128, "bfloat16"),
                    ("D", 4096, "bfloat16"), ("NR", 4096, "bfloat16")):
     SCRATCH[_n] = ("sbuf", [128, 2, _w], _d)
 for _s in "01":
     for _n, _w, _d in (("ROCK", 4096 + 128, "bfloat16"), ("CO", 256, "uint16"), ("ZX", 16 * NG, "bfloat16"), ("HW", 512, "float32"),
-                       ("LS", 2, "uint16"), ("E16", 8, "uint16"), ("OF", 8, "uint16")):
+                       ("LS", 34, "uint16"), ("E16", 8, "uint16"), ("OF", 8, "uint16")):
         SCRATCH[_n + _s] = ("sbuf", [128, _w], _d)
 BANKS = ["X0", "X1", "K0", "K1", "KX", "EQ", "HT", "MM"]
 for _n in BANKS:
@@ -65,10 +65,13 @@ BIAS = {}
 SGRP = 2
 VP = 2
 LOOK = 0.4
-ZV = 4
-ABS = (6, 8, 10, 12)
-NPC = 512
-OPT = {"lx": "v", "rn": "s", "ya": "v", "ke": "s", "ef": "v"}
+ROUNDS = 3
+KS = ("EL", "HB", "U1")
+ZS = 10
+ZV = 0
+ABS = (10, 11, 13, 14)
+NPC = 256
+OPT = {"lx": "v", "rn": "s", "ya": "v", "ke": "s", "ef": "v", "z4": "v"}
 PLANS = {}
 
 
@@ -164,7 +167,52 @@ def plan(S):
             if left[k] == 0:
                 ready.setdefault(ops[k]["q"], []).append(k)
     S["end"] = end
-    return order
+    if not ROUNDS:
+        return order
+    pred = [[(j, (ops[j]["lat"] if ops[j]["sig"] else LAT) if d else 0.0) for j, d in o["deps"].items()] for o in ops]
+    after = [[] for _ in ops]
+    for i in range(n):
+        for j, l in pred[i]:
+            after[j].append((i, l))
+    start = [o["start"] for o in ops]
+    best = (end, start)
+    for _ in range(ROUNDS):
+        rank = sorted(range(n), key=lambda i: (-(start[i] + ops[i]["cost"]), -start[i], -i))
+        back = place(ops, rank, after, [o["lat"] for o in ops])
+        rank = sorted(range(n), key=lambda i: (-(back[i] + ops[i]["cost"]), -back[i], i))
+        start = place(ops, rank, pred, [0.0] * n)
+        end = max(s + o["cost"] + o["lat"] for s, o in zip(start, ops))
+        if end < best[0]:
+            best = (end, start)
+    S["end"], start = best
+    for s, o in zip(start, ops):
+        o["start"] = s
+    return sorted(range(n), key=lambda i: start[i])
+
+
+def place(ops, rank, pred, first):
+    start = [None] * len(ops)
+    lines = {}
+    for i in rank:
+        t = first[i]
+        for j, l in pred[i]:
+            t = max(t, start[j] + ops[j]["cost"] + l)
+        c = ops[i]["cost"]
+        a, b = lines.setdefault(ops[i]["q"], ([], []))
+        lo, hi = 0, len(a)
+        while lo < hi:
+            mid = (lo + hi) // 2
+            if b[mid] <= t:
+                lo = mid + 1
+            else:
+                hi = mid
+        while lo < len(a) and a[lo] < t + c - 1e-9:
+            t = max(t, b[lo])
+            lo += 1
+        a.insert(lo, t)
+        b.insert(lo, t + c)
+        start[i] = t
+    return start
 
 
 def issue(S, order, eng, T):
@@ -272,6 +320,11 @@ def record(g, core, T, topo):
             n = "%d%d" % (s, a)
             dma("y", "ld_r" + n, T["ROCK%d" % s][rows(a), 0:4096], T.rock[rows(s), :], [], ["ROCK" + n], 5.0 + 3.5 * s)
 
+    def scaled(n, R, W, *xs):
+        if n in KS:
+            SC(128 * len(xs), R, W, *[ac(o, a, AF.Copy, scale=c) for o, a, c in xs])
+        else:
+            V(64, R, W, *[ts(o, a, c, None, A.mult) for o, a, c in xs])
     S["st"] = "k"
     G(1, [], ["PI"], ioI(T.PI[:, 0:1], [[1, 1]], 0, 1))
     G(128, [], ["GR"], ioF(T.GR[:], [[1, 8], [0, 16]], 0, 0))
@@ -295,27 +348,31 @@ def record(g, core, T, topo):
     for s in range(2):
         V(64, ["MM", "BLK"], ["W2%d" % s], ts(T.W2[:, s, :], T.BLK[:], T.MM[:, 2 * s:2 * s + 1], 2.0, A.mult, A.mult))
     V(64, ["MM"], ["LIM"], ts(T.LIM[:], T.MM[:, 1:4:2], 0.5, None, A.add))
-    V(64, ["LIM"], ["TOP0"], cp(T.TOP[:, :, 0], T.LIM[:]))
+    V(64, ["LIM"], ["TOP0"], cp(T.TOP[:, 0, 68:70], T.LIM[:]))
+    V(140, [], ["CNz"], ms(T.CN[:, 0, :], 0.0), ms(T.CN[:, 1, :], 1.0))
+    V(64, ["CNz", "LIM"], ["CN"], cp(T.CN[:, 0, 68:69], T.LIM[:, 0:1]), tt(T.CN[:, 0, 69:70], T.LIM[:, 1:2], T.LIM[:, 0:1], A.subtract),
+      *[ms(T.CN[:, x, c:c + 1], y) for x, c, y in ((0, 32, -0.375), (0, 33, 1.5 * 2 ** 23), (0, 34, -1.5 * 2 ** 23), (1, 32, 0.25), (1, 35, -4.0))])
     for s in range(2):
         V(64, ["FI%d0" % s, "FI%d1" % s], ["F0%d" % s], ts(T.F[:, s, :], T.FI[:, s, :], -2048.0, None, A.add))
-    pw = [32, 32, 64, 128] if INT else [32, 64, 128, 256]
+    pw = [32, 32, 64, 128]
     for m in range(4):
         V(64, ["IB"], ["SCM%d" % m], ts(T.SCM[:, m, :], T.IB[:], float(pw[m]), None, A.mult))
     V(64, ["IB"], ["NIB"], ts(T.NIB[:], T.IB[:], -1.0, None, A.mult))
     V(64, [], ["L3z"], ms(T.L3[:], 1.0))
     V(64, ["L3z", "CR"], ["L3"], cp(T.L3[0:1, :], T.CR[0:1, :]))
-    V(160, [], ["R3z"], ms(T.R3[:], 0.0))
+    V(256, [], ["R3z"], ms(T.R3[:], 0.0))
     fills = []
     for m in range(4):
         c = (2048 + 613 * m) * 2 ** (5 + m) - 2 ** 23
-        if INT and m:
+        if m:
             c -= (2048 + 613 * (m - 1)) * 2 ** (4 + m) - 2 ** 23
         hi = (c >> 16) << 16
         lo1 = ((c - hi) >> 8) << 8
         for row, x in ((0, 37 * pw[m]), (32, hi), (64, lo1), (96, c - hi - lo1)):
             if x:
-                fills.append(ms(T.R3[row:row + 1, 1 + m:320:5], float(x)))
-    fills.append(ms(T.R3[32:33, 0:320:5], 2048.0))
+                fills.append(ms(T.R3[row:row + 1, 4 + m:512:8], float(x)))
+    for row, col, x in ((32, 0, -2048.0), (64, 0, 1.0), (32, 1, 1.5 * 2 ** 23), (32, 2, -1.5 * 2 ** 23), (32, 3, 1.0)):
+        fills.append(ms(T.R3[row:row + 1, col:512:8], x))
     V(64, ["R3z"], ["R3"], *fills)
     V(64, ["PIr"], ["PIs"], ts(T.PI[:, 5:6], T.PI[:, 1:2], 1.0, None, A.add))
     V(64, ["PIs"], ["PIt"], ts(T.PI[:, 6:7], T.PI[:, 5:6], 15, None, A.bitwise_and))
@@ -332,14 +389,17 @@ def record(g, core, T, topo):
     G(144, [], ["XK"], ioF(T.XK[:], [[1, 144]], -15, 0))
     V(64, ["r"], ["g16"], ts(T.RF[:, 13:14], gp, 16.0, None, A.mult))
     V(144, ["XK", "g16"], ["RK"], *[ts(T.RK[:, x, :], T.XK[:], T.RF[:, 13:14], (256.0, 1.0)[x], A.is_equal, A.mult) for x in range(2)])
-    if INT:
-        for s in range(2):
-            V(320, [], ["UIa%d" % s], ms(T.UI[:, s, :], 1))
-            V(64, ["UIa%d" % s], ["UI%d" % s], ms(T.UI[:, s, 0:320:5], 0))
+    for s in range(2):
+        if "U%d" % s in KS:
+            G(512, [], ["UIa%d" % s], ioF(T.UI[:, s, :], [[0, 512]], 1, 0))
+        else:
+            V(512, [], ["UIa%d" % s], ms(T.UI[:, s, :], 1.0))
+        V(192, ["UIa%d" % s], ["UI%d" % s], *[ms(T.UI[:, s, c:512:8], x) for c, x in ((0, 0.0), (1, 2.0 ** -12), (3, -4096.0))])
+        V(64, [], ["NS%d" % s], ms(T.NS[:, s, :], 0.0))
     V(64, ["CR", "r"], ["KT"], ts(T.KT[:], T.CR[:, 0:16], r, None, A.is_equal))
     V(64, ["KT"], ["NKT"], ts(T.NKT[:], T.KT[:], -1.0, None, A.mult))
     for l in range(0, 16, 4):
-        V(256, ["BLK", "NKT"], ["EL%d" % l], *[ts(T.EL[:, x, :], T.BLK[:], T.NKT[:, x:x + 1], None, A.mult) for x in range(l, l + 4)])
+        scaled("EL", ["BLK", "NKT"], ["EL%d" % l], *[(T.EL[:, x, :], T.BLK[:], T.NKT[:, x:x + 1]) for x in range(l, l + 4)])
     V(64, ["CR", "r"], ["T3"], ts(T.T3[:], T.CR[:], r, -(2.0 ** 40), A.is_gt, A.mult))
     V(128, ["T3", "BLK"], ["SLB"], tt(T.SLB[:], T.T3[:], T.BLK[:], A.mult))
     for l in range(16):
@@ -353,8 +413,7 @@ def record(g, core, T, topo):
     V(64, ["CR", "r"], ["T3"], ts(T.T3[:], T.CR[:], r, None, A.is_ge))
     V(128, ["T3", "BLK"], ["QC"], tt(T.QQ[:, 2, :], T.T3[:], T.BLK[:], A.mult))
     V(128, ["KT"], ["KH"], ts(T.KH[:, 0:1], T.KT[:, 15:16], -512.0, None, A.mult), ts(T.KH[:, 1:2], T.KT[:, 15:16], 512.0, -32.0, A.mult, A.add))
-    V(192, ["BLK", "KH"], ["WX"], ts(T.WX[:, 0, :], T.BLK[:], 32.0, None, A.mult), ts(T.WX[:, 1, :], T.BLK[:], T.KH[:, 0:1], None, A.mult),
-      ts(T.WX[:, 2, :], T.BLK[:], T.KH[:, 1:2], None, A.mult))
+    scaled("WX", ["BLK", "KH"], ["WX"], (T.WX[:, 0, :], T.BLK[:], 32.0), (T.WX[:, 1, :], T.BLK[:], T.KH[:, 0:1]), (T.WX[:, 2, :], T.BLK[:], T.KH[:, 1:2]))
     G(32, [], ["T4j"], ioF(T.T4[:, 0:32], [[1, 32]], 0, 0))
     V(64, ["CR", "r"], ["T3"], ts(T.T3[:, 0:32], T.CR[:, 0:32], r, -2048.0, A.not_equal, A.mult))
     V(64, ["T3", "T4j"], ["CJ"], tt(T.CJ[:], T.T3[:, 0:32], T.T4[:, 0:32], A.add))
@@ -372,27 +431,28 @@ def record(g, core, T, topo):
     V(64, ["r"], ["m16"], ts(T.RF[:, 9:10], mi, 16.0, None, A.mult))
     V(72, ["XR", "m16"], ["RW"], ts(T.RW[:], T.XR[:], T.RF[:, 9:10], None, A.is_equal))
     V(128, ["r"], ["hh"], ts(T.RF[:, 10:11], ha, -0.5, 0.5, A.mult, A.add), ts(T.RF[:, 11:12], ha, 0.5, None, A.mult))
-    V(192, ["IB", "hh"], ["HB"], ts(T.HB[:, 0, :], T.IB[:], T.RF[:, 10:11], None, A.mult), ts(T.HB[:, 1, :], T.IB[:], T.RF[:, 11:12], None, A.mult),
-      ts(T.HB[:, 2, :], T.IB[:], 0.5, None, A.mult))
-    V(64, [], ["QR"], ms(T.QR[0:1, :], -0.25))
+    scaled("HB", ["IB", "hh"], ["HB"], (T.HB[:, 0, :], T.IB[:], T.RF[:, 10:11]), (T.HB[:, 1, :], T.IB[:], T.RF[:, 11:12]), (T.HB[:, 2, :], T.IB[:], 0.5))
+    V(128, [], ["QR"], ms(T.QR[0:1, :], -0.25), ms(T.QR[32:33, :], 2048.0))
+    V(64, [], ["QSz"], ms(T.QS[32:33, :], 0.0))
+    V(64, ["QSz"], ["QS"], ms(T.QS[32:33, 0:64:2], 1.0))
     V(256, ["r"], ["KM"], *[ts(T.KH[:, 4 + x:5 + x], mi, float(x), None, A.is_equal) for x in range(4)])
     for x in range(4):
-        V(128, ["ONES", "NEG", "KM"], ["GS%d" % x], ts(T.GS[:, x, :], T.ONES[:], T.KH[:, 4 + x:5 + x], None, A.mult),
-          ts(T.GS[:, 4 + x, :], T.NEG[:], T.KH[:, 4 + x:5 + x], None, A.mult))
+        scaled("GS", ["ONES", "NEG", "KM"], ["GS%d" % x], (T.GS[:, x, :], T.ONES[:], T.KH[:, 4 + x:5 + x]), (T.GS[:, 4 + x, :], T.NEG[:], T.KH[:, 4 + x:5 + x]))
     G(128, [], ["G4"], ioF(T.G4[:], [[0, 2], [1, 4], [0, 16]], 0, 0))
     V(64, ["CR", "r"], ["T3"], ts(T.T3[:], T.CR[:], r, 100.0, A.not_equal, A.mult))
     V(128, ["T3", "G4"], ["G4"], tt(T.G4[:], T.G4[:], T.T3[:], A.add))
     V(256, ["G4"], ["BK"], *[ts(T.BK[:, x, :], T.G4[:], float(x), 8192.0, A.is_equal, A.mult) for x in range(4)])
     G(8, [], ["DUMPa"], ioF(T.DUMP[:], [[16, 8]], 4096, 0))
     V(64, ["DUMPa", "r"], ["DUMP"], ts(T.DUMP[:], T.DUMP[:], r, None, A.add))
-    for t in range(NV):
+    V(64, [], ["b128"], ms(T.RF[:, 12:13], 129.0))
+    S["st"] = ""
+
+    def earlier(t):
         a = t + 1
         G(128, [], ["CL%d" % t], ioF(T.CL[0:1, t, :], [[64, 2], [1, 2 ** a], [2 ** a, 2 ** (6 - a)]], 0, 0))
         PE(256, ["CL%d" % t, "ONES", "NEG"], ["EQ"], [(T.EQ[:, 0:128], T.ONES[0:1, :], T.CL[0:1, t, :], True, False),
                                                       (T.EQ[:, 0:128], T.CL[0:1, t, :], T.NEG[0:1, :], False, True)])
         V(128, ["EQ"], ["MK%d" % t], ts(T.MK[:, t, :], T.EQ[:, 0:128], 0.0, 8192.0, A.is_ge, A.mult))
-    V(64, [], ["b128"], ms(T.RF[:, 12:13], 129.0))
-    S["st"] = ""
 
     MM, EQ, KX, HT = T.MM, T.EQ, T.KX, T.HT
     IB = T.IB[:]
@@ -412,38 +472,42 @@ def record(g, core, T, topo):
         k, H, xk = "%d%d" % (t, s), str(s), "X%d" % s
         o = 2 * t + s
         X, CO, ZX = T[xk], T["CO" + H], T["ZX" + H]
-        nX = X[:, 128:448:5]
-        mm = [(X[:, 128:448], T.L3[0:97, :], T.R3[0:97, :], True, False)]
-        for m in range(5):
+        nodes = [(X[:, 384:448], T.QR[32:33, :], T.ONES[32:33, 0:64], True, False)] + [(X[:, 384 + 32 * b:416 + 32 * b], IB, T.F[:, o, b:64:2], False, b == 1) for b in range(2)]
+        PE(192, ["F" + k, "QR", "ONES", "IB"], [xk], nodes)
+        SC(64, [xk], ["UI" + H], ac(T.UI[:, s, 4:512:8], X[:, 384:448], AF.Copy))
+        mm = [(X[:], T.L3[0:97, :], T.R3[0:97, :], True, False)]
+        for m in range(4):
             for b in range(2):
-                mm.append((X[:, 128 + 160 * b + m:288 + 160 * b:5], T.SCM[:, m - 1, :] if m else IB, T.F[:, o, b:64:2], False, m == 4 and b == 1))
-        PE(320 + 640, ["F" + k, "L3", "R3", "IB"] + ["SCM%d" % m for m in range(4)], [xk], mm)
-        for x in range(2):
-            PE(128, zk(t, s) + ["W2" + H, "BLK"], [xk], [(X[:, 64 * x + 32 * b:64 * x + 32 * b + 32], (T.W2[:, s, :], T.BLK[:])[x], T.Z[:, o, b:64:2], True, True)
-                                                        for b in range(2)])
-        u1 = T.UI[:, s, 1:320:5]
-        V(128, [xk], ["UA" + H], ts(T.UA[:, s, :], X[:, 0:128], 1.0, None, A.add))
-        V(64, ["UA" + H], ["UI" + H], ts(u1, T.UA[:, s, 0:64], 4095, None, A.bitwise_and))
-        if INT:
-            V(320, [xk, "UI" + H], ["HM%s%d" % (H, m) for m in range(4)], scan(T.HM[:, s, :], T.UI[:, s, :], X[:, 128:448], 0.0, A.mult, A.add))
-        else:
-            V(64, [xk, "UI" + H], ["QI" + H], tt(T.QI[:, s, :], nX, u1, A.mult))
+                mm.append((X[:, 256 * b + 4 + m:256 * b + 256:8], T.SCM[:, m, :], T.F[:, o, b:64:2], False, False))
+        PE(512 + 512, ["F" + k, "L3", "R3"] + ["SCM%d" % m for m in range(4)], [xk], mm)
+        PE(256, zk(t, s) + ["W2" + H], [xk], [(X[:, 256 * b + x:256 * b + 256:8], T.W2[:, s, :], T.Z[:, o, b:64:2], False, x + b == 4) for x in (0, 3) for b in range(2)])
+        V(512, [xk, "UI" + H], ["HM" + H], scan(T.HM[:, s, :], T.UI[:, s, :], X[:], 0.0, A.mult, A.add))
+        for m in range(4):
+            V(64, ["HM" + H], ["C4%s%d" % (H, m)], ts(T.C4[:, s, m:256:4], T.HM[:, s, 4 + m:512:8], 5 + m, 4095, A.arith_shift_right, A.bitwise_and))
+        PE(192 + 128, ["F" + k, "QR", "ONES", "IB", "BLK"] + zk(t, s), [xk], nodes + [(X[:, 192 + 32 * b:224 + 32 * b], T.BLK[:], T.Z[:, o, b:64:2], True, True) for b in range(2)])
+        V(64, [xk], ["UA" + H], ts(T.UA[:, s, :], X[:, 192:256], 1.0, None, A.add))
+        if U16B:
+            V(256, ["HM" + H], ["COs" + H], *[ts(CO[:, 4 * NG + m:256:4], T.HM[:, s, 8 * NG + 4 + m:512:8], 5 + m, 4095, A.arith_shift_right, A.bitwise_and) for m in range(4)])
             for m in range(4):
-                V(64, [xk, "QI" + H], ["HM%s%d" % (H, m)], tt(T.HM[:, s, 1 + m:320:5], X[:, 129 + m:448:5], T.QI[:, s, :], A.add))
-        for m in range(4):
-            V(64, ["HM%s%d" % (H, m)], ["C4%s%d" % (H, m)], ts(T.C4[:, s, m:256:4], T.HM[:, s, 1 + m:320:5], 5 + m, 4095, A.arith_shift_right, A.bitwise_and))
-        V(256 - 4 * NG, ["C4%s%d" % (H, m) for m in range(4)], ["COs" + H], cp(CO[:, 4 * NG:256], T.C4[:, s, 4 * NG:256]))
-        for m in range(4):
-            V(64, ["C4%s%d" % (H, m)], ["COv%s%d" % (H, m)], cp(CO[:, NG * m:NG * m + NG], T.C4[:, s, m:4 * NG:4]))
+                V(64, ["HM" + H], ["COv%s%d" % (H, m)], ts(CO[:, NG * m:NG * m + NG], T.HM[:, s, 4 + m:8 * NG:8], 5 + m, 4095, A.arith_shift_right, A.bitwise_and))
+        else:
+            V(256 - 4 * NG, ["C4%s%d" % (H, m) for m in range(4)], ["COs" + H], cp(CO[:, 4 * NG:256], T.C4[:, s, 4 * NG:256]))
+            for m in range(4):
+                V(64, ["C4%s%d" % (H, m)], ["COv%s%d" % (H, m)], cp(CO[:, NG * m:NG * m + NG], T.C4[:, s, m:4 * NG:4]))
         for p in range(16):
             if p < ZV:
                 V(64, zk(t, s), ["ZX%s%d" % (H, p)], cp(ZX[:, p:16 * NG:16], T.Z[:, o, 0:2 * NG:2]))
+            elif p < ZV + ZS:
+                SC(NG, zk(t, s), ["ZX%s%d" % (H, p)], ac(ZX[:, p:16 * NG:16], T.Z[:, o, 0:2 * NG:2], AF.Copy))
             else:
                 G(NG, zk(t, s), ["ZX%s%d" % (H, p)], sel(ZX[:, p:16 * NG:16], T.Z[:, o, 0:2 * NG:2], [[0, NG]], A.is_ge, 0.0, 0, 0))
-        V(64, ["UA" + H], ["SI" + H], ts(T.SI[:, s, :], T.UA[:, s, 64:128], 15, None, A.bitwise_and))
-        V(64, ["UI" + H], ["UF" + H], ts(T.UF[:, s, :], T.UI[:, s, 161:320:5], 16.0, 65536.0 - 16 - 2 ** 18, A.mult, A.add))
+        V(64, ["UA" + H], ["SI" + H], ts(T.SI[:, s, :], T.UA[:, s, :], 15, None, A.bitwise_and))
+        V(64, ["HM" + H], ["UF" + H], ts(T.UF[:, s, :], T.HM[:, s, 259:512:8], 16.0, 65536.0 - 16 - 2 ** 18, A.mult, A.add))
         V(128, ["SI" + H, "rp1"], [xk, "SM" + H], *[ts(X[:, 64 * a:64 * a + 64], T.SI[:, s, :], T.RF[:, 6 + a:7 + a], None, A.is_equal) for a in range(2)])
-        V(64, zk(t, s), ["Z4" + H], ts(T.Z4[:, s, :], T.Z[:, o, :], 0.25, 129 - 0.375, A.mult, A.add))
+        if OPT["z4"] == "s":
+            SC(64, zk(t, s), ["Z4" + H], ac(T.Z4[:, s, :], T.Z[:, o, :], AF.Copy, scale=0.25, bias=129 - 0.375))
+        else:
+            V(64, zk(t, s), ["Z4" + H], ts(T.Z4[:, s, :], T.Z[:, o, :], 0.25, 129 - 0.375, A.mult, A.add))
 
     def moves(t, s):
         H = str(s)
@@ -479,7 +543,7 @@ def record(g, core, T, topo):
         cuts = {0: [16 * NG * m for m in range(5)] + ([2048] if NG < 32 else []), 1: list(range(2048, 4097, NPC))}
         for ch in (0, 1):
             for a, b in zip(cuts[ch][:-1], cuts[ch][1:]):
-                V((b - a) // 2, parts(a, b) + ["TOP%d" % t], ["N%s_%d" % (H, a)], ts(T.NR[:, s, a:b], T.D[:, s, a:b], T.TOP[:, s, t:t + 1], None, A.is_le))
+                V((b - a) // 2, parts(a, b) + ["TOP%d" % t], ["N%s_%d" % (H, a)], ts(T.NR[:, s, a:b], T.D[:, s, a:b], T.TOP[:, t, 68 + s:69 + s], None, A.is_le))
         K0, K1 = T.K0, T.K1
         for p0 in range(0, 16, 4):
             PE(256 + 128 * (p0 == 0), parts(0, 2048) + ["WD", "CM", "ONES"], ["K0"], [(K0[:, 0:128], T.CM[0:1, 0:128], T.ONES[0:1, :], True, False)][:p0 == 0] +
@@ -509,14 +573,10 @@ def record(g, core, T, topo):
         k, H, xk = "%d%d" % (t, s), str(s), "X%d" % s
         o = 2 * t + s
         X = T[xk]
-        if INT:
-            kb, kn = T.KS[:, s, 3:256:4], ["KS%s0" % H, "KS%s1" % H]
-        else:
-            kb, kn = T.KB[:, s, :], ["KB" + H]
-            V(64, ["KS%s0" % H, "KS%s1" % H], kn, cp(kb, T.KS[:, s, 3:256:4]))
+        kb, kn = T.KS[:, s, 3:256:4], ["KS%s0" % H, "KS%s1" % H]
         V(64, kn, ["KC" + H], ts(T.KC[:, s, :], kb, 255, 5, A.bitwise_and, A.arith_shift_right))
         V(64, kn, ["NB" + H], ts(T.NB[:, s, :], kb, 5, 1, A.arith_shift_right, A.bitwise_and))
-        V(64, ["NB" + H, xk], ["PRn" + H], tt(T.PR[:, s, 256:320], X[:, 128:448:5], T.NB[:, s, :], A.mult))
+        V(64, ["NB" + H, xk], ["PRn" + H], tt(T.PR[:, s, 256:320], X[:, 384:448], T.NB[:, s, :], A.mult))
         NP = X[:, 448:512]
         PE(256 + 128, ["PRn" + H, "NI32", "F" + k, "IB"], [xk], [(NP, T.NI32[:], T.PR[:, s, 256:320], True, False)] +
            [(X[:, 448 + 32 * b:480 + 32 * b], IB, T.F[:, o, b:64:2], False, False) for b in range(2)])
@@ -533,10 +593,10 @@ def record(g, core, T, topo):
         X = T[xk]
         NP = X[:, 448:512]
         HW, LS = T["HW" + H], T["LS" + H]
-        SS, JJ = T.NS[:, s, 0:32], T.NS[:, s, 32:64]
+        JJ = T.NS[:, s, 1:64:2]
         V(64, [xk], ["HF" + H], ts(T.HF[:, s, :], NP, 0.125, 1281 - 0.4375, A.mult, A.add))
         V(64, [xk], ["JC" + H], cp(T.JC[:, s, :], NP))
-        SC(64, [xk], ["NS" + H], ac(T.NS[:, s, :], NP, AF.Copy, bias=2048.0))
+        SC(32, [xk], ["NS" + H], ac(JJ, X[:, 480:512], AF.Copy, bias=2048.0))
         for b, bk in ((0, "EQ"), (1, "KX")):
             mm = []
             for l in range(8):
@@ -554,20 +614,26 @@ def record(g, core, T, topo):
                 mm += [(HT[:, 32 * i:32 * i + 32], T.CS[:, i, :], T.JC[:, s, 32:64], True, False), (HT[:, 32 * i:32 * i + 32], T.NIB[:], T.JC[:, s, 0:32], False, True)]
             PE(256, ["JC" + H, "CS%d" % (x // 4 * 4), "NIB"], ["HT"], mm)
         SC(512, ["HT"], ["HW" + H], ac(HW[:], HT[:], AF.Copy))
-        PE(256 + 64, ["JC" + H, "UF" + H, "I32", "I32B"], [xk], [(X[:, 128:160], T.I32[:], T.UF[:, s, :], True, False), (X[:, 128:160], T.I32B[:], T.JC[:, s, 32:64], False, True)])
+        PE(256 + 192, ["JC" + H, "UF" + H, "I32", "I32B", "IB", "QR", "QS"], [xk],
+           [(X[:, 128:192], T.QR[32:33, :], T.QS[32:33, :], True, False), (X[:, 129:192:2], T.I32[:], T.UF[:, s, :], False, False),
+            (X[:, 129:192:2], T.I32B[:], T.JC[:, s, 32:64], False, False), (X[:, 128:192:2], IB, T.JC[:, s, 0:32], False, True)])
         pm = T.PM[:, s, :]
         V(64, ["MM"], ["PM" + H], ts(pm, MM[:, 0:32], 0.0, None, A.max))
         PE(192, ["PM" + H, "QA", "QB", "QC"], ["MM"], [(MM[:, 32 + 32 * x:64 + 32 * x], T.QQ[:, x, :], pm, True, True) for x in range(3)])
         V(96, ["MM"], ["MS" + H], ts(T.MS[:, s, 0:96], MM[:, 32:128], 0.5, None, A.is_ge))
         PE(256, ["MS" + H, "WX", "CJ", "IB"], ["MM"], [(MM[:, 128:160], IB, T.CJ[:], True, False)] +
            [(MM[:, 128:160], T.WX[:, x, :], T.MS[:, s, 32 * x:32 * x + 32], False, x == 2) for x in range(3)])
-        V(64, ["MM", "R1"], ["SX" + H], scan(T.SX[:, s, :], T.R1[:], MM[:, 128:160], 0.0, A.mult, A.max))
-        V(64, ["SX" + H], ["LS" + H], cp(LS[:], T.SX[:, s, 15:32:16]))
         V(64, ["MS" + H], ["CD" + H], tt(T.MS[:, s, 96:128], T.MS[:, s, 0:32], T.MS[:, s, 32:64], A.subtract))
-        V(57 + 32 * GAT, ["LS" + H, "HW" + H, "CD" + H], ["DMs" + H], tt(T.DM[:, s, 0:32], HW[:].indirect(LS[:]), T.MS[:, s, 96:128], A.mult))
-        V(64, ["NS" + H], ["JI" + H], tt(T.JI[:, s, :], JJ, SS, A.mult))
-        V(64, ["JI" + H, xk], ["JU" + H], tt(T.JU[:, s, :], X[:, 128:160], T.JI[:, s, :], A.add))
-        V(64, ["JU" + H], ["JX" + H], ts(T.JX[:, s, :], T.JU[:, s, :], 5, 4095, A.arith_shift_right, A.bitwise_and))
+        if U16S:
+            V(64, ["MM", "R1"], ["LS" + H], scan(LS[:, 1:33], T.R1[:], MM[:, 128:160], 0.0, A.mult, A.max))
+            V(2 * (57 + 16 * GAT), ["LS" + H, "HW" + H, "CD" + H], ["DMs" + H],
+              *[tt(T.DM[:, s, 16 * c:16 * c + 16], HW[:].indirect(LS[:, 16 * c + 16:16 * c + 17]), T.MS[:, s, 96 + 16 * c:112 + 16 * c], A.mult) for c in range(2)])
+        else:
+            V(64, ["MM", "R1"], ["SX" + H], scan(T.SX[:, s, :], T.R1[:], MM[:, 128:160], 0.0, A.mult, A.max))
+            V(64, ["SX" + H], ["LS" + H], cp(LS[:, 0:2], T.SX[:, s, 15:32:16]))
+            V(57 + 32 * GAT, ["LS" + H, "HW" + H, "CD" + H], ["DMs" + H], tt(T.DM[:, s, 0:32], HW[:].indirect(LS[:, 0:2]), T.MS[:, s, 96:128], A.mult))
+        V(64, ["NS" + H, xk], ["JU" + H], scan(T.JU[:, s, :], T.NS[:, s, :], X[:, 128:192], 0.0, A.mult, A.add))
+        V(64, ["JU" + H], ["JX" + H], ts(T.JX[:, s, :], T.JU[:, s, 1:64:2], 5, 4095, A.arith_shift_right, A.bitwise_and))
         V(64, ["JX" + H, "NS" + H], ["DFj" + H], tt(T.DF[:, s, 32:64], T.JX[:, s, :], JJ, A.subtract))
         V(64, ["DFj" + H, "MS" + H], ["DMj" + H], tt(T.DM[:, s, 32:64], T.DF[:, s, 32:64], T.MS[:, s, 64:96], A.mult))
         V(64, ["DMs" + H, "DMj" + H, xk], ["FO" + k], tt(T.FO[:, o, :], NP, T.DM[:, s, :], A.add))
@@ -637,8 +703,11 @@ def record(g, core, T, topo):
             else:
                 V(64, ["LO%s%d" % (H, x), "WD"], ["LX%s%d" % (H, x)], ts(lx, T.WD[:, 8:16], lo, None, A.mult))
             PE(64, ["LX%s%d" % (H, x), "BK"], ["MM"], [(VV, T.BK[:, x, :], lx, False, x == 3)])
-        V(64, ["MM", "EF" + H], ["OT" + H], tt(T.OT[:, s, :], VV, T.EF[:, s, :], A.max))
-        V(64, ["OT" + H], ["OF" + H], cp(OF[:], T.OT[:, s, :]))
+        if U16T:
+            V(64, ["MM", "EF" + H], ["OF" + H], tt(OF[:], VV, T.EF[:, s, :], A.max))
+        else:
+            V(64, ["MM", "EF" + H], ["OT" + H], tt(T.OT[:, s, :], VV, T.EF[:, s, :], A.max))
+            V(64, ["OT" + H], ["OF" + H], cp(OF[:], T.OT[:, s, :]))
         V(57 + 128 * SCA, ["OF" + H, "RN" + H], rk(s), cp(RO[:].indirect(OF[:]), T.RN[:, s, :]))
         if last:
             for a in range(2):
@@ -650,13 +719,13 @@ def record(g, core, T, topo):
                 dma("ys"[a * s], "od_x" + n, T.yx[rows(s), 2048 * a:2048 * a + 2048], RO[rows(a), 2048 * a:2048 * a + 2048], rk(s), ["ox" + n], 3.5)
 
     def count(t):
-        PE(128, ["MS0", "MS1", "S15"], ["HT"], [(HT[:, 256:288], T.S15[:], T.MS[:, s, 64:96], s == 0, s == 1) for s in range(2)])
-        V(64, ["HT"], ["CN"], lambda: v.tensor_reduce(T.CN[:, 0:1], HT[:, 256:288], AxisListType.X, A.add))
-        V(64, ["CN"], ["CI0"], cp(T.CI[:, 0:1], T.CN[:, 0:1]))
-        V(64, ["CI0"], ["CI1"], ts(T.CI[:, 1:2], T.CI[:, 0:1], 3, None, A.bitwise_and))
-        V(128, ["CI1", "LIM"], ["TOP%d" % (t + 1)], *[ts(T.TOP[:, s, t + 1:t + 2], T.CI[:, 1:2], T.LIM[:, s:s + 1], None, A.add) for s in range(2)])
+        PE(280 + 256, ["MS0", "MS1", "S15", "I32", "CN"], ["K0"], [(T.K0[:, 256:326], T.I32[:], T.CN[:, 0, :], True, False)] +
+           [(T.K0[:, 256 + 36 * x:288 + 36 * x], T.S15[:], T.MS[:, s, 64:96], False, s + x == 2) for s in range(2) for x in range(2)])
+        V(70, ["K0", "CN"], ["TOP%d" % (t + 1)], scan(T.TOP[:, t + 1, :], T.CN[:, 1, :], T.K0[:, 256:326], 0.0, A.mult, A.add))
 
     for t in range(NV):
+        S["st"] = "k"
+        earlier(t)
         for s in range(2):
             for f, n in ((claims, "c"), (moves, "m"), (choice, "s"), (meetings, "e")):
                 S["st"] = n + str(s)

@@ -2,9 +2,6 @@ from concourse.mybir import AluOpType as A, ActivationFunctionType as AF, AxisLi
 
 NV = 5
 NG = 32
-U16S = True
-U16B = False
-U16T = True
 SCRATCH = {
     "PI": ("sbuf", [128, 8], "int32"), "RF": ("sbuf", [128, 16], "float32"),
     "ONES": ("sbuf", [128, 128], "bfloat16"), "NEG": ("sbuf", [128, 128], "bfloat16"), "IB": ("sbuf", [128, 128], "bfloat16"),
@@ -18,24 +15,25 @@ SCRATCH = {
     "SCM": ("sbuf", [128, 4, 128], "bfloat16"), "L3": ("sbuf", [128, 128], "bfloat16"), "R3": ("sbuf", [128, 512], "bfloat16"),
     "WD": ("sbuf", [128, 16], "bfloat16"), "CM": ("sbuf", [128, 256], "bfloat16"), "RS": ("sbuf", [128, 128], "bfloat16"),
     "XK": ("sbuf", [128, 144], "bfloat16"), "RK": ("sbuf", [128, 2, 144], "bfloat16"), "NIB": ("sbuf", [128, 128], "bfloat16"),
-    "R1": ("sbuf", [128, 32], "bfloat16"), "CJ": ("sbuf", [128, 32], "bfloat16"),
+    "R1": ("sbuf", [128, 64], "bfloat16"), "CJ": ("sbuf", [128, 32], "bfloat16"),
     "EL": ("sbuf", [128, 16, 128], "bfloat16"), "PL": ("sbuf", [128, 16, 128], "bfloat16"), "CS": ("sbuf", [128, 16, 128], "bfloat16"),
     "SLB": ("sbuf", [128, 128], "bfloat16"), "QQ": ("sbuf", [128, 3, 128], "bfloat16"), "WX": ("sbuf", [128, 3, 128], "bfloat16"),
     "S15": ("sbuf", [128, 128], "bfloat16"), "I32B": ("sbuf", [128, 128], "bfloat16"), "HB": ("sbuf", [128, 3, 128], "bfloat16"),
-    "SEL": ("sbuf", [128, 4, 128], "bfloat16"), "GS": ("sbuf", [128, 8, 128], "bfloat16"), "BK": ("sbuf", [128, 4, 128], "bfloat16"),
+    "SEL": ("sbuf", [128, 6, 128], "bfloat16"), "GS": ("sbuf", [128, 8, 128], "bfloat16"), "BK": ("sbuf", [128, 4, 128], "bfloat16"),
     "CL": ("sbuf", [128, NV, 128], "bfloat16"), "MK": ("sbuf", [128, NV, 128], "bfloat16"), "DUMP": ("sbuf", [128, 8], "float32"),
-    "QR": ("sbuf", [128, 128], "bfloat16"), "QS": ("sbuf", [128, 64], "bfloat16"),
+    "QR": ("sbuf", [128, 192], "bfloat16"), "QS": ("sbuf", [128, 64], "bfloat16"),
     "WI": ("sbuf", [128, 2], "int32"), "WL": ("sbuf", [128, 2], "bfloat16"), "W2": ("sbuf", [128, 2, 128], "bfloat16"),
-    "LIM": ("sbuf", [128, 2], "float32"), "TOP": ("sbuf", [128, NV, 70], "float32"), "CN": ("sbuf", [128, 2, 70], "float32"),
+    "LIM": ("sbuf", [128, 2], "float32"), "TOP": ("sbuf", [128, NV, 72], "bfloat16"), "CN": ("sbuf", [128, 2, 72], "float32"),
+    "BQ": ("sbuf", [128, 128], "bfloat16"), "CK": ("sbuf", [128, 64], "bfloat16"),
     "FI": ("sbuf", [128, 2, 64], "int32"),
     "F": ("sbuf", [128, 2 * NV, 64], "float16"), "FO": ("sbuf", [128, 2 * NV, 64], "float16"),
     "Z": ("sbuf", [128, 2 * NV, 64], "bfloat16"), "ZO": ("sbuf", [128, 2 * NV, 64], "bfloat16"),
     "YF": ("sbuf", [128, 2, 64], "float32"), "YZ": ("sbuf", [128, 2, 64], "bfloat16"),
 }
-for _n, _w, _d in (("UA", 64, "int32"), ("UI", 512, "float32"), ("SI", 64, "int32"), ("HM", 512, "int32"),
+for _n, _w, _d in (("UA", 64, "float32"), ("UI", 512, "float32"), ("Z5", 64, "float32"), ("SU", 64, "float16"), ("HM", 512, "int32"),
                    ("C4", 256, "int32"), ("UF", 32, "float32"), ("Z4", 64, "bfloat16"), ("KE", 128, "float32"),
-                   ("KS", 256, "int32"), ("KC", 64, "int32"), ("NB", 64, "int32"), ("PR", 320, "float32"), ("HF", 64, "float16"),
-                   ("JC", 64, "float16"), ("NS", 64, "float32"), ("EQB", 512, "bfloat16"), ("PM", 32, "bfloat16"),
+                   ("KS", 256, "int32"), ("KC", 64, "int32"), ("NB", 64, "int32"), ("PR", 320, "float32"), ("HF", 96, "float16"),
+                   ("JC", 64, "float16"), ("NS", 64, "float32"), ("EQB", 512, "bfloat16"), ("PM", 64, "bfloat16"),
                    ("MS", 128, "bfloat16"), ("SX", 32, "float32"), ("JU", 64, "int32"), ("JX", 32, "int32"),
                    ("DF", 64, "float32"), ("DM", 64, "float32"), ("MF", 128, "float16"), ("EF", 8, "float32"), ("YA", 128, "bfloat16"),
                    ("LO", 4, "float32"), ("LX", 32, "bfloat16"), ("OT", 8, "float32"), ("RN", 128, "bfloat16"),
@@ -43,7 +41,7 @@ for _n, _w, _d in (("UA", 64, "int32"), ("UI", 512, "float32"), ("SI", 64, "int3
     SCRATCH[_n] = ("sbuf", [128, 2, _w], _d)
 for _s in "01":
     for _n, _w, _d in (("ROCK", 4096 + 128, "bfloat16"), ("CO", 256, "uint16"), ("ZX", 16 * NG, "bfloat16"), ("HW", 512, "float32"),
-                       ("LS", 34, "uint16"), ("E16", 8, "uint16"), ("OF", 8, "uint16")):
+                       ("LS", 34, "uint16"), ("EO", 66, "uint16"), ("E16", 8, "uint16"), ("OF", 8, "uint16")):
         SCRATCH[_n + _s] = ("sbuf", [128, _w], _d)
 BANKS = ["X0", "X1", "K0", "K1", "KX", "EQ", "HT", "MM"]
 for _n in BANKS:
@@ -61,17 +59,20 @@ DML = 1.8
 GAT = 1.56
 SCA = 3.8
 SFIX = 70
-BIAS = {}
+BIAS = {'e0': 3.25, 'c1': 1.5, 'cvUA': -2, 'stX1': 2, 'etEQ': -1, 'e1': 1.5, 'msD0': 0.25, 'ctX0': 2, 'evDM': 0.25, 'itMM': 0.5,
+        'mvKS': -0.25, 'isRN': 0.25, 'evLS': -0.5, 'cvCO': 0.5, 'ivE1': -0.5, 'i1': 0.25, 'ivLX': 0.25}
 SGRP = 2
 VP = 2
-LOOK = 0.4
-ROUNDS = 3
-KS = ("EL", "HB", "U1")
-ZS = 10
-ZV = 0
-ABS = (10, 11, 13, 14)
+LOOK = 0.3
+ROUNDS = 2
+SWAPS = 0
+TABOO = 30
+KS = ("GS", "WX", "U0", "U1")
+ZS = 12
+ZV = 2
+ABS = (10, 10, 11, 12)
 NPC = 256
-OPT = {"lx": "v", "rn": "s", "ya": "v", "ke": "s", "ef": "v", "z4": "v"}
+OPT = {"lx": "v", "rn": "s", "hf": "2", "ke": "s", "z4": "s", "z5": "s", "nb": "HT"}
 PLANS = {}
 
 
@@ -128,7 +129,7 @@ def plan(S):
         for k in succ[i]:
             b = max(b, pri[k] + (o["lat"] if o["sig"] else (LAT if ops[k]["deps"][i] else 0.0)))
         pri[i] = b + o["cost"]
-    pri = [p + BIAS.get(o["st"][:1] + o["q"] + o["nm"][:2], 0.0) for p, o in zip(pri, ops)]
+    pri = [p + BIAS.get(o["st"][:1] + o["q"] + o["nm"][:2], 0.0) + BIAS.get(o["st"], 0.0) for p, o in zip(pri, ops)]
     left = [len(o["deps"]) for o in ops]
     ready = {}
     est = [0.0] * n
@@ -185,9 +186,84 @@ def plan(S):
         if end < best[0]:
             best = (end, start)
     S["end"], start = best
+    if SWAPS:
+        S["end"], start = polish(ops, sorted(range(n), key=lambda i: start[i]), pred, after)
     for s, o in zip(start, ops):
         o["start"] = s
     return sorted(range(n), key=lambda i: start[i])
+
+
+def polish(ops, order, pred, after):
+    n = len(ops)
+    cost = [o["cost"] for o in ops]
+    last = [o["lat"] for o in ops]
+    prev, nxt, tail_of = [-1] * n, [-1] * n, {}
+    for i in order:
+        j = tail_of.get(ops[i]["q"], -1)
+        prev[i] = j
+        if j >= 0:
+            nxt[j] = i
+        tail_of[ops[i]["q"]] = i
+    best, taboo = None, {}
+    for it in range(SWAPS):
+        head, tail = [0.0] * n, [0.0] * n
+        for i in order:
+            j = prev[i]
+            t = head[j] + cost[j] if j >= 0 else 0.0
+            for j, l in pred[i]:
+                x = head[j] + cost[j] + l
+                if x > t:
+                    t = x
+            head[i] = t
+        end = 0.0
+        for i in reversed(order):
+            j = nxt[i]
+            t = tail[j] if j >= 0 else 0.0
+            if last[i] > t:
+                t = last[i]
+            for j, l in after[i]:
+                x = tail[j] + l
+                if x > t:
+                    t = x
+            tail[i] = t + cost[i]
+            if t + cost[i] > end:
+                end = t + cost[i]
+        if best is None or end < best[0] - 1e-9:
+            best = (end, head)
+        pick = None
+        for u in order:
+            v = nxt[u]
+            if v < 0 or head[u] + tail[u] < end - 1e-9 or head[u] + cost[u] + tail[v] < end - 1e-9 or u in ops[v]["deps"]:
+                continue
+            p, s = prev[u], nxt[v]
+            hv = max([head[p] + cost[p] if p >= 0 else 0.0] + [head[j] + cost[j] + l for j, l in pred[v]])
+            hu = max([hv + cost[v]] + [head[j] + cost[j] + l for j, l in pred[u]])
+            tu = cost[u] + max([tail[s] if s >= 0 else 0.0, last[u]] + [tail[j] + l for j, l in after[u]])
+            tv = cost[v] + max([tu, last[v]] + [tail[j] + l for j, l in after[v]])
+            e = max(hv + tv, hu + tu)
+            if taboo.get((v, u), -1) >= it and e >= best[0] - 1e-9:
+                continue
+            if pick is None or e < pick[0]:
+                pick = (e, u, v)
+        if pick is None:
+            break
+        _, u, v = pick
+        taboo[(u, v)] = it + TABOO
+        p, s = prev[u], nxt[v]
+        prev[v], nxt[v], prev[u], nxt[u] = p, u, v, s
+        if p >= 0:
+            nxt[p] = v
+        if s >= 0:
+            prev[s] = u
+        a, b = order.index(u), order.index(v)
+        behind, ahead = {u}, []
+        for i in order[a + 1:b]:
+            if prev[i] in behind or any(j in behind for j, l in pred[i]):
+                behind.add(i)
+            else:
+                ahead.append(i)
+        order[a:b + 1] = ahead + [v] + [i for i in order[a:b] if i in behind]
+    return best
 
 
 def place(ops, rank, pred, first):
@@ -312,7 +388,7 @@ def record(g, core, T, topo):
         for a in range(2):
             n = "%d%d" % (s, a)
             dma("y", "ld_f" + n, T.FI[rows(a), s, :], T.front[rows(s), rows(a)], [], ["FI" + n], 2.2)
-            dma("s", "ld_v" + n, T.Z[rows(a), s, :], T.vein[rows(s), rows(a)], [], ["Zl" + n], 2.2)
+            dma("s", "ld_v" + n, T.YZ[rows(a), s, :], T.vein[rows(s), rows(a)], [], ["Zl" + n], 2.2)
         if s == 0:
             dma("s", "ld_wi", T.WI[:, 0:1], T.w[:], [], ["WI0"], 2.2)
             dma("s", "ld_li", T.WI[:, 1:2], T.lim[:], [], ["WI1"], 2.2)
@@ -335,24 +411,27 @@ def record(g, core, T, topo):
     G(128, ["ONES"], ["IB"], sel(T.IB[:], T.ONES[:], [[-1, 128]], A.is_equal, 0.0, 0, 1))
     for a in range(2):
         G(128, ["ONES"], ["SEL%d" % a], sel(T.SEL[:, a, :], T.ONES[:], [[0, 2], [-1, 64]], A.is_equal, 0.0, -64 * a, 1))
-        V(64, ["SEL%d" % a], ["NSEL%d" % a], ts(T.SEL[:, 2 + a, :], T.SEL[:, a, :], -1.0, None, A.mult))
+        scaled("SE", ["SEL%d" % a], ["NSEL%d" % a], (T.SEL[:, 2 + a, :], T.SEL[:, a, :], -1.0), (T.SEL[:, 4 + a, :], T.SEL[:, a, :], -0.5))
     V(64, ["PI"], ["PIr"], ts(T.PI[:, 1:2], T.PI[:, 0:1], 15, None, A.bitwise_and))
     V(64, ["PI"], ["PIg"], ts(T.PI[:, 2:3], T.PI[:, 0:1], 4, None, A.arith_shift_right))
     V(64, ["PI"], ["PIm"], ts(T.PI[:, 3:4], T.PI[:, 0:1], 4, 3, A.arith_shift_right, A.bitwise_and))
-    V(64, ["PI"], ["PIa"], ts(T.PI[:, 4:5], T.PI[:, 0:1], 6, None, A.arith_shift_right))
-    V(64, ["PIr", "PIg", "PIm", "PIa"], ["r"], cp(T.RF[:, 0:4], T.PI[:, 1:5]))
-    r, gp, mi, ha = T.RF[:, 0:1], T.RF[:, 1:2], T.RF[:, 2:3], T.RF[:, 3:4]
+    V(64, ["PIr", "PIg", "PIm"], ["r"], cp(T.RF[:, 0:3], T.PI[:, 1:4]))
+    r, gp, mi = T.RF[:, 0:1], T.RF[:, 1:2], T.RF[:, 2:3]
     V(64, ["GR", "r"], ["BLK"], ts(T.BLK[:], T.GR[:], gp, None, A.is_equal))
     V(64, ["WI0", "WI1"], ["WL"], cp(T.WL[:], T.WI[:]))
     PE(128, ["WL", "SEL0", "SEL1"], ["MM"], [(T.MM[:, 2 * s:2 * s + 2], T.SEL[:, s, :], T.WL[:], True, True) for s in range(2)])
     for s in range(2):
-        V(64, ["MM", "BLK"], ["W2%d" % s], ts(T.W2[:, s, :], T.BLK[:], T.MM[:, 2 * s:2 * s + 1], 2.0, A.mult, A.mult))
-    V(64, ["MM"], ["LIM"], ts(T.LIM[:], T.MM[:, 1:4:2], 0.5, None, A.add))
-    V(64, ["LIM"], ["TOP0"], cp(T.TOP[:, 0, 68:70], T.LIM[:]))
-    V(140, [], ["CNz"], ms(T.CN[:, 0, :], 0.0), ms(T.CN[:, 1, :], 1.0))
-    V(64, ["CNz", "LIM"], ["CN"], cp(T.CN[:, 0, 68:69], T.LIM[:, 0:1]), tt(T.CN[:, 0, 69:70], T.LIM[:, 1:2], T.LIM[:, 0:1], A.subtract),
-      *[ms(T.CN[:, x, c:c + 1], y) for x, c, y in ((0, 32, -0.375), (0, 33, 1.5 * 2 ** 23), (0, 34, -1.5 * 2 ** 23), (1, 32, 0.25), (1, 35, -4.0))])
+        V(64, ["MM", "BLK"], ["W2%d" % s], ts(T.W2[:, s, :], T.BLK[:], T.MM[:, 2 * s:2 * s + 1], None, A.mult))
+    V(64, ["MM"], ["LIM"], ts(T.LIM[:], T.MM[:, 1:4:2], 1.0, None, A.add))
+    V(128, ["LIM"], ["TOP0"], cp(T.TOP[:, 0, 68:72:2], T.LIM[:]), ts(T.TOP[:, 0, 69:72:2], T.LIM[:], 2.0, None, A.mult))
+    V(144, [], ["CNz"], ms(T.CN[:, 0, :], 0.0), ms(T.CN[:, 1, :], 1.0))
+    V(64, ["CNz", "LIM"], ["CN"], cp(T.CN[:, 0, 68:69], T.LIM[:, 0:1]), tt(T.CN[:, 0, 70:71], T.LIM[:, 1:2], T.LIM[:, 0:1], A.subtract),
+      *[ms(T.CN[:, x, c:d:2], y) for x, c, d, y in ((0, 32, 33, -0.375), (0, 33, 34, 1.5 * 2 ** 23), (0, 34, 35, -1.5 * 2 ** 23), (1, 32, 33, 0.25),
+                                                    (1, 35, 36, -4.0), (1, 69, 72, 2.0), (1, 70, 71, 0.5))])
+    V(64, ["BLK"], ["BQ"], ts(T.BQ[:], T.BLK[:], 1.0 / 32, None, A.mult))
     for s in range(2):
+        V(64, ["Zl%d0" % s, "Zl%d1" % s], ["Z0%d" % s], ts(T.Z[:, s, :], T.YZ[:, s, :], 2.0, None, A.mult))
+        V(64, ["ONES"], ["MF%d" % s], ts(T.MF[:, s, :], T.ONES[:], 0.0, None, A.mult))
         V(64, ["FI%d0" % s, "FI%d1" % s], ["F0%d" % s], ts(T.F[:, s, :], T.FI[:, s, :], -2048.0, None, A.add))
     pw = [32, 32, 64, 128]
     for m in range(4):
@@ -374,10 +453,6 @@ def record(g, core, T, topo):
     for row, col, x in ((32, 0, -2048.0), (64, 0, 1.0), (32, 1, 1.5 * 2 ** 23), (32, 2, -1.5 * 2 ** 23), (32, 3, 1.0)):
         fills.append(ms(T.R3[row:row + 1, col:512:8], x))
     V(64, ["R3z"], ["R3"], *fills)
-    V(64, ["PIr"], ["PIs"], ts(T.PI[:, 5:6], T.PI[:, 1:2], 1.0, None, A.add))
-    V(64, ["PIs"], ["PIt"], ts(T.PI[:, 6:7], T.PI[:, 5:6], 15, None, A.bitwise_and))
-    V(64, ["r"], ["h100"], ts(T.RF[:, 4:5], ha, 100.0, None, A.mult), ts(T.RF[:, 5:6], ha, -100.0, 100.0, A.mult, A.add))
-    V(128, ["PIt", "h100"], ["rp1"], *[ts(T.RF[:, 6 + a:7 + a], T.PI[:, 6:7], T.RF[:, 4 + a:5 + a], None, A.add) for a in range(2)])
     V(128, ["BLK"], ["WD"], ts(T.WD[:, 0:8], T.BLK[:, 0:128:16], 256.0, None, A.mult), cp(T.WD[:, 8:16], T.BLK[:, 0:128:16]))
     G(128, [], ["CM"], ioF(T.CM[0:1, 0:4 * NG], [[64, 4], [0, NG]], 23, 0), ioF(T.CM[0:1, 4 * NG:256], [[0, 64 - NG], [64, 4]], 23, 0))
     G(NG, ["ONE32"], ["PERM"], *([sel(T.PERM[:, m:4 * NG:4], T.ONE32[:, 0:NG], [[-1, NG]], A.is_equal, 0.0, -NG * m, 1) for m in range(4)] +
@@ -388,7 +463,7 @@ def record(g, core, T, topo):
     V(64, ["RSz"], ["RS"], ms(T.RS[:, 0:128:4], float(2 ** 22)))
     G(144, [], ["XK"], ioF(T.XK[:], [[1, 144]], -15, 0))
     V(64, ["r"], ["g16"], ts(T.RF[:, 13:14], gp, 16.0, None, A.mult))
-    V(144, ["XK", "g16"], ["RK"], *[ts(T.RK[:, x, :], T.XK[:], T.RF[:, 13:14], (256.0, 1.0)[x], A.is_equal, A.mult) for x in range(2)])
+    V(144, ["XK", "g16"], ["RK"], *[ts(T.RK[:, x, :], T.XK[:], T.RF[:, 13:14], (128.0, 1.0)[x], A.is_equal, A.mult) for x in range(2)])
     for s in range(2):
         if "U%d" % s in KS:
             G(512, [], ["UIa%d" % s], ioF(T.UI[:, s, :], [[0, 512]], 1, 0))
@@ -417,7 +492,9 @@ def record(g, core, T, topo):
     G(32, [], ["T4j"], ioF(T.T4[:, 0:32], [[1, 32]], 0, 0))
     V(64, ["CR", "r"], ["T3"], ts(T.T3[:, 0:32], T.CR[:, 0:32], r, -2048.0, A.not_equal, A.mult))
     V(64, ["T3", "T4j"], ["CJ"], tt(T.CJ[:], T.T3[:, 0:32], T.T4[:, 0:32], A.add))
-    V(64, ["CR"], ["R1"], ts(T.R1[:], T.CR[:, 0:32], 0.0, None, A.is_gt))
+    V(64, ["CR"], ["R1"], ts(T.R1[:], T.CR[:, 0:64], 0.0, None, A.is_gt))
+    V(64, ["CR", "r"], ["CKa"], ts(T.CK[:], T.CR[:, 0:64], r, -8192.0, A.not_equal, A.mult))
+    V(64, ["CKa"], ["CK"], ts(T.CK[:], T.CK[:], 2048.0, None, A.add))
     G(128, [], ["TI"], ioI(T.TI[:], [[-1, 128]], 128, 1))
     V(128, ["TI"], ["TI"], ts(T.TI[:], T.TI[:], 15, None, A.bitwise_and))
     V(64, ["BLK"], ["T3"], ts(T.T3[:], T.BLK[:], -100.0, 100.0, A.mult, A.add))
@@ -425,16 +502,13 @@ def record(g, core, T, topo):
     for l in range(0, 16, 4):
         V(256, ["T4"], ["CS%d" % l], *[ts(T.CS[:, x, :], T.T4[:], float((x + 1) % 16), None, A.is_equal) for x in range(l, l + 4)])
     V(64, ["IB"], ["I32B"], ts(T.I32B[:], T.IB[:], 32.0, None, A.mult))
-    V(64, ["ONES", "KT"], ["S15"], ts(T.S15[:], T.ONES[:], T.KT[:, 15:16], None, A.mult))
     V(64, [], ["XRz"], ms(T.XR[:], -1.0))
     G(128, ["XRz"], ["XR"], ioF(T.XR[:, 15:143], [[0, 2], [1, 64]], 0, 0))
     V(64, ["r"], ["m16"], ts(T.RF[:, 9:10], mi, 16.0, None, A.mult))
     V(72, ["XR", "m16"], ["RW"], ts(T.RW[:], T.XR[:], T.RF[:, 9:10], None, A.is_equal))
-    V(128, ["r"], ["hh"], ts(T.RF[:, 10:11], ha, -0.5, 0.5, A.mult, A.add), ts(T.RF[:, 11:12], ha, 0.5, None, A.mult))
-    scaled("HB", ["IB", "hh"], ["HB"], (T.HB[:, 0, :], T.IB[:], T.RF[:, 10:11]), (T.HB[:, 1, :], T.IB[:], T.RF[:, 11:12]), (T.HB[:, 2, :], T.IB[:], 0.5))
-    V(128, [], ["QR"], ms(T.QR[0:1, :], -0.25), ms(T.QR[32:33, :], 2048.0))
-    V(64, [], ["QSz"], ms(T.QS[32:33, :], 0.0))
-    V(64, ["QSz"], ["QS"], ms(T.QS[32:33, 0:64:2], 1.0))
+    V(128, [], ["QR"], ms(T.QR[0:1, 128:192], -1.0 / 16), ms(T.QR[0:1, 0:128], 2048.0))
+    V(64, [], ["QSz"], ms(T.QS[0:1, :], 0.0))
+    V(64, ["QSz"], ["QS"], ms(T.QS[0:1, 0:64:2], 1.0))
     V(256, ["r"], ["KM"], *[ts(T.KH[:, 4 + x:5 + x], mi, float(x), None, A.is_equal) for x in range(4)])
     for x in range(4):
         scaled("GS", ["ONES", "NEG", "KM"], ["GS%d" % x], (T.GS[:, x, :], T.ONES[:], T.KH[:, 4 + x:5 + x]), (T.GS[:, 4 + x, :], T.NEG[:], T.KH[:, 4 + x:5 + x]))
@@ -444,7 +518,7 @@ def record(g, core, T, topo):
     V(256, ["G4"], ["BK"], *[ts(T.BK[:, x, :], T.G4[:], float(x), 8192.0, A.is_equal, A.mult) for x in range(4)])
     G(8, [], ["DUMPa"], ioF(T.DUMP[:], [[16, 8]], 4096, 0))
     V(64, ["DUMPa", "r"], ["DUMP"], ts(T.DUMP[:], T.DUMP[:], r, None, A.add))
-    V(64, [], ["b128"], ms(T.RF[:, 12:13], 129.0))
+    V(64, [], ["b128"], ms(T.RF[:, 12:13], 129.5))
     S["st"] = ""
 
     def earlier(t):
@@ -458,7 +532,7 @@ def record(g, core, T, topo):
     IB = T.IB[:]
 
     def zk(t, s):
-        return ["Zl%d0" % s, "Zl%d1" % s] if t == 0 else ["Z%d%d" % (t, s)]
+        return ["Z%d%d" % (t, s)]
 
     def rk(s):
         return ["ROCK%d0" % s, "ROCK%d1" % s]
@@ -472,7 +546,7 @@ def record(g, core, T, topo):
         k, H, xk = "%d%d" % (t, s), str(s), "X%d" % s
         o = 2 * t + s
         X, CO, ZX = T[xk], T["CO" + H], T["ZX" + H]
-        nodes = [(X[:, 384:448], T.QR[32:33, :], T.ONES[32:33, 0:64], True, False)] + [(X[:, 384 + 32 * b:416 + 32 * b], IB, T.F[:, o, b:64:2], False, b == 1) for b in range(2)]
+        nodes = [(X[:, 384:448], T.QR[0:1, 0:128], T.ONES[0:1, 0:64], True, False)] + [(X[:, 384 + 32 * b:416 + 32 * b], IB, T.F[:, o, b:64:2], False, b == 1) for b in range(2)]
         PE(192, ["F" + k, "QR", "ONES", "IB"], [xk], nodes)
         SC(64, [xk], ["UI" + H], ac(T.UI[:, s, 4:512:8], X[:, 384:448], AF.Copy))
         mm = [(X[:], T.L3[0:97, :], T.R3[0:97, :], True, False)]
@@ -484,30 +558,29 @@ def record(g, core, T, topo):
         V(512, [xk, "UI" + H], ["HM" + H], scan(T.HM[:, s, :], T.UI[:, s, :], X[:], 0.0, A.mult, A.add))
         for m in range(4):
             V(64, ["HM" + H], ["C4%s%d" % (H, m)], ts(T.C4[:, s, m:256:4], T.HM[:, s, 4 + m:512:8], 5 + m, 4095, A.arith_shift_right, A.bitwise_and))
-        PE(192 + 128, ["F" + k, "QR", "ONES", "IB", "BLK"] + zk(t, s), [xk], nodes + [(X[:, 192 + 32 * b:224 + 32 * b], T.BLK[:], T.Z[:, o, b:64:2], True, True) for b in range(2)])
-        V(64, [xk], ["UA" + H], ts(T.UA[:, s, :], X[:, 192:256], 1.0, None, A.add))
-        if U16B:
-            V(256, ["HM" + H], ["COs" + H], *[ts(CO[:, 4 * NG + m:256:4], T.HM[:, s, 8 * NG + 4 + m:512:8], 5 + m, 4095, A.arith_shift_right, A.bitwise_and) for m in range(4)])
-            for m in range(4):
-                V(64, ["HM" + H], ["COv%s%d" % (H, m)], ts(CO[:, NG * m:NG * m + NG], T.HM[:, s, 4 + m:8 * NG:8], 5 + m, 4095, A.arith_shift_right, A.bitwise_and))
-        else:
-            V(256 - 4 * NG, ["C4%s%d" % (H, m) for m in range(4)], ["COs" + H], cp(CO[:, 4 * NG:256], T.C4[:, s, 4 * NG:256]))
-            for m in range(4):
-                V(64, ["C4%s%d" % (H, m)], ["COv%s%d" % (H, m)], cp(CO[:, NG * m:NG * m + NG], T.C4[:, s, m:4 * NG:4]))
+        PE(192 + 192, ["F" + k, "QR", "ONES", "IB", "BQ", "L3"] + zk(t, s), [xk], nodes + [(X[:, 192:256], T.L3[0:1, :], T.QR[0:1, 128:192], True, False)] +
+           [(X[:, 192 + 32 * b:224 + 32 * b], T.BQ[:], T.Z[:, o, b:64:2], False, b == 1) for b in range(2)])
+        V(256 - 4 * NG, ["C4%s%d" % (H, m) for m in range(4)], ["COs" + H], cp(CO[:, 4 * NG:256], T.C4[:, s, 4 * NG:256]))
+        for m in range(4):
+            V(64, ["C4%s%d" % (H, m)], ["COv%s%d" % (H, m)], cp(CO[:, NG * m:NG * m + NG], T.C4[:, s, m:4 * NG:4]))
         for p in range(16):
             if p < ZV:
-                V(64, zk(t, s), ["ZX%s%d" % (H, p)], cp(ZX[:, p:16 * NG:16], T.Z[:, o, 0:2 * NG:2]))
+                V(64, zk(t, s), ["ZX%s%d" % (H, p)], ts(ZX[:, p:16 * NG:16], T.Z[:, o, 0:2 * NG:2], 0.5, None, A.mult))
             elif p < ZV + ZS:
-                SC(NG, zk(t, s), ["ZX%s%d" % (H, p)], ac(ZX[:, p:16 * NG:16], T.Z[:, o, 0:2 * NG:2], AF.Copy))
+                SC(NG, zk(t, s), ["ZX%s%d" % (H, p)], ac(ZX[:, p:16 * NG:16], T.Z[:, o, 0:2 * NG:2], AF.Copy, scale=0.5))
             else:
-                G(NG, zk(t, s), ["ZX%s%d" % (H, p)], sel(ZX[:, p:16 * NG:16], T.Z[:, o, 0:2 * NG:2], [[0, NG]], A.is_ge, 0.0, 0, 0))
-        V(64, ["UA" + H], ["SI" + H], ts(T.SI[:, s, :], T.UA[:, s, :], 15, None, A.bitwise_and))
+                G(NG, ["ZX%s%d" % (H, p % 2)], ["ZX%s%d" % (H, p)], sel(ZX[:, p:16 * NG:16], ZX[:, p % 2:16 * NG:16], [[0, NG]], A.is_ge, 0.0, 0, 0))
+        V(64, [xk], ["UA" + H], ts(T.UA[:, s, :], X[:, 192:256], 1.5 * 2 ** 23, 1.5 * 2 ** 23, A.add, A.subtract))
+        V(64, [xk, "UA" + H], [xk, "SM" + H], tt(X[:, 0:64], X[:, 192:256], T.UA[:, s, :], A.is_equal))
         V(64, ["HM" + H], ["UF" + H], ts(T.UF[:, s, :], T.HM[:, s, 259:512:8], 16.0, 65536.0 - 16 - 2 ** 18, A.mult, A.add))
-        V(128, ["SI" + H, "rp1"], [xk, "SM" + H], *[ts(X[:, 64 * a:64 * a + 64], T.SI[:, s, :], T.RF[:, 6 + a:7 + a], None, A.is_equal) for a in range(2)])
         if OPT["z4"] == "s":
-            SC(64, zk(t, s), ["Z4" + H], ac(T.Z4[:, s, :], T.Z[:, o, :], AF.Copy, scale=0.25, bias=129 - 0.375))
+            SC(64, zk(t, s), ["Z4" + H], ac(T.Z4[:, s, :], T.Z[:, o, :], AF.Copy, scale=0.125, bias=129 - 0.375))
         else:
-            V(64, zk(t, s), ["Z4" + H], ts(T.Z4[:, s, :], T.Z[:, o, :], 0.25, 129 - 0.375, A.mult, A.add))
+            V(64, zk(t, s), ["Z4" + H], ts(T.Z4[:, s, :], T.Z[:, o, :], 0.125, 129 - 0.375, A.mult, A.add))
+        if OPT["z5"] == "s":
+            SC(64, zk(t, s), ["Z5" + H], *[ac(T.Z5[:, s, 32 * b:32 * b + 32], T.Z[:, o, b:64:2], AF.Copy, scale=0.5, bias=-0.5) for b in range(2)])
+        else:
+            V(64, zk(t, s), ["Z5" + H], *[ts(T.Z5[:, s, 32 * b:32 * b + 32], T.Z[:, o, b:64:2], 0.5, -0.5, A.mult, A.add) for b in range(2)])
 
     def moves(t, s):
         H = str(s)
@@ -520,7 +593,7 @@ def record(g, core, T, topo):
             run.append(len(S["ops"]))
             for c in range(c0, c0 + SGRP):
                 z = 2 * c if c < 32 else 2 * (c - 32) + 1
-                calls.append(ac(T.D[:, s, 64 * c:64 * c + 64], RO[:, 0:4096].indirect(CO[:, 4 * c:4 * c + 4]), AF.Abs, bias=T.Z[:, o, z:z + 1], scale=-1.0))
+                calls.append(ac(T.D[:, s, 64 * c:64 * c + 64], RO[:, 0:4096].indirect(CO[:, 4 * c:4 * c + 4]), AF.Abs, bias=T.Z[:, o, z:z + 1], scale=-2.0))
             SC(SGRP * (64 * GAT + 5), rk(s) + zk(t, s) + ["COs" + H], ["D%s_%d" % (H, c) for c in range(c0, c0 + SGRP)], *calls)
         for m in range(4):
             dm = T.D[:, s, 16 * NG * m:16 * NG * (m + 1)]
@@ -543,7 +616,7 @@ def record(g, core, T, topo):
         cuts = {0: [16 * NG * m for m in range(5)] + ([2048] if NG < 32 else []), 1: list(range(2048, 4097, NPC))}
         for ch in (0, 1):
             for a, b in zip(cuts[ch][:-1], cuts[ch][1:]):
-                V((b - a) // 2, parts(a, b) + ["TOP%d" % t], ["N%s_%d" % (H, a)], ts(T.NR[:, s, a:b], T.D[:, s, a:b], T.TOP[:, t, 68 + s:69 + s], None, A.is_le))
+                V((b - a) // 2, parts(a, b) + ["TOP%d" % t], ["N%s_%d" % (H, a)], ts(T.NR[:, s, a:b], T.D[:, s, a:b], T.TOP[:, t, 68 + 2 * s + (a >= 64 * NG):69 + 2 * s + (a >= 64 * NG)], None, A.is_lt))
         K0, K1 = T.K0, T.K1
         for p0 in range(0, 16, 4):
             PE(256 + 128 * (p0 == 0), parts(0, 2048) + ["WD", "CM", "ONES"], ["K0"], [(K0[:, 0:128], T.CM[0:1, 0:128], T.ONES[0:1, :], True, False)][:p0 == 0] +
@@ -594,16 +667,21 @@ def record(g, core, T, topo):
         NP = X[:, 448:512]
         HW, LS = T["HW" + H], T["LS" + H]
         JJ = T.NS[:, s, 1:64:2]
-        V(64, [xk], ["HF" + H], ts(T.HF[:, s, :], NP, 0.125, 1281 - 0.4375, A.mult, A.add))
+        V(64, [xk], ["HF" + H], ts(T.HF[:, s, 0:64], NP, 0.125, 1281 - 0.4375, A.mult, A.add))
+        if OPT["hf"] == "2":
+            V(64, [xk], ["HG" + H], ts(T.HF[:, s, 64:96], X[:, 480:512], 0.125, 1281 - 0.4375, A.mult, A.add))
         V(64, [xk], ["JC" + H], cp(T.JC[:, s, :], NP))
         SC(32, [xk], ["NS" + H], ac(JJ, X[:, 480:512], AF.Copy, bias=2048.0))
         for b, bk in ((0, "EQ"), (1, "KX")):
             mm = []
             for l in range(8):
                 dd = T[bk][:, 32 * l:32 * l + 32]
-                mm.append((dd, IB, T.HF[:, s, 32:64], True, False))
-                mm.append((dd, T.EL[:, 8 * b + l, :], T.HF[:, s, 0:32], False, True))
-            PE(16 * 64, ["HF" + H, "IB", "EL%d" % (8 * b), "EL%d" % (8 * b + 4)], [bk], mm)
+                if OPT["hf"] != "2":
+                    mm.append((dd, IB, T.HF[:, s, 32:64], True, False))
+                elif l % 2 == 0:
+                    mm.append((T[bk][:, 32 * l:32 * l + 64], IB, T.HF[:, s, 32:96], True, False))
+                mm.append((dd, T.EL[:, 8 * b + l, :], T.HF[:, s, 0:32], False, OPT["hf"] != "2" or l % 2 == 1))
+            PE(len(mm) * 64, ["HF" + H, "IB", "EL%d" % (8 * b), "EL%d" % (8 * b + 4)] + ["HG" + H][:OPT["hf"] == "2"], [bk], mm)
             V(256, [bk], ["EQB%s%d" % (H, b)], ts(T.EQB[:, s, 256 * b:256 * b + 256], T[bk][:, 0:256], 0.0, None, A.is_equal))
         for b in range(2):
             PE(512, ["EQB%s%d" % (H, b)] + ["PL%d" % l for l in range(8 * b, 8 * b + 8)], ["MM"],
@@ -615,23 +693,20 @@ def record(g, core, T, topo):
             PE(256, ["JC" + H, "CS%d" % (x // 4 * 4), "NIB"], ["HT"], mm)
         SC(512, ["HT"], ["HW" + H], ac(HW[:], HT[:], AF.Copy))
         PE(256 + 192, ["JC" + H, "UF" + H, "I32", "I32B", "IB", "QR", "QS"], [xk],
-           [(X[:, 128:192], T.QR[32:33, :], T.QS[32:33, :], True, False), (X[:, 129:192:2], T.I32[:], T.UF[:, s, :], False, False),
+           [(X[:, 128:192], T.QR[0:1, 0:128], T.QS[0:1, :], True, False), (X[:, 129:192:2], T.I32[:], T.UF[:, s, :], False, False),
             (X[:, 129:192:2], T.I32B[:], T.JC[:, s, 32:64], False, False), (X[:, 128:192:2], IB, T.JC[:, s, 0:32], False, True)])
-        pm = T.PM[:, s, :]
+        pm = T.PM[:, s, 0:32]
         V(64, ["MM"], ["PM" + H], ts(pm, MM[:, 0:32], 0.0, None, A.max))
+        if t < NV - 1:
+            V(64, ["MM"], ["PN" + H], ts(T.PM[:, s, 32:64], MM[:, 0:32], 0.5, None, A.is_ge))
         PE(192, ["PM" + H, "QA", "QB", "QC"], ["MM"], [(MM[:, 32 + 32 * x:64 + 32 * x], T.QQ[:, x, :], pm, True, True) for x in range(3)])
         V(96, ["MM"], ["MS" + H], ts(T.MS[:, s, 0:96], MM[:, 32:128], 0.5, None, A.is_ge))
         PE(256, ["MS" + H, "WX", "CJ", "IB"], ["MM"], [(MM[:, 128:160], IB, T.CJ[:], True, False)] +
            [(MM[:, 128:160], T.WX[:, x, :], T.MS[:, s, 32 * x:32 * x + 32], False, x == 2) for x in range(3)])
         V(64, ["MS" + H], ["CD" + H], tt(T.MS[:, s, 96:128], T.MS[:, s, 0:32], T.MS[:, s, 32:64], A.subtract))
-        if U16S:
-            V(64, ["MM", "R1"], ["LS" + H], scan(LS[:, 1:33], T.R1[:], MM[:, 128:160], 0.0, A.mult, A.max))
-            V(2 * (57 + 16 * GAT), ["LS" + H, "HW" + H, "CD" + H], ["DMs" + H],
-              *[tt(T.DM[:, s, 16 * c:16 * c + 16], HW[:].indirect(LS[:, 16 * c + 16:16 * c + 17]), T.MS[:, s, 96 + 16 * c:112 + 16 * c], A.mult) for c in range(2)])
-        else:
-            V(64, ["MM", "R1"], ["SX" + H], scan(T.SX[:, s, :], T.R1[:], MM[:, 128:160], 0.0, A.mult, A.max))
-            V(64, ["SX" + H], ["LS" + H], cp(LS[:, 0:2], T.SX[:, s, 15:32:16]))
-            V(57 + 32 * GAT, ["LS" + H, "HW" + H, "CD" + H], ["DMs" + H], tt(T.DM[:, s, 0:32], HW[:].indirect(LS[:, 0:2]), T.MS[:, s, 96:128], A.mult))
+        V(64, ["MM", "R1"], ["LS" + H], scan(LS[:, 1:33], T.R1[:, 0:32], MM[:, 128:160], 0.0, A.mult, A.max))
+        V(2 * (57 + 16 * GAT), ["LS" + H, "HW" + H, "CD" + H], ["DMs" + H],
+          *[tt(T.DM[:, s, 16 * c:16 * c + 16], HW[:].indirect(LS[:, 16 * c + 16:16 * c + 17]), T.MS[:, s, 96 + 16 * c:112 + 16 * c], A.mult) for c in range(2)])
         V(64, ["NS" + H, xk], ["JU" + H], scan(T.JU[:, s, :], T.NS[:, s, :], X[:, 128:192], 0.0, A.mult, A.add))
         V(64, ["JU" + H], ["JX" + H], ts(T.JX[:, s, :], T.JU[:, s, 1:64:2], 5, 4095, A.arith_shift_right, A.bitwise_and))
         V(64, ["JX" + H, "NS" + H], ["DFj" + H], tt(T.DF[:, s, 32:64], T.JX[:, s, :], JJ, A.subtract))
@@ -657,42 +732,39 @@ def record(g, core, T, topo):
         if not last:
             send("f", t, s, ["FO" + k])
         mf = T.MF[:, s, :]
-        V(128, ["FO" + k, xk, "SM" + H], ["MF" + H], *[tt(T.MF[:, s, 64 * a:64 * a + 64], X[:, 64 * a:64 * a + 64], T.FO[:, o, :], A.mult) for a in range(2)])
-        EL, VV = MM[:, 160:168], MM[:, 168:176]
-        PE(1024, ["MF" + H, "RW"], ["MM"], [(EL, T.RW[:, 15 - p:143 - p], T.MF[:, s, p:128:16], p == 0, p == 15) for p in range(16)])
-        V(64, ["MM"], ["E16" + H], ts(E16[:], EL, 2048.0, None, A.add))
-        if OPT["ef"] == "s":
-            SC(8, ["MM"], ["EF" + H], ac(T.EF[:, s, :], EL, AF.Copy, bias=2048.0))
+        V(128, ["FO" + k, xk, "SM" + H], ["MF" + H], *[tt(T.MF[rows(a), s, 64 * a:64 * a + 64], X[rows(a), 0:64], T.FO[rows(a), o, :], A.mult) for a in range(2)])
+        EO = T["EO" + H]
+        PE(192, ["MF" + H, "BLK", "IB", "CK"], ["MM"], [(MM[:, 176:240], IB, T.CK[:], True, False)] +
+           [(MM[:, 176:240], T.BLK[:], T.MF[:, s, 64 * a:64 * a + 64], False, a == 1) for a in range(2)])
+        V(64, ["MM", "R1"], ["EO" + H], scan(EO[:, 1:65], T.R1[:], MM[:, 176:240], 0.0, A.mult, A.max))
+        V(4 * (57 + 16 * GAT), rk(s) + ["EO" + H, "Z5" + H], ["SU" + H],
+          *[tt(T.SU[:, s, 16 * c:16 * c + 16], RO[:, 0:4096].indirect(EO[:, 16 * c + 16:16 * c + 17]), T.Z5[:, s, 16 * c:16 * c + 16], A.add) for c in range(4)])
+        V(64, ["SU" + H], ["ZO" + k], ts(T.ZO[:, o, :], T.SU[:, s, :], 1.5 * 2 ** 24, 1.5 * 2 ** 24, A.add, A.subtract))
+        if last:
+            V(128, ["ZO" + k], ["YZ" + H], *[ts(T.YZ[:, s, 32 * b:32 * b + 32], T.ZO[:, o, b:64:2], 0.5, None, A.mult) for b in range(2)])
+            V(128, ["FO" + k], ["YF" + H], *[ts(T.YF[:, s, 32 * b:32 * b + 32], T.FO[:, o, b:64:2], 2048.0, None, A.add) for b in range(2)])
         else:
-            V(64, ["MM"], ["EF" + H], ts(T.EF[:, s, :], EL, 2048.0, None, A.add))
-        ya = T.YA[:, s, :]
-        if OPT["ya"] == "s":
-            SC(128 * GAT + 5, rk(s) + ["E16" + H], ["YA" + H], ac(ya, RO[:, 0:4096].indirect(E16[:]), AF.Copy))
-        else:
-            V(128 * GAT + 57, rk(s) + ["E16" + H], ["YA" + H], cp(ya, RO[:, 0:4096].indirect(E16[:])))
+            send("z", t, s, ["ZO" + k])
+        EL, VV = HT[:, 0:8], HT[:, 8:16]
+        PE(1024, ["MF" + H, "RW"], ["HT"], [(EL, T.RW[:, 15 - p:143 - p], T.MF[:, s, p:128:16], p == 0, p == 15) for p in range(16)])
+        V(64, ["HT"], ["E16" + H], ts(E16[:], EL, 2048.0, None, A.add))
         for x in range(4):
             bk = "EQ"
             dd = EQ[:, 128 * x:128 * x + 128]
             PE(384, ["MF" + H, "MK%d" % t, "IB", "GS%d" % x], [bk], [(dd, IB, T.MK[:, t, :], True, False), (dd, T.GS[:, x, :], mf, False, False),
                                                                     (dd, mf, T.GS[:, 4 + x, :], False, True)])
-        zz = HT[:, 0:64]
-        PE(64 * 3, zk(t, s) + ["QR", "ONES", "HB"], ["HT"], [(zz, T.QR[0:1, :], T.ONES[0:1, 0:64], True, False)] +
-           [(HT[:, 32 * b:32 * b + 32], T.HB[:, 2, :], T.Z[:, o, b:64:2], False, False) for b in range(2)])
-        PE(128, ["YA" + H, "HB"], ["HT"], [(zz, T.HB[:, a, :], T.YA[:, s, 64 * a:64 * a + 64], False, a == 1) for a in range(2)])
-        big = 1.5 * 2 ** 23
-        if last:
-            V(128, ["HT"], ["YZ" + H], *[ts(T.YZ[:, s, 32 * b:32 * b + 32], HT[:, b:64:2], big, big, A.add, A.subtract) for b in range(2)])
-            V(128, ["FO" + k], ["YF" + H], *[ts(T.YF[:, s, 32 * b:32 * b + 32], T.FO[:, o, b:64:2], 2048.0, None, A.add) for b in range(2)])
-        else:
-            V(64, ["HT"], ["ZO" + k], ts(T.ZO[:, o, :], zz, big, big, A.add, A.subtract))
-            send("z", t, s, ["ZO" + k])
-        PE(128 + 256, ["YA" + H, "Z4" + H, "IB", "NSEL0", "NSEL1"], ["HT"], [(HT[:, 128:256], IB, ya, True, False)] +
-           [(HT[:, 128 + 64 * a + 32 * b:160 + 64 * a + 32 * b], T.SEL[:, 2 + a, :], T.Z4[:, s, b:64:2], False, a + b == 2) for a in range(2) for b in range(2)])
+        mm = []
+        for a in range(2):
+            mm.append((MM[:, 256 + 64 * a:320 + 64 * a], T.SEL[:, a, :], T.SU[:, s, :], True, False))
+            for b in range(2):
+                dd = MM[:, 256 + 64 * a + 32 * b:288 + 64 * a + 32 * b]
+                mm += [(dd, T.SEL[:, 2 + a, :], T.Z4[:, s, b:64:2], False, False), (dd, T.SEL[:, 4 + a, :], T.Z[:, o, b:64:2], False, b == 1)]
+        PE(640, ["SU" + H, "Z4" + H, "SEL0", "SEL1", "NSEL0", "NSEL1"] + zk(t, s), ["MM"], mm)
         if OPT["rn"] == "s":
-            SC(128, ["HT", "b128"], ["RN" + H], ac(T.RN[:, s, :], HT[:, 128:256], AF.Relu, bias=T.RF[:, 12:13]))
+            SC(128, ["MM", "b128"], ["RN" + H], ac(T.RN[:, s, :], MM[:, 256:384], AF.Relu, bias=T.RF[:, 12:13]))
         else:
-            V(128, ["HT"], ["RN" + H], ts(T.RN[:, s, :], HT[:, 128:256], 129.0, 0.0, A.add, A.max))
-        PE(256, ["DUMP", "I32"], ["MM"], [(VV, T.I32[:], T.DUMP[:], True, False)])
+            V(128, ["MM"], ["RN" + H], ts(T.RN[:, s, :], MM[:, 256:384], 129.5, 0.0, A.add, A.max))
+        PE(256, ["DUMP", "I32"], ["HT"], [(VV, T.I32[:], T.DUMP[:], True, False)])
         for x in range(4):
             bk = "EQ"
             dd = EQ[:, 128 * x:128 * x + 128]
@@ -702,12 +774,8 @@ def record(g, core, T, topo):
                 SC(8, ["LO%s%d" % (H, x), "WD"], ["LX%s%d" % (H, x)], ac(lx, T.WD[:, 8:16], AF.Copy, scale=lo))
             else:
                 V(64, ["LO%s%d" % (H, x), "WD"], ["LX%s%d" % (H, x)], ts(lx, T.WD[:, 8:16], lo, None, A.mult))
-            PE(64, ["LX%s%d" % (H, x), "BK"], ["MM"], [(VV, T.BK[:, x, :], lx, False, x == 3)])
-        if U16T:
-            V(64, ["MM", "EF" + H], ["OF" + H], tt(OF[:], VV, T.EF[:, s, :], A.max))
-        else:
-            V(64, ["MM", "EF" + H], ["OT" + H], tt(T.OT[:, s, :], VV, T.EF[:, s, :], A.max))
-            V(64, ["OT" + H], ["OF" + H], cp(OF[:], T.OT[:, s, :]))
+            PE(64, ["LX%s%d" % (H, x), "BK"], ["HT"], [(VV, T.BK[:, x, :], lx, False, x == 3)])
+        V(64, ["HT", "E16" + H], ["OF" + H], tt(OF[:], VV, E16[:], A.max))
         V(57 + 128 * SCA, ["OF" + H, "RN" + H], rk(s), cp(RO[:].indirect(OF[:]), T.RN[:, s, :]))
         if last:
             for a in range(2):
@@ -719,9 +787,11 @@ def record(g, core, T, topo):
                 dma("ys"[a * s], "od_x" + n, T.yx[rows(s), 2048 * a:2048 * a + 2048], RO[rows(a), 2048 * a:2048 * a + 2048], rk(s), ["ox" + n], 3.5)
 
     def count(t):
-        PE(280 + 256, ["MS0", "MS1", "S15", "I32", "CN"], ["K0"], [(T.K0[:, 256:326], T.I32[:], T.CN[:, 0, :], True, False)] +
-           [(T.K0[:, 256 + 36 * x:288 + 36 * x], T.S15[:], T.MS[:, s, 64:96], False, s + x == 2) for s in range(2) for x in range(2)])
-        V(70, ["K0", "CN"], ["TOP%d" % (t + 1)], scan(T.TOP[:, t + 1, :], T.CN[:, 1, :], T.K0[:, 256:326], 0.0, A.mult, A.add))
+        bk = OPT["nb"]
+        for s in range(2):
+            PE(128 + 288 * (s == 0), ["PN%d" % s, "ONES", "I32", "CN"], [bk], [(T[bk][:, 256:328], T.I32[:], T.CN[:, 0, :], True, False)][:s == 0] +
+               [(T[bk][:, 256 + 36 * x:288 + 36 * x], T.ONES[:], T.PM[:, s, 32:64], False, s + x == 2) for x in range(2)])
+        V(72, [bk, "CN"], ["TOP%d" % (t + 1)], scan(T.TOP[:, t + 1, :], T.CN[:, 1, :], T[bk][:, 256:328], 0.0, A.mult, A.add))
 
     for t in range(NV):
         S["st"] = "k"

from concourse.mybir import AluOpType as A, ActivationFunctionType as AF, AxisListType

NV = 5
NG = 32
SCRATCH = {
    "PI": ("sbuf", [128, 8], "int32"), "RF": ("sbuf", [128, 16], "float32"),
    "ONES": ("sbuf", [128, 128], "bfloat16"), "NEG": ("sbuf", [128, 128], "bfloat16"), "IB": ("sbuf", [128, 128], "bfloat16"),
    "I32": ("sbuf", [128, 128], "float32"), "NI32": ("sbuf", [128, 128], "float32"), "ONE32": ("sbuf", [128, 128], "float32"),
    "PERM": ("sbuf", [128, 128], "float32"),
    "GR": ("sbuf", [128, 128], "bfloat16"), "CR": ("sbuf", [128, 128], "bfloat16"), "G4": ("sbuf", [128, 128], "bfloat16"),
    "XR": ("sbuf", [128, 144], "bfloat16"), "RW": ("sbuf", [128, 144], "bfloat16"), "BLK": ("sbuf", [128, 128], "bfloat16"),
    "T1": ("sbuf", [128, 128], "float32"), "T2": ("sbuf", [128, 128], "float32"), "T3": ("sbuf", [128, 128], "bfloat16"),
    "T4": ("sbuf", [128, 128], "bfloat16"), "TI": ("sbuf", [128, 128], "int32"), "P4": ("sbuf", [128, 128], "float32"),
    "KT": ("sbuf", [128, 16], "float32"), "NKT": ("sbuf", [128, 16], "float32"), "KH": ("sbuf", [128, 8], "float32"),
    "SCM": ("sbuf", [128, 4, 128], "bfloat16"), "L3": ("sbuf", [128, 128], "bfloat16"), "R3": ("sbuf", [128, 512], "bfloat16"),
    "WD": ("sbuf", [128, 16], "bfloat16"), "CM": ("sbuf", [128, 256], "bfloat16"), "RS": ("sbuf", [128, 128], "bfloat16"),
    "XK": ("sbuf", [128, 144], "bfloat16"), "RK": ("sbuf", [128, 2, 144], "bfloat16"), "NIB": ("sbuf", [128, 128], "bfloat16"),
    "R1": ("sbuf", [128, 64], "bfloat16"), "CJ": ("sbuf", [128, 32], "bfloat16"),
    "EL": ("sbuf", [128, 16, 128], "bfloat16"), "PL": ("sbuf", [128, 16, 128], "bfloat16"), "CS": ("sbuf", [128, 16, 128], "bfloat16"),
    "SLB": ("sbuf", [128, 128], "bfloat16"), "QQ": ("sbuf", [128, 3, 128], "bfloat16"), "WX": ("sbuf", [128, 3, 128], "bfloat16"),
    "S15": ("sbuf", [128, 128], "bfloat16"), "I32B": ("sbuf", [128, 128], "bfloat16"), "HB": ("sbuf", [128, 3, 128], "bfloat16"),
    "SEL": ("sbuf", [128, 6, 128], "bfloat16"), "GS": ("sbuf", [128, 8, 128], "bfloat16"), "BK": ("sbuf", [128, 4, 128], "bfloat16"),
    "CL": ("sbuf", [128, NV, 128], "bfloat16"), "MK": ("sbuf", [128, NV, 128], "bfloat16"), "DUMP": ("sbuf", [128, 8], "float32"),
    "QR": ("sbuf", [128, 192], "bfloat16"), "QS": ("sbuf", [128, 64], "bfloat16"),
    "WI": ("sbuf", [128, 2], "int32"), "WL": ("sbuf", [128, 2], "bfloat16"), "W2": ("sbuf", [128, 2, 128], "bfloat16"),
    "LIM": ("sbuf", [128, 2], "float32"), "TOP": ("sbuf", [128, NV, 72], "bfloat16"), "CN": ("sbuf", [128, 2, 72], "float32"),
    "BQ": ("sbuf", [128, 128], "bfloat16"), "CK": ("sbuf", [128, 64], "bfloat16"),
    "FI": ("sbuf", [128, 2, 64], "int32"),
    "F": ("sbuf", [128, 2 * NV, 64], "float16"), "FO": ("sbuf", [128, 2 * NV, 64], "float16"),
    "Z": ("sbuf", [128, 2 * NV, 64], "bfloat16"), "ZO": ("sbuf", [128, 2 * NV, 64], "bfloat16"),
    "YF": ("sbuf", [128, 2, 64], "float32"), "YZ": ("sbuf", [128, 2, 64], "bfloat16"),
}
for _n, _w, _d in (("UA", 64, "float32"), ("UI", 512, "float32"), ("Z5", 64, "float32"), ("SU", 64, "float16"), ("HM", 512, "int32"),
                   ("C4", 256, "int32"), ("UF", 32, "float32"), ("Z4", 64, "bfloat16"), ("KE", 128, "float32"),
                   ("KS", 256, "int32"), ("KC", 64, "int32"), ("NB", 64, "int32"), ("PR", 320, "float32"), ("HF", 96, "float16"),
                   ("JC", 64, "float16"), ("NS", 64, "float32"), ("EQB", 512, "bfloat16"), ("PM", 64, "bfloat16"),
                   ("MS", 128, "bfloat16"), ("SX", 32, "float32"), ("JU", 64, "int32"), ("JX", 32, "int32"),
                   ("DF", 64, "float32"), ("DM", 64, "float32"), ("MF", 128, "float16"), ("EF", 8, "float32"), ("YA", 128, "bfloat16"),
                   ("LO", 4, "float32"), ("LX", 32, "bfloat16"), ("OT", 8, "float32"), ("RN", 128, "bfloat16"),
                   ("D", 4096, "bfloat16"), ("NR", 4096, "bfloat16")):
    SCRATCH[_n] = ("sbuf", [128, 2, _w], _d)
for _s in "01":
    for _n, _w, _d in (("ROCK", 4096 + 128, "bfloat16"), ("CO", 256, "uint16"), ("ZX", 16 * NG, "bfloat16"), ("HW", 512, "float32"),
                       ("LS", 34, "uint16"), ("EO", 66, "uint16"), ("E16", 8, "uint16"), ("OF", 8, "uint16")):
        SCRATCH[_n + _s] = ("sbuf", [128, _w], _d)
BANKS = ["X0", "X1", "K0", "K1", "KX", "EQ", "HT", "MM"]
for _n in BANKS:
    SCRATCH[_n] = ("psum", [128, 512], "float32")

LOADS = ["wi", "li"] + [n + s + a for n in "fvr" for s in "01" for a in "01"]
STORES = [n + s + a for n in "fzx" for s in "01" for a in "01"]
SEMAPHORES = (["sv", "ss", "st", "sg", "sl"] + ["ld_" + n for n in LOADS] + ["od_" + n for n in STORES] +
              ["ar%s%d%d" % (k, t, s) for k in "fz" for t in range(1, NV) for s in range(2)])
QSEM = {"v": "sv", "s": "ss", "t": "st", "g": "sg"}
CYC = 0.00085
PEC = 0.00043
LAT = 0.28
DML = 1.8
GAT = 1.56
SCA = 3.8
SFIX = 70
BIAS = {'e0': 3.25, 'c1': 1.5, 'cvUA': -2, 'stX1': 2, 'etEQ': -1, 'e1': 1.5, 'msD0': 0.25, 'ctX0': 2, 'evDM': 0.25, 'itMM': 0.5,
        'mvKS': -0.25, 'isRN': 0.25, 'evLS': -0.5, 'cvCO': 0.5, 'ivE1': -0.5, 'i1': 0.25, 'ivLX': 0.25}
SGRP = 2
VP = 2
LOOK = 0.3
ROUNDS = 2
SWAPS = 0
TABOO = 30
KS = ("GS", "WX", "U0", "U1")
ZS = 12
ZV = 2
ABS = (10, 10, 11, 12)
NPC = 256
OPT = {"lx": "v", "rn": "s", "hf": "2", "ke": "s", "z4": "s", "z5": "s", "nb": "HT"}
PLANS = {}


def add(S, q, cost, reads, writes, fn, sig=None, lat=0.0):
    i = len(S["ops"])
    deps = {}

    def dep(j, sem):
        if j != i:
            deps[j] = deps.get(j, False) or sem
    for k in reads + writes:
        if k in BANKS:
            for q2, j in S["b"].setdefault(k, {}).items():
                dep(j, q2 != q)
    for k in reads:
        if k not in BANKS:
            for j in S["w"].get(k, []):
                dep(j, True)
    for k in writes:
        if k not in BANKS:
            for j in S["w"].get(k, []) + S["r"].get(k, []):
                dep(j, True)
    for k in reads + writes:
        if k in BANKS:
            S["b"][k][q] = i
        elif k in writes:
            S["w"][k] = [i]
            S["r"][k] = []
    for k in reads:
        if k not in BANKS and k not in writes:
            S["r"].setdefault(k, []).append(i)
    S["ops"].append({"q": q, "cost": cost, "deps": deps, "fn": fn, "sig": sig, "lat": lat, "st": S.get("st", ""), "nm": " ".join(writes)})
    return i


def plan(S):
    ops = S["ops"]
    n = len(ops)
    succ = [[] for _ in range(n)]
    for i, o in enumerate(ops):
        for j in o["deps"]:
            succ[j].append(i)
    pri = [0.0] * n
    left = [len(x) for x in succ]
    back = [i for i in range(n) if left[i] == 0]
    for i in back:
        for j in ops[i]["deps"]:
            left[j] -= 1
            if left[j] == 0:
                back.append(j)
    for i in back:
        o = ops[i]
        b = 0.0
        for k in succ[i]:
            b = max(b, pri[k] + (o["lat"] if o["sig"] else (LAT if ops[k]["deps"][i] else 0.0)))
        pri[i] = b + o["cost"]
    pri = [p + BIAS.get(o["st"][:1] + o["q"] + o["nm"][:2], 0.0) + BIAS.get(o["st"], 0.0) for p, o in zip(pri, ops)]
    left = [len(o["deps"]) for o in ops]
    ready = {}
    est = [0.0] * n
    free = {}
    for i in range(n):
        if left[i] == 0:
            ready.setdefault(ops[i]["q"], []).append(i)
    order = []
    end = 0.0
    while len(order) < n:
        best = None
        for q, lst in ready.items():
            if lst:
                st = max(free.get(q, 0.0), min(est[i] for i in lst))
                if best is None or st < best[0]:
                    best = (st, q)
        st, q = best
        lst = ready[q]
        c = max((i for i in lst if est[i] <= st + 1e-9), key=lambda i: (pri[i], -i))
        for i in lst:
            if pri[i] > pri[c] and est[i] < st + LOOK * ops[c]["cost"]:
                c = i
        st = max(st, est[c])
        lst.remove(c)
        o = ops[c]
        fin = st + o["cost"]
        free[q] = fin
        o["start"] = st
        end = max(end, fin + o["lat"])
        order.append(c)
        for k in succ[c]:
            d = ops[k]["deps"][c]
            l = o["lat"] if o["sig"] else (LAT if d else 0.0)
            est[k] = max(est[k], fin + l if d else st)
            left[k] -= 1
            if left[k] == 0:
                ready.setdefault(ops[k]["q"], []).append(k)
    S["end"] = end
    if not ROUNDS:
        return order
    pred = [[(j, (ops[j]["lat"] if ops[j]["sig"] else LAT) if d else 0.0) for j, d in o["deps"].items()] for o in ops]
    after = [[] for _ in ops]
    for i in range(n):
        for j, l in pred[i]:
            after[j].append((i, l))
    start = [o["start"] for o in ops]
    best = (end, start)
    for _ in range(ROUNDS):
        rank = sorted(range(n), key=lambda i: (-(start[i] + ops[i]["cost"]), -start[i], -i))
        back = place(ops, rank, after, [o["lat"] for o in ops])
        rank = sorted(range(n), key=lambda i: (-(back[i] + ops[i]["cost"]), -back[i], i))
        start = place(ops, rank, pred, [0.0] * n)
        end = max(s + o["cost"] + o["lat"] for s, o in zip(start, ops))
        if end < best[0]:
            best = (end, start)
    S["end"], start = best
    if SWAPS:
        S["end"], start = polish(ops, sorted(range(n), key=lambda i: start[i]), pred, after)
    for s, o in zip(start, ops):
        o["start"] = s
    return sorted(range(n), key=lambda i: start[i])


def polish(ops, order, pred, after):
    n = len(ops)
    cost = [o["cost"] for o in ops]
    last = [o["lat"] for o in ops]
    prev, nxt, tail_of = [-1] * n, [-1] * n, {}
    for i in order:
        j = tail_of.get(ops[i]["q"], -1)
        prev[i] = j
        if j >= 0:
            nxt[j] = i
        tail_of[ops[i]["q"]] = i
    best, taboo = None, {}
    for it in range(SWAPS):
        head, tail = [0.0] * n, [0.0] * n
        for i in order:
            j = prev[i]
            t = head[j] + cost[j] if j >= 0 else 0.0
            for j, l in pred[i]:
                x = head[j] + cost[j] + l
                if x > t:
                    t = x
            head[i] = t
        end = 0.0
        for i in reversed(order):
            j = nxt[i]
            t = tail[j] if j >= 0 else 0.0
            if last[i] > t:
                t = last[i]
            for j, l in after[i]:
                x = tail[j] + l
                if x > t:
                    t = x
            tail[i] = t + cost[i]
            if t + cost[i] > end:
                end = t + cost[i]
        if best is None or end < best[0] - 1e-9:
            best = (end, head)
        pick = None
        for u in order:
            v = nxt[u]
            if v < 0 or head[u] + tail[u] < end - 1e-9 or head[u] + cost[u] + tail[v] < end - 1e-9 or u in ops[v]["deps"]:
                continue
            p, s = prev[u], nxt[v]
            hv = max([head[p] + cost[p] if p >= 0 else 0.0] + [head[j] + cost[j] + l for j, l in pred[v]])
            hu = max([hv + cost[v]] + [head[j] + cost[j] + l for j, l in pred[u]])
            tu = cost[u] + max([tail[s] if s >= 0 else 0.0, last[u]] + [tail[j] + l for j, l in after[u]])
            tv = cost[v] + max([tu, last[v]] + [tail[j] + l for j, l in after[v]])
            e = max(hv + tv, hu + tu)
            if taboo.get((v, u), -1) >= it and e >= best[0] - 1e-9:
                continue
            if pick is None or e < pick[0]:
                pick = (e, u, v)
        if pick is None:
            break
        _, u, v = pick
        taboo[(u, v)] = it + TABOO
        p, s = prev[u], nxt[v]
        prev[v], nxt[v], prev[u], nxt[u] = p, u, v, s
        if p >= 0:
            nxt[p] = v
        if s >= 0:
            prev[s] = u
        a, b = order.index(u), order.index(v)
        behind, ahead = {u}, []
        for i in order[a + 1:b]:
            if prev[i] in behind or any(j in behind for j, l in pred[i]):
                behind.add(i)
            else:
                ahead.append(i)
        order[a:b + 1] = ahead + [v] + [i for i in order[a:b] if i in behind]
    return best


def place(ops, rank, pred, first):
    start = [None] * len(ops)
    lines = {}
    for i in rank:
        t = first[i]
        for j, l in pred[i]:
            t = max(t, start[j] + ops[j]["cost"] + l)
        c = ops[i]["cost"]
        a, b = lines.setdefault(ops[i]["q"], ([], []))
        lo, hi = 0, len(a)
        while lo < hi:
            mid = (lo + hi) // 2
            if b[mid] <= t:
                lo = mid + 1
            else:
                hi = mid
        while lo < len(a) and a[lo] < t + c - 1e-9:
            t = max(t, b[lo])
            lo += 1
        a.insert(lo, t)
        b.insert(lo, t + c)
        start[i] = t
    return start


def issue(S, order, eng, T):
    ops = S["ops"]
    cnt = {}
    known = {q: {} for q in eng}
    for i in order:
        o = ops[i]
        q = o["q"]
        kn = known[q]
        need = {}
        for j, sem in o["deps"].items():
            if sem:
                s, val = ops[j]["done"]
                if kn.get(s, 0) < val:
                    need[s] = max(need.get(s, 0), val)
        for s in sorted(need):
            eng[q].wait_ge(T.sem[s], need[s])
        for j, sem in o["deps"].items():
            if sem:
                for s, val in ops[j]["clock"].items():
                    if kn.get(s, 0) < val:
                        kn[s] = val
        if o["sig"]:
            o["fn"]()
            o["done"] = o["sig"]
        else:
            s = QSEM[q]
            cnt[s] = cnt.get(s, 0) + 1
            o["fn"]().then_inc(T.sem[s], 1)
            o["done"] = (s, cnt[s])
        o["clock"] = dict(kn)
        o["clock"][o["done"][0]] = o["done"][1]
    return cnt


def record(g, core, T, topo):
    rank = T.rank_of(core)
    S = {"ops": [], "w": {}, "r": {}, "b": {}, "sends": 0, "last": {}}
    v, sc, te = g.vector, g.scalar, g.tensor

    def seq(calls):
        def fn():
            for c in calls:
                x = c()
            return x
        return fn

    def V(cyc, R, W, *calls):
        return add(S, "v", max(cyc, 64 * len(calls)) * CYC, R, W, seq(calls))

    def SC(cyc, R, W, *calls):
        return add(S, "s", (cyc + SFIX * len(calls)) * CYC, R, W, seq(calls))

    def PE(cyc, R, W, mms):
        return add(S, "t", cyc * PEC, R, W, seq([(lambda m: lambda: te.matmul(*m))(m) for m in mms]))

    def G(n, R, W, *calls):
        return add(S, "g", (0.17 + 2 * n * CYC) * len(calls), R, W, seq(calls))

    def ts(out, in0, s1, s2, op0, op1=None):
        if op1 is None:
            return lambda: v.tensor_scalar(out, in0, s1, None, op0)
        return lambda: v.tensor_scalar(out, in0, s1, s2, op0, op1)

    def tt(out, a, b, op):
        return lambda: v.tensor_tensor(out, a, b, op)

    def cp(out, a):
        return lambda: v.tensor_copy(out, a)

    def ac(out, a, f, **kw):
        return lambda: sc.activation(out, a, f, **kw)

    def ms(ap, c):
        return lambda: v.memset(ap, c)

    def scan(out, d0, d1, init, op0, op1):
        return lambda: v.tensor_tensor_scan(out, d0, d1, init, op0, op1)

    def ioF(ap, pat, base, cm):
        return lambda: g.iota(ap, pat, base, cm, allow_small_or_imprecise_dtypes=True)

    def ioI(ap, pat, base, cm):
        return lambda: g.iota(ap, pat, base, cm)

    def sel(out, a, pat, op, fill, base, cm):
        return lambda: g.affine_select(out, a, pat, op, fill, base, cm)

    def dma(q, sem, out, in_, R, W, lat):
        e = g.sync if q == "y" else g.scalar
        add(S, q, 0.06, R, W, lambda: e.dma_start(out, in_).then_inc(T.sem[sem], 16), (sem, 16), lat)

    def rows(s):
        return slice(64 * s, 64 * s + 64)
    for s in range(2):
        for a in range(2):
            n = "%d%d" % (s, a)
            dma("y", "ld_f" + n, T.FI[rows(a), s, :], T.front[rows(s), rows(a)], [], ["FI" + n], 2.2)
            dma("s", "ld_v" + n, T.YZ[rows(a), s, :], T.vein[rows(s), rows(a)], [], ["Zl" + n], 2.2)
        if s == 0:
            dma("s", "ld_wi", T.WI[:, 0:1], T.w[:], [], ["WI0"], 2.2)
            dma("s", "ld_li", T.WI[:, 1:2], T.lim[:], [], ["WI1"], 2.2)
        for a in range(2):
            n = "%d%d" % (s, a)
            dma("y", "ld_r" + n, T["ROCK%d" % s][rows(a), 0:4096], T.rock[rows(s), :], [], ["ROCK" + n], 5.0 + 3.5 * s)

    def scaled(n, R, W, *xs):
        if n in KS:
            SC(128 * len(xs), R, W, *[ac(o, a, AF.Copy, scale=c) for o, a, c in xs])
        else:
            V(64, R, W, *[ts(o, a, c, None, A.mult) for o, a, c in xs])
    S["st"] = "k"
    G(1, [], ["PI"], ioI(T.PI[:, 0:1], [[1, 1]], 0, 1))
    G(128, [], ["GR"], ioF(T.GR[:], [[1, 8], [0, 16]], 0, 0))
    G(128, [], ["CR"], ioF(T.CR[:], [[0, 8], [1, 16]], 0, 0))
    V(64, [], ["ONES"], ms(T.ONES[:], 1.0))
    V(64, [], ["NEG"], ms(T.NEG[:], -1.0))
    V(128, [], ["ONE32"], ms(T.ONE32[:], 1.0))
    G(128, ["ONES"], ["IB"], sel(T.IB[:], T.ONES[:], [[-1, 128]], A.is_equal, 0.0, 0, 1))
    for a in range(2):
        G(128, ["ONES"], ["SEL%d" % a], sel(T.SEL[:, a, :], T.ONES[:], [[0, 2], [-1, 64]], A.is_equal, 0.0, -64 * a, 1))
        scaled("SE", ["SEL%d" % a], ["NSEL%d" % a], (T.SEL[:, 2 + a, :], T.SEL[:, a, :], -1.0), (T.SEL[:, 4 + a, :], T.SEL[:, a, :], -0.5))
    V(64, ["PI"], ["PIr"], ts(T.PI[:, 1:2], T.PI[:, 0:1], 15, None, A.bitwise_and))
    V(64, ["PI"], ["PIg"], ts(T.PI[:, 2:3], T.PI[:, 0:1], 4, None, A.arith_shift_right))
    V(64, ["PI"], ["PIm"], ts(T.PI[:, 3:4], T.PI[:, 0:1], 4, 3, A.arith_shift_right, A.bitwise_and))
    V(64, ["PIr", "PIg", "PIm"], ["r"], cp(T.RF[:, 0:3], T.PI[:, 1:4]))
    r, gp, mi = T.RF[:, 0:1], T.RF[:, 1:2], T.RF[:, 2:3]
    V(64, ["GR", "r"], ["BLK"], ts(T.BLK[:], T.GR[:], gp, None, A.is_equal))
    V(64, ["WI0", "WI1"], ["WL"], cp(T.WL[:], T.WI[:]))
    PE(128, ["WL", "SEL0", "SEL1"], ["MM"], [(T.MM[:, 2 * s:2 * s + 2], T.SEL[:, s, :], T.WL[:], True, True) for s in range(2)])
    for s in range(2):
        V(64, ["MM", "BLK"], ["W2%d" % s], ts(T.W2[:, s, :], T.BLK[:], T.MM[:, 2 * s:2 * s + 1], None, A.mult))
    V(64, ["MM"], ["LIM"], ts(T.LIM[:], T.MM[:, 1:4:2], 1.0, None, A.add))
    V(128, ["LIM"], ["TOP0"], cp(T.TOP[:, 0, 68:72:2], T.LIM[:]), ts(T.TOP[:, 0, 69:72:2], T.LIM[:], 2.0, None, A.mult))
    V(144, [], ["CNz"], ms(T.CN[:, 0, :], 0.0), ms(T.CN[:, 1, :], 1.0))
    V(64, ["CNz", "LIM"], ["CN"], cp(T.CN[:, 0, 68:69], T.LIM[:, 0:1]), tt(T.CN[:, 0, 70:71], T.LIM[:, 1:2], T.LIM[:, 0:1], A.subtract),
      *[ms(T.CN[:, x, c:d:2], y) for x, c, d, y in ((0, 32, 33, -0.375), (0, 33, 34, 1.5 * 2 ** 23), (0, 34, 35, -1.5 * 2 ** 23), (1, 32, 33, 0.25),
                                                    (1, 35, 36, -4.0), (1, 69, 72, 2.0), (1, 70, 71, 0.5))])
    V(64, ["BLK"], ["BQ"], ts(T.BQ[:], T.BLK[:], 1.0 / 32, None, A.mult))
    for s in range(2):
        V(64, ["Zl%d0" % s, "Zl%d1" % s], ["Z0%d" % s], ts(T.Z[:, s, :], T.YZ[:, s, :], 2.0, None, A.mult))
        V(64, ["ONES"], ["MF%d" % s], ts(T.MF[:, s, :], T.ONES[:], 0.0, None, A.mult))
        V(64, ["FI%d0" % s, "FI%d1" % s], ["F0%d" % s], ts(T.F[:, s, :], T.FI[:, s, :], -2048.0, None, A.add))
    pw = [32, 32, 64, 128]
    for m in range(4):
        V(64, ["IB"], ["SCM%d" % m], ts(T.SCM[:, m, :], T.IB[:], float(pw[m]), None, A.mult))
    V(64, ["IB"], ["NIB"], ts(T.NIB[:], T.IB[:], -1.0, None, A.mult))
    V(64, [], ["L3z"], ms(T.L3[:], 1.0))
    V(64, ["L3z", "CR"], ["L3"], cp(T.L3[0:1, :], T.CR[0:1, :]))
    V(256, [], ["R3z"], ms(T.R3[:], 0.0))
    fills = []
    for m in range(4):
        c = (2048 + 613 * m) * 2 ** (5 + m) - 2 ** 23
        if m:
            c -= (2048 + 613 * (m - 1)) * 2 ** (4 + m) - 2 ** 23
        hi = (c >> 16) << 16
        lo1 = ((c - hi) >> 8) << 8
        for row, x in ((0, 37 * pw[m]), (32, hi), (64, lo1), (96, c - hi - lo1)):
            if x:
                fills.append(ms(T.R3[row:row + 1, 4 + m:512:8], float(x)))
    for row, col, x in ((32, 0, -2048.0), (64, 0, 1.0), (32, 1, 1.5 * 2 ** 23), (32, 2, -1.5 * 2 ** 23), (32, 3, 1.0)):
        fills.append(ms(T.R3[row:row + 1, col:512:8], x))
    V(64, ["R3z"], ["R3"], *fills)
    V(128, ["BLK"], ["WD"], ts(T.WD[:, 0:8], T.BLK[:, 0:128:16], 256.0, None, A.mult), cp(T.WD[:, 8:16], T.BLK[:, 0:128:16]))
    G(128, [], ["CM"], ioF(T.CM[0:1, 0:4 * NG], [[64, 4], [0, NG]], 23, 0), ioF(T.CM[0:1, 4 * NG:256], [[0, 64 - NG], [64, 4]], 23, 0))
    G(NG, ["ONE32"], ["PERM"], *([sel(T.PERM[:, m:4 * NG:4], T.ONE32[:, 0:NG], [[-1, NG]], A.is_equal, 0.0, -NG * m, 1) for m in range(4)] +
                                 ([sel(T.PERM[:, 4 * NG:128], T.ONE32[:, 4 * NG:128], [[-1, 128 - 4 * NG]], A.is_equal, 0.0, -4 * NG, 1)] if NG < 32 else [])))
    V(128, ["IB"], ["I32"], cp(T.I32[:], T.IB[:]))
    V(128, ["IB"], ["NI32"], ts(T.NI32[:], T.IB[:], -1.0, None, A.mult))
    V(64, [], ["RSz"], ms(T.RS[:], 0.0))
    V(64, ["RSz"], ["RS"], ms(T.RS[:, 0:128:4], float(2 ** 22)))
    G(144, [], ["XK"], ioF(T.XK[:], [[1, 144]], -15, 0))
    V(64, ["r"], ["g16"], ts(T.RF[:, 13:14], gp, 16.0, None, A.mult))
    V(144, ["XK", "g16"], ["RK"], *[ts(T.RK[:, x, :], T.XK[:], T.RF[:, 13:14], (128.0, 1.0)[x], A.is_equal, A.mult) for x in range(2)])
    for s in range(2):
        if "U%d" % s in KS:
            G(512, [], ["UIa%d" % s], ioF(T.UI[:, s, :], [[0, 512]], 1, 0))
        else:
            V(512, [], ["UIa%d" % s], ms(T.UI[:, s, :], 1.0))
        V(192, ["UIa%d" % s], ["UI%d" % s], *[ms(T.UI[:, s, c:512:8], x) for c, x in ((0, 0.0), (1, 2.0 ** -12), (3, -4096.0))])
        V(64, [], ["NS%d" % s], ms(T.NS[:, s, :], 0.0))
    V(64, ["CR", "r"], ["KT"], ts(T.KT[:], T.CR[:, 0:16], r, None, A.is_equal))
    V(64, ["KT"], ["NKT"], ts(T.NKT[:], T.KT[:], -1.0, None, A.mult))
    for l in range(0, 16, 4):
        scaled("EL", ["BLK", "NKT"], ["EL%d" % l], *[(T.EL[:, x, :], T.BLK[:], T.NKT[:, x:x + 1]) for x in range(l, l + 4)])
    V(64, ["CR", "r"], ["T3"], ts(T.T3[:], T.CR[:], r, -(2.0 ** 40), A.is_gt, A.mult))
    V(128, ["T3", "BLK"], ["SLB"], tt(T.SLB[:], T.T3[:], T.BLK[:], A.mult))
    for l in range(16):
        G(128, ["SLB"], ["PL%d" % l], sel(T.PL[:, l, :], T.SLB[:], [[-1, 128]], A.not_equal, 4.0 ** (15 - l), 0, 1))
    V(256, ["CR"], ["T1", "T2"], ts(T.T1[:], T.CR[:], 0.0, 4.0, A.is_gt, A.mult), ts(T.T2[:], T.CR[:], 0.0, 4.0 ** -16, A.is_equal, A.mult))
    V(128, ["T1", "T2"], ["P4"], scan(T.P4[:], T.T1[:], T.T2[:], 0.0, A.mult, A.add))
    V(256, ["P4", "BLK"], ["QA"], tt(T.QQ[:, 0, :], T.P4[:], T.BLK[:], A.mult))
    V(64, ["P4", "KT"], ["T1"], tt(T.T1[:, 0:16], T.P4[:, 0:16], T.KT[:], A.mult))
    V(64, ["T1"], ["p4c"], lambda: v.tensor_reduce(T.RF[:, 8:9], T.T1[:, 0:16], AxisListType.X, A.add))
    V(64, ["QA", "p4c"], ["QB"], ts(T.QQ[:, 1, :], T.QQ[:, 0, :], T.RF[:, 8:9], 4.0, A.mult, A.mult))
    V(64, ["CR", "r"], ["T3"], ts(T.T3[:], T.CR[:], r, None, A.is_ge))
    V(128, ["T3", "BLK"], ["QC"], tt(T.QQ[:, 2, :], T.T3[:], T.BLK[:], A.mult))
    V(128, ["KT"], ["KH"], ts(T.KH[:, 0:1], T.KT[:, 15:16], -512.0, None, A.mult), ts(T.KH[:, 1:2], T.KT[:, 15:16], 512.0, -32.0, A.mult, A.add))
    scaled("WX", ["BLK", "KH"], ["WX"], (T.WX[:, 0, :], T.BLK[:], 32.0), (T.WX[:, 1, :], T.BLK[:], T.KH[:, 0:1]), (T.WX[:, 2, :], T.BLK[:], T.KH[:, 1:2]))
    G(32, [], ["T4j"], ioF(T.T4[:, 0:32], [[1, 32]], 0, 0))
    V(64, ["CR", "r"], ["T3"], ts(T.T3[:, 0:32], T.CR[:, 0:32], r, -2048.0, A.not_equal, A.mult))
    V(64, ["T3", "T4j"], ["CJ"], tt(T.CJ[:], T.T3[:, 0:32], T.T4[:, 0:32], A.add))
    V(64, ["CR"], ["R1"], ts(T.R1[:], T.CR[:, 0:64], 0.0, None, A.is_gt))
    V(64, ["CR", "r"], ["CKa"], ts(T.CK[:], T.CR[:, 0:64], r, -8192.0, A.not_equal, A.mult))
    V(64, ["CKa"], ["CK"], ts(T.CK[:], T.CK[:], 2048.0, None, A.add))
    G(128, [], ["TI"], ioI(T.TI[:], [[-1, 128]], 128, 1))
    V(128, ["TI"], ["TI"], ts(T.TI[:], T.TI[:], 15, None, A.bitwise_and))
    V(64, ["BLK"], ["T3"], ts(T.T3[:], T.BLK[:], -100.0, 100.0, A.mult, A.add))
    V(256, ["TI", "T3", "T4j", "CJ"], ["T4"], tt(T.T4[:], T.TI[:], T.T3[:], A.add))
    for l in range(0, 16, 4):
        V(256, ["T4"], ["CS%d" % l], *[ts(T.CS[:, x, :], T.T4[:], float((x + 1) % 16), None, A.is_equal) for x in range(l, l + 4)])
    V(64, ["IB"], ["I32B"], ts(T.I32B[:], T.IB[:], 32.0, None, A.mult))
    V(64, [], ["XRz"], ms(T.XR[:], -1.0))
    G(128, ["XRz"], ["XR"], ioF(T.XR[:, 15:143], [[0, 2], [1, 64]], 0, 0))
    V(64, ["r"], ["m16"], ts(T.RF[:, 9:10], mi, 16.0, None, A.mult))
    V(72, ["XR", "m16"], ["RW"], ts(T.RW[:], T.XR[:], T.RF[:, 9:10], None, A.is_equal))
    V(128, [], ["QR"], ms(T.QR[0:1, 128:192], -1.0 / 16), ms(T.QR[0:1, 0:128], 2048.0))
    V(64, [], ["QSz"], ms(T.QS[0:1, :], 0.0))
    V(64, ["QSz"], ["QS"], ms(T.QS[0:1, 0:64:2], 1.0))
    V(256, ["r"], ["KM"], *[ts(T.KH[:, 4 + x:5 + x], mi, float(x), None, A.is_equal) for x in range(4)])
    for x in range(4):
        scaled("GS", ["ONES", "NEG", "KM"], ["GS%d" % x], (T.GS[:, x, :], T.ONES[:], T.KH[:, 4 + x:5 + x]), (T.GS[:, 4 + x, :], T.NEG[:], T.KH[:, 4 + x:5 + x]))
    G(128, [], ["G4"], ioF(T.G4[:], [[0, 2], [1, 4], [0, 16]], 0, 0))
    V(64, ["CR", "r"], ["T3"], ts(T.T3[:], T.CR[:], r, 100.0, A.not_equal, A.mult))
    V(128, ["T3", "G4"], ["G4"], tt(T.G4[:], T.G4[:], T.T3[:], A.add))
    V(256, ["G4"], ["BK"], *[ts(T.BK[:, x, :], T.G4[:], float(x), 8192.0, A.is_equal, A.mult) for x in range(4)])
    G(8, [], ["DUMPa"], ioF(T.DUMP[:], [[16, 8]], 4096, 0))
    V(64, ["DUMPa", "r"], ["DUMP"], ts(T.DUMP[:], T.DUMP[:], r, None, A.add))
    V(64, [], ["b128"], ms(T.RF[:, 12:13], 129.5))
    S["st"] = ""

    def earlier(t):
        a = t + 1
        G(128, [], ["CL%d" % t], ioF(T.CL[0:1, t, :], [[64, 2], [1, 2 ** a], [2 ** a, 2 ** (6 - a)]], 0, 0))
        PE(256, ["CL%d" % t, "ONES", "NEG"], ["EQ"], [(T.EQ[:, 0:128], T.ONES[0:1, :], T.CL[0:1, t, :], True, False),
                                                      (T.EQ[:, 0:128], T.CL[0:1, t, :], T.NEG[0:1, :], False, True)])
        V(128, ["EQ"], ["MK%d" % t], ts(T.MK[:, t, :], T.EQ[:, 0:128], 0.0, 8192.0, A.is_ge, A.mult))

    MM, EQ, KX, HT = T.MM, T.EQ, T.KX, T.HT
    IB = T.IB[:]

    def zk(t, s):
        return ["Z%d%d" % (t, s)]

    def rk(s):
        return ["ROCK%d0" % s, "ROCK%d1" % s]

    def follow(q, i):
        if q in S["last"]:
            S["ops"][i]["deps"].setdefault(S["last"][q], False)
        S["last"][q] = i

    def claims(t, s):
        k, H, xk = "%d%d" % (t, s), str(s), "X%d" % s
        o = 2 * t + s
        X, CO, ZX = T[xk], T["CO" + H], T["ZX" + H]
        nodes = [(X[:, 384:448], T.QR[0:1, 0:128], T.ONES[0:1, 0:64], True, False)] + [(X[:, 384 + 32 * b:416 + 32 * b], IB, T.F[:, o, b:64:2], False, b == 1) for b in range(2)]
        PE(192, ["F" + k, "QR", "ONES", "IB"], [xk], nodes)
        SC(64, [xk], ["UI" + H], ac(T.UI[:, s, 4:512:8], X[:, 384:448], AF.Copy))
        mm = [(X[:], T.L3[0:97, :], T.R3[0:97, :], True, False)]
        for m in range(4):
            for b in range(2):
                mm.append((X[:, 256 * b + 4 + m:256 * b + 256:8], T.SCM[:, m, :], T.F[:, o, b:64:2], False, False))
        PE(512 + 512, ["F" + k, "L3", "R3"] + ["SCM%d" % m for m in range(4)], [xk], mm)
        PE(256, zk(t, s) + ["W2" + H], [xk], [(X[:, 256 * b + x:256 * b + 256:8], T.W2[:, s, :], T.Z[:, o, b:64:2], False, x + b == 4) for x in (0, 3) for b in range(2)])
        V(512, [xk, "UI" + H], ["HM" + H], scan(T.HM[:, s, :], T.UI[:, s, :], X[:], 0.0, A.mult, A.add))
        for m in range(4):
            V(64, ["HM" + H], ["C4%s%d" % (H, m)], ts(T.C4[:, s, m:256:4], T.HM[:, s, 4 + m:512:8], 5 + m, 4095, A.arith_shift_right, A.bitwise_and))
        PE(192 + 192, ["F" + k, "QR", "ONES", "IB", "BQ", "L3"] + zk(t, s), [xk], nodes + [(X[:, 192:256], T.L3[0:1, :], T.QR[0:1, 128:192], True, False)] +
           [(X[:, 192 + 32 * b:224 + 32 * b], T.BQ[:], T.Z[:, o, b:64:2], False, b == 1) for b in range(2)])
        V(256 - 4 * NG, ["C4%s%d" % (H, m) for m in range(4)], ["COs" + H], cp(CO[:, 4 * NG:256], T.C4[:, s, 4 * NG:256]))
        for m in range(4):
            V(64, ["C4%s%d" % (H, m)], ["COv%s%d" % (H, m)], cp(CO[:, NG * m:NG * m + NG], T.C4[:, s, m:4 * NG:4]))
        for p in range(16):
            if p < ZV:
                V(64, zk(t, s), ["ZX%s%d" % (H, p)], ts(ZX[:, p:16 * NG:16], T.Z[:, o, 0:2 * NG:2], 0.5, None, A.mult))
            elif p < ZV + ZS:
                SC(NG, zk(t, s), ["ZX%s%d" % (H, p)], ac(ZX[:, p:16 * NG:16], T.Z[:, o, 0:2 * NG:2], AF.Copy, scale=0.5))
            else:
                G(NG, ["ZX%s%d" % (H, p % 2)], ["ZX%s%d" % (H, p)], sel(ZX[:, p:16 * NG:16], ZX[:, p % 2:16 * NG:16], [[0, NG]], A.is_ge, 0.0, 0, 0))
        V(64, [xk], ["UA" + H], ts(T.UA[:, s, :], X[:, 192:256], 1.5 * 2 ** 23, 1.5 * 2 ** 23, A.add, A.subtract))
        V(64, [xk, "UA" + H], [xk, "SM" + H], tt(X[:, 0:64], X[:, 192:256], T.UA[:, s, :], A.is_equal))
        V(64, ["HM" + H], ["UF" + H], ts(T.UF[:, s, :], T.HM[:, s, 259:512:8], 16.0, 65536.0 - 16 - 2 ** 18, A.mult, A.add))
        if OPT["z4"] == "s":
            SC(64, zk(t, s), ["Z4" + H], ac(T.Z4[:, s, :], T.Z[:, o, :], AF.Copy, scale=0.125, bias=129 - 0.375))
        else:
            V(64, zk(t, s), ["Z4" + H], ts(T.Z4[:, s, :], T.Z[:, o, :], 0.125, 129 - 0.375, A.mult, A.add))
        if OPT["z5"] == "s":
            SC(64, zk(t, s), ["Z5" + H], *[ac(T.Z5[:, s, 32 * b:32 * b + 32], T.Z[:, o, b:64:2], AF.Copy, scale=0.5, bias=-0.5) for b in range(2)])
        else:
            V(64, zk(t, s), ["Z5" + H], *[ts(T.Z5[:, s, 32 * b:32 * b + 32], T.Z[:, o, b:64:2], 0.5, -0.5, A.mult, A.add) for b in range(2)])

    def moves(t, s):
        H = str(s)
        o = 2 * t + s
        CO, ZX, RO = T["CO" + H], T["ZX" + H], T["ROCK" + H]
        nv = 64 * NG
        run = []
        for c0 in list(range(NG, 32, SGRP)) + list(range(32, 64, SGRP)):
            calls = []
            run.append(len(S["ops"]))
            for c in range(c0, c0 + SGRP):
                z = 2 * c if c < 32 else 2 * (c - 32) + 1
                calls.append(ac(T.D[:, s, 64 * c:64 * c + 64], RO[:, 0:4096].indirect(CO[:, 4 * c:4 * c + 4]), AF.Abs, bias=T.Z[:, o, z:z + 1], scale=-2.0))
            SC(SGRP * (64 * GAT + 5), rk(s) + zk(t, s) + ["COs" + H], ["D%s_%d" % (H, c) for c in range(c0, c0 + SGRP)], *calls)
        for m in range(4):
            dm = T.D[:, s, 16 * NG * m:16 * NG * (m + 1)]
            n = NG // VP
            before = list(S["r"].get("E%s_%d" % (H, m), []))
            for x in range(VP):
                e0 = 16 * (NG * m + n * x)
                V(57 + GAT * 16 * n, rk(s) + ["COv%s%d" % (H, m), "E%s_%d" % (H, m)] + ["ZX%s%d" % (H, b) for b in range(16)], ["G%s_%d_%d" % (H, m, x)],
                  tt(T.D[:, s, e0:e0 + 16 * n], RO[:, 0:4096].indirect(CO[:, NG * m + n * x:NG * m + n * x + n]), ZX[:, 16 * n * x:16 * n * (x + 1)], A.subtract))
                for j in before:
                    S["ops"][-1]["deps"][j] = True
                follow("v", len(S["ops"]) - 1)
            run.insert(ABS[m] + m, SC(16 * NG, ["G%s_%d_%d" % (H, m, x) for x in range(VP)], ["E%s_%d" % (H, m)], ac(dm, dm, AF.Abs)))
        for i in run:
            follow("s", i)

        def parts(a, b):
            return (["E%s_%d" % (H, m) for m in range(4) if 16 * NG * m < b and 16 * NG * (m + 1) > a] +
                    ["D%s_%d" % (H, c) for c in range(NG, 64) if 64 * c < b and 64 * c + 64 > a])
        cuts = {0: [16 * NG * m for m in range(5)] + ([2048] if NG < 32 else []), 1: list(range(2048, 4097, NPC))}
        for ch in (0, 1):
            for a, b in zip(cuts[ch][:-1], cuts[ch][1:]):
                V((b - a) // 2, parts(a, b) + ["TOP%d" % t], ["N%s_%d" % (H, a)], ts(T.NR[:, s, a:b], T.D[:, s, a:b], T.TOP[:, t, 68 + 2 * s + (a >= 64 * NG):69 + 2 * s + (a >= 64 * NG)], None, A.is_lt))
        K0, K1 = T.K0, T.K1
        for p0 in range(0, 16, 4):
            PE(256 + 128 * (p0 == 0), parts(0, 2048) + ["WD", "CM", "ONES"], ["K0"], [(K0[:, 0:128], T.CM[0:1, 0:128], T.ONES[0:1, :], True, False)][:p0 == 0] +
               [(K0[:, p:128:16], T.D[:, s, p:2048:16], T.WD[:, 0:8], False, False) for p in range(p0, p0 + 4)])
        for p0 in range(0, 16, 4):
            PE(256, ["N%s_%d" % (H, a) for a in cuts[0][:-1]] + ["WD"], ["K0"],
               [(K0[:, p:128:16], T.NR[:, s, p:2048:16], T.WD[:, 8:16], False, p == 15) for p in range(p0, p0 + 4)])
        ke = T.KE[:, s, 0:128]
        if OPT["ke"] == "s":
            SC(128, ["K0"], ["KE" + H], ac(ke, K0[:, 0:128], AF.Copy))
        else:
            V(128, ["K0"], ["KE" + H], cp(ke, K0[:, 0:128]))
        PE(512, ["KE" + H, "PERM"], ["KX"], [(KX[:, 0:128], ke, T.PERM[:], True, True)])
        V(128, ["KX", "RS"], ["KS%s0" % H], scan(T.KS[:, s, 0:128], T.RS[:], KX[:, 0:128], 0.0, A.add, A.min))
        for x in range(2):
            a0, kk = 2048 + 1024 * x, K1[:, 64 * x:64 * x + 64]
            for p0 in range(0, 16, 4):
                first = x == 0 and p0 == 0
                PE(256 + 128 * first, parts(a0, a0 + 1024) + ["RK", "CM", "ONES"], ["K1"], [(K1[:, 0:128], T.ONES[0:1, :], T.CM[0:1, 128:256], True, False)][:first] +
                   [(kk, T.RK[:, 0, 15 - p:143 - p], T.D[:, s, a0 + p:a0 + 1024:16], False, False) for p in range(p0, p0 + 4)])
            for p0 in range(0, 16, 4):
                PE(256, ["N%s_%d" % (H, a) for a in cuts[1][:-1] if a0 <= a < a0 + 1024] + ["RK"], ["K1"],
                   [(kk, T.RK[:, 1, 15 - p:143 - p], T.NR[:, s, a0 + p:a0 + 1024:16], False, x == 1 and p == 15) for p in range(p0, p0 + 4)])
        V(128, ["K1", "RS"], ["KS%s1" % H], scan(T.KS[:, s, 128:256], T.RS[:], K1[:, 0:128], 0.0, A.add, A.min))

    def choice(t, s):
        k, H, xk = "%d%d" % (t, s), str(s), "X%d" % s
        o = 2 * t + s
        X = T[xk]
        kb, kn = T.KS[:, s, 3:256:4], ["KS%s0" % H, "KS%s1" % H]
        V(64, kn, ["KC" + H], ts(T.KC[:, s, :], kb, 255, 5, A.bitwise_and, A.arith_shift_right))
        V(64, kn, ["NB" + H], ts(T.NB[:, s, :], kb, 5, 1, A.arith_shift_right, A.bitwise_and))
        V(64, ["NB" + H, xk], ["PRn" + H], tt(T.PR[:, s, 256:320], X[:, 384:448], T.NB[:, s, :], A.mult))
        NP = X[:, 448:512]
        PE(256 + 128, ["PRn" + H, "NI32", "F" + k, "IB"], [xk], [(NP, T.NI32[:], T.PR[:, s, 256:320], True, False)] +
           [(X[:, 448 + 32 * b:480 + 32 * b], IB, T.F[:, o, b:64:2], False, False) for b in range(2)])
        for m in range(4):
            V(64, ["KC" + H], ["KX", "KM%d" % m], ts(KX[:, 256 + 64 * m:320 + 64 * m], T.KC[:, s, :], float(2 * m + 1), None, A.is_equal))
        for m in range(4):
            V(64, ["KX", "KM%d" % m, "C4%s%d" % (H, m)], ["PR%s%d" % (H, m)],
              tt(T.PR[:, s, 64 * m:64 * m + 64], KX[:, 256 + 64 * m:320 + 64 * m], T.C4[:, s, m:256:4], A.mult))
            PE(256, ["PR%s%d" % (H, m), "I32"], [xk], [(NP, T.I32[:], T.PR[:, s, 64 * m:64 * m + 64], False, m == 3)])

    def meetings(t, s):
        k, H, xk = "%d%d" % (t, s), str(s), "X%d" % s
        o = 2 * t + s
        X = T[xk]
        NP = X[:, 448:512]
        HW, LS = T["HW" + H], T["LS" + H]
        JJ = T.NS[:, s, 1:64:2]
        V(64, [xk], ["HF" + H], ts(T.HF[:, s, 0:64], NP, 0.125, 1281 - 0.4375, A.mult, A.add))
        if OPT["hf"] == "2":
            V(64, [xk], ["HG" + H], ts(T.HF[:, s, 64:96], X[:, 480:512], 0.125, 1281 - 0.4375, A.mult, A.add))
        V(64, [xk], ["JC" + H], cp(T.JC[:, s, :], NP))
        SC(32, [xk], ["NS" + H], ac(JJ, X[:, 480:512], AF.Copy, bias=2048.0))
        for b, bk in ((0, "EQ"), (1, "KX")):
            mm = []
            for l in range(8):
                dd = T[bk][:, 32 * l:32 * l + 32]
                if OPT["hf"] != "2":
                    mm.append((dd, IB, T.HF[:, s, 32:64], True, False))
                elif l % 2 == 0:
                    mm.append((T[bk][:, 32 * l:32 * l + 64], IB, T.HF[:, s, 32:96], True, False))
                mm.append((dd, T.EL[:, 8 * b + l, :], T.HF[:, s, 0:32], False, OPT["hf"] != "2" or l % 2 == 1))
            PE(len(mm) * 64, ["HF" + H, "IB", "EL%d" % (8 * b), "EL%d" % (8 * b + 4)] + ["HG" + H][:OPT["hf"] == "2"], [bk], mm)
            V(256, [bk], ["EQB%s%d" % (H, b)], ts(T.EQB[:, s, 256 * b:256 * b + 256], T[bk][:, 0:256], 0.0, None, A.is_equal))
        for b in range(2):
            PE(512, ["EQB%s%d" % (H, b)] + ["PL%d" % l for l in range(8 * b, 8 * b + 8)], ["MM"],
               [(MM[:, 0:32], T.PL[:, l, :], T.EQB[:, s, 32 * l:32 * l + 32], l == 0, l == 15) for l in range(8 * b, 8 * b + 8)])
        for x in range(0, 16, 2):
            mm = []
            for i in (x, x + 1):
                mm += [(HT[:, 32 * i:32 * i + 32], T.CS[:, i, :], T.JC[:, s, 32:64], True, False), (HT[:, 32 * i:32 * i + 32], T.NIB[:], T.JC[:, s, 0:32], False, True)]
            PE(256, ["JC" + H, "CS%d" % (x // 4 * 4), "NIB"], ["HT"], mm)
        SC(512, ["HT"], ["HW" + H], ac(HW[:], HT[:], AF.Copy))
        PE(256 + 192, ["JC" + H, "UF" + H, "I32", "I32B", "IB", "QR", "QS"], [xk],
           [(X[:, 128:192], T.QR[0:1, 0:128], T.QS[0:1, :], True, False), (X[:, 129:192:2], T.I32[:], T.UF[:, s, :], False, False),
            (X[:, 129:192:2], T.I32B[:], T.JC[:, s, 32:64], False, False), (X[:, 128:192:2], IB, T.JC[:, s, 0:32], False, True)])
        pm = T.PM[:, s, 0:32]
        V(64, ["MM"], ["PM" + H], ts(pm, MM[:, 0:32], 0.0, None, A.max))
        if t < NV - 1:
            V(64, ["MM"], ["PN" + H], ts(T.PM[:, s, 32:64], MM[:, 0:32], 0.5, None, A.is_ge))
        PE(192, ["PM" + H, "QA", "QB", "QC"], ["MM"], [(MM[:, 32 + 32 * x:64 + 32 * x], T.QQ[:, x, :], pm, True, True) for x in range(3)])
        V(96, ["MM"], ["MS" + H], ts(T.MS[:, s, 0:96], MM[:, 32:128], 0.5, None, A.is_ge))
        PE(256, ["MS" + H, "WX", "CJ", "IB"], ["MM"], [(MM[:, 128:160], IB, T.CJ[:], True, False)] +
           [(MM[:, 128:160], T.WX[:, x, :], T.MS[:, s, 32 * x:32 * x + 32], False, x == 2) for x in range(3)])
        V(64, ["MS" + H], ["CD" + H], tt(T.MS[:, s, 96:128], T.MS[:, s, 0:32], T.MS[:, s, 32:64], A.subtract))
        V(64, ["MM", "R1"], ["LS" + H], scan(LS[:, 1:33], T.R1[:, 0:32], MM[:, 128:160], 0.0, A.mult, A.max))
        V(2 * (57 + 16 * GAT), ["LS" + H, "HW" + H, "CD" + H], ["DMs" + H],
          *[tt(T.DM[:, s, 16 * c:16 * c + 16], HW[:].indirect(LS[:, 16 * c + 16:16 * c + 17]), T.MS[:, s, 96 + 16 * c:112 + 16 * c], A.mult) for c in range(2)])
        V(64, ["NS" + H, xk], ["JU" + H], scan(T.JU[:, s, :], T.NS[:, s, :], X[:, 128:192], 0.0, A.mult, A.add))
        V(64, ["JU" + H], ["JX" + H], ts(T.JX[:, s, :], T.JU[:, s, 1:64:2], 5, 4095, A.arith_shift_right, A.bitwise_and))
        V(64, ["JX" + H, "NS" + H], ["DFj" + H], tt(T.DF[:, s, 32:64], T.JX[:, s, :], JJ, A.subtract))
        V(64, ["DFj" + H, "MS" + H], ["DMj" + H], tt(T.DM[:, s, 32:64], T.DF[:, s, 32:64], T.MS[:, s, 64:96], A.mult))
        V(64, ["DMs" + H, "DMj" + H, xk], ["FO" + k], tt(T.FO[:, o, :], NP, T.DM[:, s, :], A.add))

    def send(kind, t, s, R):
        dst = T.cores[(rank + 3) % 8]
        rid, pid, _ = topo.addr(dst)
        n, mask = len(topo.engines(core, dst)), topo.mask(core, dst)
        o = 2 * t + s
        src, out = (T.FO, T.F) if kind == "f" else (T.ZO, T.Z)
        sem = "ar%s%d%d" % (kind, t + 1, s)
        add(S, "g", 0.1, R, [("F" if kind == "f" else "Z") + "%d%d" % (t + 1, s)],
            lambda: g.remote_dma(out[:, o + 2, :], src[:, o, :], T.sem[sem], T.sem.sl, pid, rid, mask), (sem, n), DML)
        S["sends"] += n

    def mining(t, s):
        k, H, xk = "%d%d" % (t, s), str(s), "X%d" % s
        o = 2 * t + s
        X, E16, OF, RO = T[xk], T["E16" + H], T["OF" + H], T["ROCK" + H]
        last = t == NV - 1
        if not last:
            send("f", t, s, ["FO" + k])
        mf = T.MF[:, s, :]
        V(128, ["FO" + k, xk, "SM" + H], ["MF" + H], *[tt(T.MF[rows(a), s, 64 * a:64 * a + 64], X[rows(a), 0:64], T.FO[rows(a), o, :], A.mult) for a in range(2)])
        EO = T["EO" + H]
        PE(192, ["MF" + H, "BLK", "IB", "CK"], ["MM"], [(MM[:, 176:240], IB, T.CK[:], True, False)] +
           [(MM[:, 176:240], T.BLK[:], T.MF[:, s, 64 * a:64 * a + 64], False, a == 1) for a in range(2)])
        V(64, ["MM", "R1"], ["EO" + H], scan(EO[:, 1:65], T.R1[:], MM[:, 176:240], 0.0, A.mult, A.max))
        V(4 * (57 + 16 * GAT), rk(s) + ["EO" + H, "Z5" + H], ["SU" + H],
          *[tt(T.SU[:, s, 16 * c:16 * c + 16], RO[:, 0:4096].indirect(EO[:, 16 * c + 16:16 * c + 17]), T.Z5[:, s, 16 * c:16 * c + 16], A.add) for c in range(4)])
        V(64, ["SU" + H], ["ZO" + k], ts(T.ZO[:, o, :], T.SU[:, s, :], 1.5 * 2 ** 24, 1.5 * 2 ** 24, A.add, A.subtract))
        if last:
            V(128, ["ZO" + k], ["YZ" + H], *[ts(T.YZ[:, s, 32 * b:32 * b + 32], T.ZO[:, o, b:64:2], 0.5, None, A.mult) for b in range(2)])
            V(128, ["FO" + k], ["YF" + H], *[ts(T.YF[:, s, 32 * b:32 * b + 32], T.FO[:, o, b:64:2], 2048.0, None, A.add) for b in range(2)])
        else:
            send("z", t, s, ["ZO" + k])
        EL, VV = HT[:, 0:8], HT[:, 8:16]
        PE(1024, ["MF" + H, "RW"], ["HT"], [(EL, T.RW[:, 15 - p:143 - p], T.MF[:, s, p:128:16], p == 0, p == 15) for p in range(16)])
        V(64, ["HT"], ["E16" + H], ts(E16[:], EL, 2048.0, None, A.add))
        for x in range(4):
            bk = "EQ"
            dd = EQ[:, 128 * x:128 * x + 128]
            PE(384, ["MF" + H, "MK%d" % t, "IB", "GS%d" % x], [bk], [(dd, IB, T.MK[:, t, :], True, False), (dd, T.GS[:, x, :], mf, False, False),
                                                                    (dd, mf, T.GS[:, 4 + x, :], False, True)])
        mm = []
        for a in range(2):
            mm.append((MM[:, 256 + 64 * a:320 + 64 * a], T.SEL[:, a, :], T.SU[:, s, :], True, False))
            for b in range(2):
                dd = MM[:, 256 + 64 * a + 32 * b:288 + 64 * a + 32 * b]
                mm += [(dd, T.SEL[:, 2 + a, :], T.Z4[:, s, b:64:2], False, False), (dd, T.SEL[:, 4 + a, :], T.Z[:, o, b:64:2], False, b == 1)]
        PE(640, ["SU" + H, "Z4" + H, "SEL0", "SEL1", "NSEL0", "NSEL1"] + zk(t, s), ["MM"], mm)
        if OPT["rn"] == "s":
            SC(128, ["MM", "b128"], ["RN" + H], ac(T.RN[:, s, :], MM[:, 256:384], AF.Relu, bias=T.RF[:, 12:13]))
        else:
            V(128, ["MM"], ["RN" + H], ts(T.RN[:, s, :], MM[:, 256:384], 129.5, 0.0, A.add, A.max))
        PE(256, ["DUMP", "I32"], ["HT"], [(VV, T.I32[:], T.DUMP[:], True, False)])
        for x in range(4):
            bk = "EQ"
            dd = EQ[:, 128 * x:128 * x + 128]
            lo, lx = T.LO[:, s, x:x + 1], T.LX[:, s, 8 * x:8 * x + 8]
            V(128, [bk], ["LO%s%d" % (H, x)], (lambda lo, dd: lambda: v.tensor_reduce(lo, dd, AxisListType.X, A.min, negate=True, apply_absolute_value=True))(lo, dd))
            if OPT["lx"] == "s":
                SC(8, ["LO%s%d" % (H, x), "WD"], ["LX%s%d" % (H, x)], ac(lx, T.WD[:, 8:16], AF.Copy, scale=lo))
            else:
                V(64, ["LO%s%d" % (H, x), "WD"], ["LX%s%d" % (H, x)], ts(lx, T.WD[:, 8:16], lo, None, A.mult))
            PE(64, ["LX%s%d" % (H, x), "BK"], ["HT"], [(VV, T.BK[:, x, :], lx, False, x == 3)])
        V(64, ["HT", "E16" + H], ["OF" + H], tt(OF[:], VV, E16[:], A.max))
        V(57 + 128 * SCA, ["OF" + H, "RN" + H], rk(s), cp(RO[:].indirect(OF[:]), T.RN[:, s, :]))
        if last:
            for a in range(2):
                n = "%d%d" % (s, a)
                dma("y", "od_f" + n, T.yf[rows(s), rows(a)], T.YF[rows(a), s, :], ["YF" + H], ["of" + n], 2.0)
                dma("y", "od_z" + n, T.yz[rows(s), rows(a)], T.YZ[rows(a), s, :], ["YZ" + H], ["oz" + n], 2.0)
            for a in range(2):
                n = "%d%d" % (s, a)
                dma("ys"[a * s], "od_x" + n, T.yx[rows(s), 2048 * a:2048 * a + 2048], RO[rows(a), 2048 * a:2048 * a + 2048], rk(s), ["ox" + n], 3.5)

    def count(t):
        bk = OPT["nb"]
        for s in range(2):
            PE(128 + 288 * (s == 0), ["PN%d" % s, "ONES", "I32", "CN"], [bk], [(T[bk][:, 256:328], T.I32[:], T.CN[:, 0, :], True, False)][:s == 0] +
               [(T[bk][:, 256 + 36 * x:288 + 36 * x], T.ONES[:], T.PM[:, s, 32:64], False, s + x == 2) for x in range(2)])
        V(72, [bk, "CN"], ["TOP%d" % (t + 1)], scan(T.TOP[:, t + 1, :], T.CN[:, 1, :], T[bk][:, 256:328], 0.0, A.mult, A.add))

    for t in range(NV):
        S["st"] = "k"
        earlier(t)
        for s in range(2):
            for f, n in ((claims, "c"), (moves, "m"), (choice, "s"), (meetings, "e")):
                S["st"] = n + str(s)
                f(t, s)
            if s == 1 and t < NV - 1:
                S["st"] = "n"
                count(t)
            S["st"] = "i" + str(s)
            mining(t, s)
    return S


def rank_program(g, core, T, topo):
    if T.rank_of(core) is None:
        return
    S = record(g, core, T, topo)
    if "order" not in PLANS:
        PLANS["order"] = plan(S)
    eng = {"v": g.vector, "s": g.scalar, "t": g.tensor, "g": g, "y": g.sync}
    cnt = issue(S, PLANS["order"], eng, T)
    for s in sorted(cnt):
        g.wait_ge(T.sem[s], cnt[s])
    for s in STORES:
        g.wait_ge(T.sem["od_" + s], 16)
    g.wait_ge(T.sem.sl, S["sends"])
